import numpy as np, ml_dtypes
CORES = [25,29,65,69,153,157,193,197]
N = 8
import mx_ref
BF = ml_dtypes.bfloat16
def gcols(t, e):
    v = np.concatenate([t.reshape(8, 16, -1, 4), np.zeros((8, 16, 1, 4), BF)], axis=2)
    return np.ascontiguousarray(np.stack([v[g][:, e[g]] for g in range(8)])).reshape(128, -1)
def gpick(z, e):
    return np.concatenate([z[16 * g:16 * g + 16][:, e[g]] for g in range(8)])
def tile(rs):
    return np.stack(rs, axis=2).reshape(128, -1).astype(BF)
def pick(q, e):
    c = np.concatenate([q[0].reshape(128, -1, 4), np.zeros((128, 1, 4), np.uint8)], axis=1); s = np.concatenate([q[1], np.ones((16, 1), np.uint8)], axis=1)
    return (np.ascontiguousarray(c[:, e].reshape(128, -1)), np.ascontiguousarray(s[:, e]))
def join(*qs):
    return (np.concatenate([q[0] for q in qs], axis=1), np.concatenate([q[1] for q in qs], axis=1))
def put(q, e, v):
    c, s = q[0].reshape(128, -1, 4).copy(), q[1].copy(); c[:, e] = v[0].reshape(128, -1, 4); s[:, e] = v[1]
    return (c.reshape(128, -1), s)
def pk(c, s):
    return (np.ascontiguousarray(c), mx_ref.live(s))
def emit(q):
    return q[0], q[1]
def packed(v, rng):
    q = [mx_ref.quantize(np.ascontiguousarray(v[r])) for r in range(N)]
    return np.stack([a for a, b in q]), np.stack([mx_ref.plane(b, rng) for a, b in q])
def values_of_codes():
    e, c = np.zeros((128, 128, 4), np.float32), np.zeros((128, 2, 4), np.uint8)
    e[np.arange(128), np.arange(128), 0] = 1
    c[:127, :, 0] = np.arange(256).reshape(2, 128).T[:127]
    return mx_ref.matmul(mx_ref.quantize(e.reshape(128, 512).astype(BF)), (c.reshape(128, 8), np.full((16, 2), 127, np.uint8))).T.reshape(-1).astype(np.float64)
CODE_VALUE, SCALE_VALUE = values_of_codes(), 2.0 ** (np.arange(256) - 127.0)
def decode(q):
    return (CODE_VALUE[q[0]].reshape(16, 8, -1, 4) * SCALE_VALUE[q[1]][:, None, :, None] + 0.0).reshape(128, -1).astype(np.float32)
def f(rng, *shape):
    return mx_ref.flush((rng.standard_normal(shape, dtype=np.float32) * np.exp2(rng.integers(-2, 3, shape[:-1] + (1,)))).astype(BF))
def wide(rng, *shape, cols=0):
    v = rng.standard_normal(shape, dtype=np.float32) * np.exp2(rng.integers(-12, 13, shape)).astype(np.float32)
    if cols: v *= np.repeat(np.exp2(rng.integers(-cols, cols + 1, shape[:-2] + (1, shape[-1] // 4))) * (rng.random(shape[:-2] + (1, shape[-1] // 4)) > 0.0625), 4, axis=-1).astype(np.float32)
    return mx_ref.flush(v.astype(BF))
C, K, R = 320, 64, 2
STEP = [1, 2]
def partner(r, t):
    return r ^ STEP[t]
def basins(s):
    s = s + np.float32(0.0)
    j = np.arange(C)
    o = np.argsort(-s, axis=1, kind="stable")
    w = C - 1 - np.argsort(o, axis=1)
    up = w[:, None, :] > w[:, :, None]
    before, behind = j < j[:, None], j > j[:, None]
    l = np.max(np.where(up & before, j, -1), axis=2)
    r = np.min(np.where(up & behind, j, C), axis=2)
    a = np.where(l < 0, -1, np.min(np.where(before & (j > l[:, :, None]), w[:, None, :], C), axis=2))
    b = np.where(r == C, -1, np.min(np.where(behind & (j < r[:, :, None]), w[:, None, :], C), axis=2))
    other = (a < C) & (b < C) & (w < C - 1)
    q = np.where(other, np.take_along_axis(o, np.where(other, C - 1 - np.maximum(a, b), 0), axis=1), j)
    p = s - np.take_along_axis(s, q, axis=1)
    first = np.where(w == C - 1, 0, np.where(other, 1, 2))
    e = np.sort(np.lexsort((-p, first))[:, :K], axis=1)
    edge = np.full((8, 1), -1)
    beside = np.where(np.concatenate([edge, w[:, :-1]], axis=1) > np.concatenate([w[:, 1:], edge], axis=1), j - 1, j + 1)
    to = np.where(other, np.where(a > b, l, r), beside)
    np.put_along_axis(to, e, e, axis=1)
    for i in range(C.bit_length()): to = np.take_along_axis(to, to, axis=1)
    k = np.zeros((8, C), np.int64)
    np.put_along_axis(k, e, np.tile(np.arange(K), (8, 1)), axis=1)
    return e, np.take_along_axis(q, e, axis=1), to, np.take_along_axis(k, to, axis=1)
def big(v):
    v = v.astype(np.float32)
    v[np.abs(v) < np.float32(2.0 ** -16)] = 0
    return v.astype(BF)
def numbers_of(rng):
    return {"x": big(f(rng, N, 128, 4 * C)), "u": np.array(f(rng, N, 128, 512)), "v": np.array(f(rng, N, 128, 512))}
def weights(rng, w):
    c, p = packed(w, rng)
    return {"wc": c, "ws": p}
def some(rng, keep):
    w = np.array(f(rng, N, 128, 2048)).reshape(N, 128, 4, 8, 16, 4)
    w[:, :, :, :, [i for i in range(16) if i not in keep]] = 0
    return weights(rng, w.reshape(N, 128, 2048))
def unit(rng, keep, a):
    w = np.zeros((N, 128, 4, 128, 4), np.float32)
    i = np.array([i for i in range(128) if i % 16 in keep])
    for b in range(4): w[:, i, b, i, b] = a
    return weights(rng, w.reshape(N, 128, 2048).astype(BF))
def whole(rng, *shape):
    return rng.integers(4, 8, shape) * rng.choice([-1.0, 1.0], shape)
def plant(d, s, c, m, top, k):
    x = d["x"].astype(np.float32).reshape(N, 8, 16, C, 4)
    x[:, :, 0] = 0
    x[:, :, 0, :, 0] = c * m
    u = d["u"].reshape(N, 128, 128, 4)
    u[:, :, ::16] = 0
    for i in range(3): x[:, :, 8 + i] = ((s[..., None] >> np.arange(4 * i, 4 * i + 4)) & 1) * 2.0 ** np.arange(4) * m
    for h in range(0, 128, 16):
        u[:, h, h, 0] = (k * top).astype(np.float32).astype(BF)
        for i in range(3): u[:, h + 8 + i, h] = (k * 16.0 ** i).astype(np.float32).astype(BF)[:, None]
    return {"x": x.reshape(N, 128, 4 * C).astype(BF), "u": u.reshape(N, 128, 512), "v": d["v"]}
def setup_inputs(rng):
    return {**numbers_of(rng), **weights(rng, f(rng, N, 128, 2048))}
def setup_inputs_ties(rng):
    d = numbers_of(rng)
    e = rng.permutation(N)
    x = d["x"].reshape(N, 8, 16, C, 4)
    for r in range(N):
        k = np.zeros(C, int) if r == e[0] else rng.permutation(C) % 3
        a = x[r][:, :8, :3].copy()
        a[:, :, 2] = 0
        x[r][:, :8] = a[:, :, k]
    x[e[1]] = 0
    u = d["u"].reshape(N, 8, 16, 128, 4)
    u[:, :, 8:, ::16] = 0
    return {"x": x.reshape(N, 128, 4 * C), "u": u.reshape(N, 128, 512), "v": d["v"], **some(rng, range(8, 16))}
def setup_inputs_near(rng):
    d = numbers_of(rng)
    m = 2.0 ** -29
    x = np.zeros((N, 8, 16, C, 4), np.float32)
    x[:, :, 1:8] = whole(rng, N, 8, 7, C, 4) * 4 * m
    x[:, :, 11:] = whole(rng, N, 8, 5, C, 4) * m
    d["x"] = x
    j = np.arange(C)
    fall = C // 2 - 1 - j // 2
    fall = fall + 2 * (fall == C // 2 - K - 1) - 2 * (fall == C // 2 - K + 1)
    c, s = np.zeros((N, 8, C)), np.zeros((N, 8, C), np.int64)
    for r in range(N):
        g = rng.permutation(8)
        for i in range(8):
            c[r, i] = np.where(j % 2 == 1, 1.0, -1.0 * (g[i] % 2))
            s[r, i] = np.where(j % 2 == 1, fall if g[i] == 3 else j // 2, 0)
            if g[i] >= 4:
                s[r, i] = rng.integers(0, 256, C)
                c[r, i, 2 * rng.permutation(C // 2)[:2] + 1] = 2.0 ** 30
    k = np.where(rng.permutation(N) < N // 2, 2.0 ** -30, 1.0)
    return {**plant(d, s, c, m, 2.0 ** 23, k), **unit(rng, range(1, 8), 32)}
def setup_inputs_slopes(rng):
    d = numbers_of(rng)
    j = np.arange(C)
    e = np.stack([j, C - 1 - j, np.minimum(j, C - 1 - j), np.abs(j - C // 2), 0 * j, j // 2, j // 8, np.where(j < 2 * K, j % 2 * (C + j), C - 1 - j)])
    s = np.stack([e[rng.permutation(8)] for r in range(N)])
    c = np.where(rng.permutation(N) < N // 2, -1.0, 0.0)[:, None, None] * np.ones((N, 8, C))
    return {**plant(d, s, c, 1.0, 4096.0, np.ones(N)), **some(rng, range(1, 8))}
def setup_inputs_huge(rng):
    d = numbers_of(rng)
    x = 2.0 ** 30 * (0.5 + 0.3 * rng.random((N, 128, C, 4)))
    c = np.tile(np.arange(C) % 2 * 2.0 - 1.0, (N, 1))
    c[rng.permutation(N) < N // 2] = 1
    x *= c[:, None, :, None]
    g = np.stack([rng.permutation(8) % 2 * 2.0 - 1.0 for r in range(N)])
    u = d["u"].reshape(N, 128, 128, 4)
    u[:, :, ::16] = (2.0 ** 30 * (1 - 0.25 * rng.random((N, 128, 8, 4))) * g[:, None, :, None]).astype(np.float32).astype(BF)
    return {"x": x.astype(np.float32).reshape(N, 128, 4 * C).astype(BF), "u": u.reshape(N, 128, 512), "v": d["v"], **unit(rng, range(16), 1)}
def setup_inputs_spread(rng):
    d = setup_inputs(rng)
    d["x"] = big(wide(rng, N, 128, 4 * C, cols=6))
    return d
def check_inputs(d):
    b = []
    for k in ("x", "u", "v"):
        a = np.abs(d[k].astype(np.float32))
        if not (np.isfinite(a).all() and ((a == 0) | (a >= 2.0 ** -30) & (a <= 2.0 ** 30)).all()): b.append("a value of " + k)
    return b
def reference(x, u, v, wc, ws):
    qu = [mx_ref.quantize(u[r]) for r in range(N)]
    lay = [pk(wc[r], ws[r]) for r in range(N)]
    now = [x[r] for r in range(N)]
    ends = [None] * N
    for t in range(R):
        held, place, sent = [], [], []
        for r in range(N):
            q = mx_ref.quantize(now[r])
            held.append(decode(q))
            e, low, ends[r], h = basins(mx_ref.matmul(qu[r], q)[::16])
            place.append(h)
            own = held[r].astype(BF)
            blend = (gcols(own, e).astype(np.float32) + gcols(own, low).astype(np.float32)) * np.float32(0.5)
            sent.append(mx_ref.quantize(blend.astype(BF)))
        for r in range(N):
            came = sent[partner(r, t)]
            made = [np.maximum(mx_ref.matmul(pick(lay[r], np.arange(128 * b, 128 * b + 128)), came), np.float32(0.0)) * np.float32(0.03125) for b in range(4)]
            now[r] = tile([held[r][:, b::4] + gpick(made[b], place[r]) for b in range(4)])
    y, ol = np.zeros((N, 128, C), np.float32), np.zeros((N, 8, C), np.float32)
    oc, osc = np.zeros((N, 128, 4 * C), np.uint8), np.zeros((N, 16, C), np.uint8)
    for r in range(N):
        q = mx_ref.quantize(now[r])
        y[r] = mx_ref.matmul(mx_ref.quantize(v[r]), q)
        ol[r] = ends[r]
        oc[r], osc[r] = emit(q)
    return {"y": y, "ol": ol, "oc": oc, "osc": osc}

@@ -1,0 +1,506 @@
+from concourse.bass import DstId, RemoteDMATransfer
+from concourse.mybir import dt, AluOpType, AxisListType, ActivationFunctionType
+
+C, K, R = 320, 64, 2
+STEP = [1, 2]
+H = C // 2
+NB = H // 16
+ROW = H + 16
+BIG = 2.0 ** 96
+KEYS = 2.0 ** 18
+NV = [5, 6]
+NX = 132
+HOP, WAKE, LOAD, SLACK, TRIES = 3.5, 0.08, 2.0, 0.02, 1500
+F32, BF, I32, U16, CODE, PLANE = "float32", "bfloat16", "int32", "uint16", "float8_e4m3fn_x4", "uint8"
+
+_SB = {
+    "xt0": (4 * C, BF), "xt1": (4 * C, BF), "xt2": (4 * C, BF), "ut": (512, BF), "vt": (512, BF), "et": (516, BF), "ft": (512, BF),
+    "qu0": (128, CODE), "su0": (128, PLANE), "qu": (128, CODE), "su": (128, PLANE), "qv": (128, CODE), "sv": (128, PLANE),
+    "qw": (512, CODE), "sw": (512, PLANE), "qe": (512, CODE), "se": (512, PLANE),
+    "qx0": (C + 128, CODE), "sx0": (C + 128, PLANE), "qx1": (C + 128, CODE), "sx1": (C + 128, PLANE), "qx2": (C, CODE), "sx2": (C, PLANE),
+    "lc0": (384, CODE), "ls0": (384, PLANE), "lc1": (384, CODE), "ls1": (384, PLANE), "rc": (64, CODE), "rs": (256, PLANE),
+    "cI": (C + 2, F32), "cJ": (C, BF), "cP": (8, I32), "cPf": (8, F32), "cK": (32, F32), "cD": (32, F32), "cTK": (C + 2, F32), "cIT": (C + 2, F32),
+    "cRev": (H + 2, BF), "cTY": (H, F32), "mask": (C, BF), "c16": (C, BF), "c2": (H, BF), "cj1": (20, F32), "ckk": (8, F32), "cb": (64, I32),
+    "oU": (8, U16), "oX": (2, U16), "oY": (2, U16), "oD": (30, U16), "oA": (64, U16), "oH": (20, U16), "oS": (20, U16),
+    "SW": (C + 8, F32), "KB": (NB * ROW, BF), "OS": (NB * ROW, F32), "JK": (NB * H, BF), "JK2": (NB * H, BF), "CS": (NB * H, BF),
+    "TR": (C + 32, F32), "TQ": (C + 32, F32), "TB": (2 * C + 32, BF),
+    "ACC": (32, F32), "I1": (40, I32), "SC": (16, F32), "PQ": (C, F32), "SG": (H + 2, BF), "LAB": (H, BF),
+    "TH": (4 * C, BF), "TF": (2 * C, BF), "TMP": (4 * K, BF), "HR": (4 * K, F32), "GG": (2 * C, F32),
+    "ER": (K, F32), "OLR": (C, F32), "YO": (C, F32),
+}
+_ROWS = {
+    "rf": (F32, {"MN": C + 32, "DT": 32, "M1": H, "POS": H, "KEY": H + 2, "KEYN": H + 2, "DG": C, "DS": C, "NG": H, "PM": H, "DP": H,
+                 "GM": 40, "EF": 8, "QM": K, "QS": K, "SS": 32, "KR": 40, "RM": H + 2, "FS": H, "BS": H, "HT": 40}),
+    "rb": (BF, {"UP": C + 2, "PK": C, "PKM": H, "NPB": H, "Y": H, "G1": H, "EQ": H, "W": H + 2, "F1": H, "NK": H, "KZ": C, "XL": C + 2,
+                "ZZ": C, "LW": C, "NP": NX, "CNP": NX, "DL": C + 32, "LM": H, "LS": H, "RR": H, "GT": H, "NM": H + 2, "NL": H,
+                "CUT": H + 2, "NC": H, "NBK": H, "CN": H, "HM": C, "HS": C, "J3": H, "J4": H, "J5": H}),
+}
+_AT = {}
+for _b, (_d, _rows) in _ROWS.items():
+    _o = 0
+    for _n, _w in _rows.items():
+        _AT[_n] = (_b, _o, _w)
+        _o += (_w + 15) // 16 * 16
+    _SB[_b] = (_o, _d)
+SCRATCH = {n: ("sbuf", [128, w], d) for n, (w, d) in _SB.items()}
+for _n in ("pS", "pT0", "pT1", "pT2", "pT3", "pH0", "pH1", "pH2"):
+    SCRATCH[_n] = ("psum", [128, 512], F32)
+NDMA = 14
+SEMAPHORES = ["sV", "sS", "sT", "sG", "arr0", "arr1", "sent0", "sent1", "rin", "rout"] + ["d%d" % i for i in range(NDMA)]
+_ORDERS = {}
+
+
+def _relays(T, topo, src, dst):
+    return [c for c in topo.cores_of(src) if T.rank_of(c) is None and topo.die(c) == topo.die(src) and topo.may_write(c, dst)][:2]
+
+
+def _bits(engines):
+    return sum(1 << e for e in engines)
+
+
+def _relay_program(g, core, T, topo):
+    for r, src in enumerate(T.cores):
+        for t in range(R):
+            dst = T.cores[r ^ STEP[t]]
+            if topo.may_write(src, dst):
+                continue
+            rel = _relays(T, topo, src, dst)
+            if core not in rel:
+                continue
+            n = len(topo.engines(src, core)) // 2
+            rid, pid = topo.addr(dst, core)
+            m = topo.mask(core, dst)
+            g.wait_ge(T.sem.rin, n)
+            if core == rel[0]:
+                g.remote_dma(T["lc%d" % t][:, 192:256].bitcast(dt.uint8), T.rc[:].bitcast(dt.uint8), T.sem["arr%d" % t], T.sem.rout, pid, rid, m)
+            else:
+                g.remote_dma(T["ls%d" % t][:, 192:256], T.rs[:, 192:256], T.sem["arr%d" % t], T.sem.rout, pid, rid, m)
+            g.wait_ge(T.sem.rout, len(topo.engines(core, dst)))
+
+
+def _play(ops, after, way):
+    now, left, free = {}, [len(o["deps"]) for o in ops], {}
+    for i, o in enumerate(ops):
+        now[o["q"]] = 0.0
+        free.setdefault(o["q"], [])
+        if not o["deps"]:
+            free[o["q"]].append(i)
+    ready, order, end = [0.0] * len(ops), [], 0.0
+    while len(order) < len(ops):
+        q = min((q for q in free if free[q]), key=lambda q: max(now[q], min(ready[i] for i in free[q])))
+        best, t = max(free[q], key=lambda i: way[i]), now[q]
+        rb = ready[best]
+        if rb - t > 0.01:
+            fit = [i for i in free[q] if ready[i] < rb and
+                   max(ready[i], t) + ops[i]["cost"] + way[best] <= rb + max(way[best] + SLACK, ops[best]["cost"] + way[i])]
+            if fit:
+                best = max(fit, key=lambda i: way[i] - 8 * max(0.0, ready[i] - t))
+        free[q].remove(best)
+        now[q] = max(t, ready[best]) + ops[best]["cost"]
+        done = now[q] + ops[best]["lat"]
+        end = max(end, done)
+        order.append(best)
+        for j in after[best]:
+            ready[j] = max(ready[j], done + WAKE)
+            left[j] -= 1
+            if not left[j]:
+                free[ops[j]["q"]].append(j)
+    return end, order
+
+
+def _order(ops):
+    key = tuple((o["q"], o["cost"], o["lat"]) for o in ops)
+    if key not in _ORDERS:
+        way, after = [0.0] * len(ops), [[] for o in ops]
+        for i in reversed(range(len(ops))):
+            way[i] = ops[i]["cost"] + ops[i]["lat"] + max([way[j] + WAKE for j in after[i]], default=0.0)
+            for d in ops[i]["deps"]:
+                after[d].append(i)
+        best, seed = _play(ops, after, way), 1
+        for n in range(TRIES):
+            new = list(way)
+            for m in range(6):
+                seed = (seed * 6364136223846793005 + 1442695040888963407) % 2 ** 64
+                new[(seed >> 33) % len(ops)] += ((seed >> 20) % 1001 - 500) / 250.0
+            got = _play(ops, after, new)
+            if got[0] <= best[0]:
+                best, way = got, new
+        _ORDERS[key] = best[1]
+    return _ORDERS[key]
+
+
+def _emit(ops, queue, T):
+    count, known, clocks, mark = {}, {q: {} for q in queue}, {}, {}
+
+    def need(q, sem, n):
+        if known[q].get(sem, 0) < n:
+            queue[q].wait_ge(T.sem[sem], n)
+            for s, v in clocks.get((sem, n), {sem: n}).items():
+                known[q][s] = max(known[q].get(s, 0), v)
+
+    for i in _order(ops):
+        o = ops[i]
+        deps = {}
+        for d in o["deps"]:
+            if mark[d]:
+                deps[mark[d][0]] = max(deps.get(mark[d][0], 0), mark[d][1])
+        for s, n in sorted(deps.items(), key=lambda e: -len(clocks.get(e, {}))):
+            need(o["q"], s, n)
+        if o["arrive"]:
+            need(o["q"], *o["arrive"])
+        call = o["fn"]()
+        mark[i] = None
+        if o["sem"]:
+            count[o["sem"]] = count.get(o["sem"], 0) + o["inc"]
+            call.then_inc(T.sem[o["sem"]], o["inc"])
+            mark[i] = (o["sem"], count[o["sem"]])
+            clocks[mark[i]] = dict(known[o["q"]], **{o["sem"]: count[o["sem"]]})
+        count.update(o["more"])
+    for s, n in count.items():
+        need("G", s, n)
+
+
+def rank_program(g, core, T, topo):
+    rank = T.rank_of(core)
+    if rank is None:
+        _relay_program(g, core, T, topo)
+        return
+    Op, Fn = AluOpType, ActivationFunctionType
+    queue = {"V": g.vector, "S": g.scalar, "T": g.tensor, "G": g, "Y": g.sync}
+    ops, hist, dmas = [], {}, [0]
+
+    def place(name, a, b):
+        buf, o, w = _AT.get(name, (name, 0, None))
+        w = T[buf].shape[1] if w is None else w
+        return buf, o + a, o + (w if b is None else b)
+
+    def A(name, a=0, b=None, s=1):
+        buf, a, b = place(name, a, b)
+        return (T[buf][:, a:b:s] if s != 1 else T[buf][:, a:b], [(buf, a, b)], len(range(a, b, s)), False)
+
+    def rev(name, a, b, s=1):
+        buf, a, b = place(name, a, b)
+        return (T[buf][:, b - 1:(a - 1 if a else None):-s], [(buf, a, b)], len(range(a, b, s)), False)
+
+    def lane(name, b, n):
+        return (T[name][:, b:4 * n:4], [(name, b, b + 1)], n, False)
+
+    def ind(win, off):
+        return (win[0].indirect(off[0]), win[1] + off[1], 16 * off[2], True)
+
+    def issue(q, fn, reads, writes, cost, sem="", inc=1, lat=0.0, deps=(), arrive=None, more=()):
+        acc = [(x, False) for o in reads if isinstance(o, tuple) for x in o[1]] + [(x, True) for o in writes for x in o[1]]
+        deps = set(deps)
+        for (name, a, b), wr in acc:
+            for (a2, b2, wr2, i) in hist.get(name, []):
+                if (name[0] == "p" and ops[i]["q"] != q) or ((wr or wr2) and a < b2 and a2 < b):
+                    deps.add(i)
+        ops.append({"q": q, "fn": fn, "deps": deps, "cost": cost, "lat": lat, "sem": "s" + q if sem == "" else sem, "inc": inc,
+                    "arrive": arrive, "more": dict(more)})
+        for (name, a, b), wr in acc:
+            old = [h for h in hist.get(name, []) if not (wr and a <= h[0] and h[1] <= b and name[0] != "p")]
+            hist[name] = old + [(a, b, wr, len(ops) - 1)]
+        return len(ops) - 1
+
+    def ap(o):
+        return o[0] if isinstance(o, tuple) else o
+
+    def time(a, per):
+        return 0.07 + 0.0015 * a[2] if a[3] else max(64, a[2] * per) * 0.001
+
+    def narrow(*o):
+        return 0.5 if all(_SB.get(x[1][0][0], (0, F32))[1] in (BF, U16) for x in o) else 1.0
+
+    def tt(out, a, b, op):
+        issue("V", lambda: g.vector.tensor_tensor(out[0], a[0], b[0], op), [a, b], [out], time(a, 1 if a[1][0][0][0] == "p" else 2))
+
+    def ts(out, a, s1, o1, s2=None, o2=None):
+        if o2 is None:
+            issue("V", lambda: g.vector.tensor_scalar(out[0], a[0], ap(s1), None, o1), [a, s1], [out], time(a, narrow(out, a)))
+        else:
+            issue("V", lambda: g.vector.tensor_scalar(out[0], a[0], ap(s1), ap(s2), o1, o2), [a, s1, s2], [out], time(a, narrow(out, a)))
+
+    def cp(out, a):
+        issue("V", lambda: g.vector.tensor_copy(out[0], a[0]), [a], [out], time(a, narrow(out, a)))
+
+    def turn(out, a):
+        issue("V", lambda: g.vector.transpose(out[0], a[0]), [a], [out], time(a, narrow(out, a)))
+
+    def scan(out, d0, d1, init, o0, o1):
+        issue("V", lambda: g.vector.tensor_tensor_scan(out[0], d0[0], d1[0], ap(init), o0, o1), [d0, d1, init], [out], time(d0, narrow(out, d0, d1)))
+
+    def cumsum(out, d, init=0.0):
+        scan(out, d, d, init, Op.add, Op.max)
+
+    def own16(out, d, n):
+        scan(out, A("c16", 0, n), d, 0.0, Op.mult, Op.add)
+
+    def dealt(buf, row, n, at=0):
+        turn(A(buf, 0, n), A(row, at + 16, at + n + 16))
+        turn(A(buf, n, 2 * n + 32), A(row, at, at + n + 32))
+        return ind(A(buf, 0, 2 * n + 32), A("oX") if n == C else A("oY", 0, 1))
+
+    def red(out, a, op):
+        issue("V", lambda: g.vector.tensor_reduce(out[0], a[0], AxisListType.X, op), [a], [out], time(a, 1))
+
+    def fill(out, v):
+        issue("V", lambda: g.vector.memset(out[0], v), [], [out], time(out, narrow(out)))
+
+    def act(out, a, fn, bias=0.0, scale=1.0, acc=None):
+        issue("S", lambda: g.scalar.activation(out[0], a[0], fn, bias=ap(bias), scale=ap(scale), accum_out=ap(acc)),
+              [a, bias, scale], [out] + ([acc] if acc else []), time(a, 1) + (0.025 if acc else 0))
+
+    def quant(q, s, a):
+        issue("V", lambda: g.vector.quantize_mx(q[0], s[0], a[0]), [a], [q, s], 0.015 + 0.00027 * a[2])
+
+    def mm(out, wq, ws, xq, xs, **k):
+        issue("T", lambda: g.tensor.matmul_mx(out[0], wq[0], ws[0], xq[0], xs[0], True, True), [wq, ws, xq, xs], [out], 0.0006 * (out[2] + 16), **k)
+
+    def iota(out, pattern, base, cm):
+        if _SB[out[1][0][0]][1] == I32:
+            issue("G", lambda: g.iota(out[0], pattern, base, cm), [], [out], 0.16 + 0.002 * out[2])
+        else:
+            issue("G", lambda: g.iota(out[0], pattern, base, cm, allow_small_or_imprecise_dtypes=True), [], [out], 0.16 + 0.002 * out[2])
+
+    def dma(q, out, a, us, deps=()):
+        dmas[0] += 1
+        return issue(q, lambda: queue[q].dma_start(out[0], a[0]), [a], [out], 0.1, "d%d" % (dmas[0] - 1), 16, LOAD + us, deps)
+
+    def hbm(x):
+        return (x, [], 0, False)
+
+    def byte(o):
+        return (o[0].bitcast(dt.uint8),) + o[1:]
+
+    def word(o):
+        return (o[0].bitcast(dt.uint32),) + o[1:]
+
+    dma("S", A("ut"), hbm(T.u[:]), 0.7)
+    first = dma("Y", A("xt0"), hbm(T.x[:]), 1.8)
+    dma("Y", byte(A("qw")), hbm(T.wc[:]), 1.5, [first])
+    dma("Y", A("sw"), hbm(T.ws[:]), 0.5, [first])
+    dma("Y", A("vt"), hbm(T.v[:]), 0.7, [first])
+    iota(A("cK"), [[16, 32]], 0, 0)
+    for i, cm in enumerate((1, 16, 17)):
+        iota(A("cP", i, i + 1), [[0, 1]], 0, cm)
+    iota(A("cJ"), [[0, 20], [1, 16]], 0, 0)
+    iota(A("cI"), [[1, C + 2]], 0, 0)
+    iota(A("cD", 0, 20), [[-H, 2], [ROW, NB]], H, 0)
+    iota(A("cD", 20, 30), [[-H, NB]], ROW * (NB - 1), 0)
+    iota(A("cD", 30, 32), [[256, 2]], 0, 0)
+    issue("G", lambda: g.affine_select(T.cTY[:], T.cI[:, 0:H], [[-1, H]], Op.is_ge, -1000.0, K - 1, 0), [A("cI")], [A("cTY")], 0.55)
+    for o, v in ((A("ft"), 0.0), (A("et"), 0.0), (A("SW", C, C + 8), -BIG), (A("MN", 0, 16), 0.0), (A("MN", C + 16, C + 32), 0.0),
+                 (A("KEY", 0, 1), float(C * 512 + C)), (A("UP", 0, 1), 1.0), (A("UP", C, C + 2), 0.0), (A("DL", 0, 17), 1.0),
+                 (A("DL", C + 15, C + 32), 0.0), (A("W", 0, 1), 0.0), (A("RM", 0, 1), BIG), (A("NM", H, H + 2), 1.0),
+                 (A("CUT", 0, 1), 1.0), (A("KZ", 0, C, 2), 0.0), (A("SG", H, H + 2), 0.0)):
+        fill(o, v)
+    cp(A("oU"), A("cK", 0, 8))
+    ts(A("cP", 3, 4), A("cP", 0, 1), 15, Op.bitwise_and)
+    ts(A("cP", 4, 5), A("cP", 1, 2), 255, Op.bitwise_and)
+    ts(A("cP", 5, 6), A("cP", 2, 3), 4, Op.arith_shift_right, 1, Op.bitwise_and)
+    cp(A("cPf", 0, 6), A("cP", 0, 6))
+    r16 = A("cPf", 3, 4)
+    act(A("cPf", 6, 7), A("cPf", 5, 6), Fn.Identity, A("cPf", 4, 5), float(C + 16))
+    ts(A("oX"), A("cD", 30, 32), A("cPf", 6, 7), Op.add, float(2 * C), Op.min)
+    act(A("cPf", 7, 8), A("cPf", 5, 6), Fn.Identity, A("cPf", 4, 5), float(H + 16))
+    ts(A("oY", 0, 1), A("cPf", 7, 8), float(C), Op.min)
+    quant(A("lc0", 256, 384), A("ls0", 256, 384), A("ft"))
+    quant(A("lc1", 256, 384), A("ls1", 256, 384), A("ft"))
+    ts(A("c16"), A("cJ"), 0.5, Op.is_gt)
+    ts(A("mask"), A("cJ"), r16, Op.is_equal)
+    ts(A("cj1"), A("cK", 0, 20), r16, Op.add, 1.0, Op.add)
+    act(A("ckk", 0, 4), A("cj1", 0, 4), Fn.Identity, -0.5, 1.0)
+    act(A("ckk", 4, 8), A("cj1", 0, 4), Fn.Identity, -1.0 - H, 1.0)
+    ts(A("cb", 0, 32), A("cK"), r16, Op.add, 1.0, Op.subtract)
+    ts(A("et", 3, 515, 4), A("cI", 0, 128), A("cPf", 0, 1), Op.is_equal)
+    quant(A("qu0"), A("su0"), A("ut"))
+    ts(A("cb", 32, 64), A("cb", 0, 32), 1, Op.arith_shift_right)
+    cp(word(A("qu")), ind(word(A("qu0")), A("oU")))
+    cp(A("su"), ind(A("su0"), A("oU")))
+    ts(A("oD"), A("cD", 0, 30), r16, Op.add)
+    act(A("cTK"), A("cI"), Fn.Identity, 0.0, 512.0)
+    act(A("cIT", 0, C), A("cI", 0, C), Fn.Identity, 512.0, 1.0)
+    act(A("cIT", C, C + 2), A("cI", 0, 2), Fn.Identity, 0.0, 0.0)
+    act(A("cRev"), A("cI", 0, H + 2), Fn.Identity, float(H), -1.0)
+    act(A("c2"), A("cI", 0, H), Fn.Identity, -float(H), 2.0)
+    E = lambda n, b: A(n, 128 * b, 128 * b + 128)
+    for b in range(4):
+        quant(E("qe", b), E("se", b), A("et", 3 - b, 515 - b))
+    quant(A("qv"), A("sv"), A("vt"))
+
+    oN, oQ, oG, oE, oB, oL = A("oA", 0, 10), A("oA", 10, 20), A("oA", 20, 30), A("oA", 30, 34), A("oA", 34, 38), A("oA", 38, 48)
+    mask = lambda n: A("mask", 0, n)
+    banksH = ["pH0", "pH1", "pH2", "pS"]
+    M = lambda a, b: A("MN", 16 + a, 16 + b)
+    top = lambda c: A("DT", c, c + 1)
+    per = lambda c: A("DP", 16 * c + 15, 16 * c + 16)
+    cut = lambda c: ROW * c + H - 16 * c
+    sc = lambda i: A("SC", i, i + 1)
+    KP = A("KZ", 1, C, 2)
+
+    for t in range(R):
+        qx, sxp, lc, ls, nv = "qx%d" % t, "sx%d" % t, "lc%d" % t, "ls%d" % t, NV[t]
+        quant(A(qx, 0, C), A(sxp, 0, C), A("xt%d" % t))
+        mm(A("pS", 0, C), A("qu"), A("su"), A(qx, 0, C), A(sxp, 0, C))
+        for b in range(4):
+            mm(A("pT%d" % b, 0, C), E("qe", b), E("se", b), A(qx, 0, C), A(sxp, 0, C))
+        for b in range(4):
+            act(A("TH", C * b, C * b + C), A("pT%d" % b, 0, C), Fn.Copy, 0.0, 0.5)
+        for b in range(2):
+            act(A("TF", C * b, C * b + C), A("pT%d" % (2 + b), 0, C), Fn.Copy)
+        mm(A("pH0", 0, H), A("qu"), A("su"), A(qx, H, C), A(sxp, H, C))
+        cp(A("SW", 0, H), A("pS", 0, H))
+        act(A("SW", H, C), A("pH0", 0, H), Fn.Copy)
+        tt(M(0, H), A("pS", 0, C, 2), A("SW", 1, C, 2), Op.max)
+        tt(M(H, C), A("pS", 1, C, 2), A("SW", 2, C + 1, 2), Op.min)
+        cp(A("DT", 16, 32), dealt("TQ", "MN", H, H))
+        cp(A("DT", 0, 16), dealt("TR", "MN", H))
+        tt(A("UP", 1, C), A("pS", 1, C), A("SW", 0, C - 1), Op.is_gt)
+        tt(A("DL", 17, C + 15, 2), A("pS", 2, C, 2), M(0, H - 1), Op.is_gt)
+        tt(A("DL", 18, C + 16, 2), A("pS", 1, C - 1, 2), M(1, H), Op.is_lt)
+        tt(A("SS"), dealt("TB", "DL", C), A("cb", 32, 64), Op.add)
+        cp(A("oS"), A("SS", 0, 20))
+        tt(A("POS"), A("cI", 2, C + 2, 2), A("UP", 2, C + 1, 2), Op.subtract)
+        tt(A("PK"), A("UP", 0, C), A("UP", 1, C + 1), Op.is_gt)
+        tt(A("PKM"), A("PK", 0, C, 2), A("PK", 1, C, 2), Op.add)
+        act(A("NPB"), A("PKM"), Fn.Identity, -BIG, BIG)
+        tt(A("M1"), M(0, H), A("NPB"), Op.add)
+        act(A("J3"), A("PKM"), Fn.Identity, 0.0, 1.0, sc(0))
+        act(sc(7), sc(0), Fn.Relu, float(K), -1.0)
+        act(sc(8), sc(0), Fn.Identity, K + 0.5, -1.0)
+        act(A("NP"), A("PK", 0, NX), Fn.Identity, 1.0, -1.0)
+        cumsum(A("CNP"), A("NP"))
+        act(A("J4", 0, NX), A("CNP"), Fn.Sign, sc(8), -1.0, sc(9))
+        act(sc(1), sc(9), Fn.Identity, NX / 2.0, 0.5)
+        act(sc(12), sc(0), Fn.Sign, 0.5 - K, 1.0)
+        act(sc(10), sc(12), Fn.Identity, -0.5, -0.5)
+        act(sc(11), sc(10), Fn.Identity, 0.0, -(K + 0.5))
+        ts(A("GM", 0, 20), A("cj1"), sc(1), Op.is_gt)
+        ts(A("GM", 20, 40), A("cj1"), sc(1), Op.min)
+        for c in range(NB):
+            act(A("JK", H * c, H * c + H), M(H, C), Fn.Sign, top(16 + c), -1.0, A("ACC", c, c + 1))
+        ts(oN, A("ACC", 0, NB), -1.0, Op.mult, float(H), Op.add)
+        tt(A("KEY", 1, H + 1), ind(A("cTK"), oN), A("POS"), Op.add)
+        act(A("KEYN", 1, H + 1), A("KEY", 1, H + 1), Fn.Identity, -1.0, 1.0 / KEYS)
+        for c in range(NB):
+            act(A("KB", cut(c), ROW * c + ROW), M(-1, 16 * c + 15), Fn.Sign, top(c), -1.0)
+            act(A("KB", ROW * c, cut(c)), M(16 * c + 1, H + 1), Fn.Sign, top(c), -1.0)
+            scan(A("OS", cut(c), ROW * c + ROW), A("KB", cut(c), ROW * c + ROW), A("KEY", 0, 16 * c + 16), 0.0, Op.mult, Op.max)
+            scan(rev("OS", ROW * c, cut(c)), rev("KB", ROW * c, cut(c)), rev("KEYN", 16 * c + 1, H + 1), -1.0, Op.min, Op.max)
+        tt(A("DG"), ind(A("OS"), A("oD", 0, 20)), mask(C), Op.mult)
+        own16(A("DS"), A("DG"), C)
+        ts(A("KR", 0, NB), A("DS", H + 15, C, 16), 1.0, Op.add, KEYS, Op.mult)
+        tt(A("I1", 0, NB), A("DS", 15, H, 16), A("KR", 0, NB), Op.min)
+        ts(A("I1", NB, 2 * NB), A("I1", 0, NB), 511, Op.bitwise_and)
+        cp(oQ, A("I1", NB, 2 * NB))
+        tt(A("NG"), ind(A("SW"), oQ), A("M1"), Op.subtract)
+        tt(A("PM"), A("NG"), mask(H), Op.mult)
+        own16(A("DP"), A("PM"), H)
+        for c in range(nv, NB):
+            act(A("JK", H * c, H * c + H), A("NG"), Fn.Sign, per(c), -1.0)
+            act(A("JK2", H * c, H * c + H), A("JK", H * c, H * c + H), Fn.Relu, 0.0, 1.0, A("ACC", 10 + c, 11 + c))
+        for c in range(nv):
+            ts(A("JK", H * c, H * c + H), A("NG"), per(c), Op.is_lt)
+            cumsum(A("CS", H * c, H * c + H), A("JK", H * c, H * c + H))
+        cp(A("oA", 20, 20 + nv), A("CS", H - 1, nv * H, H))
+        cp(A("oA", 20 + nv, 30), A("ACC", 10 + nv, 20))
+        act(A("Y"), ind(A("cTY"), oG), Fn.Copy)
+        act(A("G1"), ind(A("cI"), oG), Fn.Copy)
+        red(sc(2), A("Y"), Op.max)
+        ts(A("EQ"), A("Y"), sc(2), Op.is_equal)
+        ts(sc(3), sc(2), sc(10), Op.mult, sc(11), Op.add)
+        act(sc(4), sc(2), Fn.Identity, -1.0, 1.0)
+        cumsum(A("W", 1, H + 1), A("EQ"))
+        ts(A("F1"), A("W", 1, H + 1), sc(3), Op.is_lt, sc(4), Op.add)
+        tt(KP, A("G1"), A("F1"), Op.is_le)
+        act(A("XL", 0, C, 2), A("PK", 1, C, 2), Fn.Identity, 0.0, -0.5)
+        cumsum(A("XL", 1, C, 2), KP, sc(7))
+        scan(A("ZZ"), A("KZ"), A("XL", 0, C), 0.0, Op.mult, Op.add)
+        for c in range(4):
+            act(A("JK2", H * c, H * c + H), A("ZZ", 1, C, 2), Fn.Sign, A("ckk", c, c + 1), -1.0, A("ACC", 20 + c, 21 + c))
+        tt(A("EF", 0, 4), A("ACC", 20, 24), A("ckk", 4, 8), Op.max)
+        ts(oE, A("EF", 0, 4), float(H), Op.add)
+        act(A("EF", 4, 8), A("EF", 0, 4), Fn.Identity, float(H), 1.0)
+        act(A("PQ", 0, C, 2), ind(A("cIT"), oQ), Fn.Copy)
+        act(A("PQ", 1, C, 2), ind(A("cIT"), oQ), Fn.Copy)
+        tt(A("PQ", 0, NX), A("PQ", 0, NX), A("PK", 0, NX), Op.mult)
+        tt(A("QM"), ind(A("PQ"), oE), mask(K), Op.mult)
+        own16(A("QS"), A("QM"), K)
+        tt(A("I1", 20, 24), A("QS", 15, K, 16), A("EF", 4, 8), Op.max)
+        ts(A("I1", 24, 28), A("I1", 20, 24), 511, Op.bitwise_and)
+        cp(oB, A("I1", 24, 28))
+        for b in range(4):
+            act(A("TMP", K * b, K * b + K), ind(A("TH", C * b, C * b + C), oE), Fn.Copy)
+            tt(lane("ft", b, K), ind(A("TH", C * b, C * b + C), oB), A("TMP", K * b, K * b + K), Op.add)
+        quant(A(qx, C, C + 128), A(sxp, C, C + 128), A("ft"))
+        other = T.cores[rank ^ STEP[t]]
+        direct = topo.may_write(core, other)
+        to = [other, other] if direct else _relays(T, topo, core, other)
+        eng = topo.engines(core, to[0])
+        half = len(eng) // 2
+        ids = [DstId(rid=topo.addr(d, core)[0], pnc=topo.addr(d, core)[1]) for d in to]
+        rsem = T.sem["arr%d" % t] if direct else T.sem.rin
+        moves = [
+            RemoteDMATransfer(dst_ids=[ids[0]], dma_engine_mask=_bits(eng[:half]), remote_sem=rsem, src=T[qx][:, C:C + K].bitcast(dt.uint8),
+                              dst=(T[lc][:, 192:256] if direct else T.rc[:]).bitcast(dt.uint8)),
+            RemoteDMATransfer(dst_ids=[ids[1]], dma_engine_mask=_bits(eng[half:]), remote_sem=rsem, src=T[sxp][:, C + K - 256:C + K],
+                              dst=T[ls][:, 0:256] if direct else T.rs[:]),
+        ]
+        came = len(topo.engines(other, core)) if direct else sum(len(topo.engines(c, core)) for c in _relays(T, topo, other, core))
+        sent = issue("G", lambda moves=moves, t=t: g.remote_dma_fused(moves, local_sem=T.sem["sent%d" % t]), [A(qx), A(sxp)], [], 0.3, None,
+                     lat=HOP if direct else 2 * HOP, more={"sent%d" % t: 2 * half, "arr%d" % t: came})
+        for c in range(NB):
+            scan(A("KB", ROW * (NB - 1 - c), cut(NB - 1 - c)), A("KB", cut(c), ROW * c + ROW), A("cRev", 0, 16 * c + 16), 0.0, Op.mult, Op.max)
+        tt(A("LM"), ind(A("KB"), A("oD", 20, 30)), mask(H), Op.mult)
+        own16(A("LS"), A("LM"), H)
+        tt(A("KR", NB, 2 * NB), A("DS", 15, H, 16), A("KR", 0, NB), Op.is_gt)
+        act(A("KR", 2 * NB, 3 * NB), A("KR", NB, 2 * NB), Fn.Identity, 0.0, float(H))
+        tt(A("KR", 3 * NB, 4 * NB), A("LS", 15, H, 16), A("KR", 2 * NB, 3 * NB), Op.max)
+        cp(oL, A("KR", 3 * NB, 4 * NB))
+        act(sc(5), sc(2), Fn.Identity, K - 0.5, -1.0)
+        act(A("J5"), A("W", 1, H + 1), Fn.Sign, sc(5), -1.0, sc(6))
+        ts(A("RR"), A("c2"), sc(6), Op.is_equal, -2.0 * BIG, Op.mult)
+        scan(A("RM", 1, H + 1), A("RR"), A("M1"), BIG, Op.add, Op.max)
+        tt(A("GT"), A("M1"), A("RM", 0, H), Op.is_gt)
+        act(A("NK"), KP, Fn.Identity, 1.0, -1.0)
+        tt(A("NM", 0, H), A("NK"), A("GT"), Op.is_gt)
+        scan(A("FS"), A("NM", 0, H), A("KEY", 1, H + 1), 4.0 * KEYS, Op.mult, Op.max)
+        scan(rev("BS", 0, H), rev("NM", 1, H + 1), rev("KEY", 1, H + 1), 0.0, Op.mult, Op.max)
+        tt(A("CUT", 1, H + 1), A("FS"), A("BS"), Op.is_equal)
+        cumsum(rev("SG", 0, H), A("CUT", 0, H))
+        act(A("NC"), A("CUT", 0, H), Fn.Identity, 1.0, -1.0)
+        tt(A("XL", 2, C + 2, 2), ind(A("SG"), oL), A("GT"), Op.mult)
+        scan(A("LW"), A("KZ"), A("XL", 1, C + 1), 0.0, Op.mult, Op.max)
+        ts(A("NL"), A("LW", 1, C, 2), 0.0, Op.is_equal)
+        scan(rev("NBK", 0, H), rev("NL", 0, H), rev("LW", 1, C, 2), 0.0, Op.mult, Op.add)
+        tt(A("CN"), A("NBK"), A("CUT", 0, H), Op.mult)
+        scan(A("LAB"), A("NC"), A("CN"), 0.0, Op.mult, Op.add)
+        tt(A("HM"), ind(A("LAB"), A("oS")), mask(C), Op.mult)
+        own16(A("HS"), A("HM"), C)
+        tt(A("HT", 0, 20), A("HS", 15, C, 16), A("GM", 0, 20), Op.mult)
+        tt(A("HT", 20, 40), A("HT", 0, 20), A("GM", 20, 40), Op.max)
+        ts(A("oH"), A("HT", 20, 40), 1.0, Op.subtract)
+        xn = "xt%d" % (t + 1)
+        for b in (2, 3, 0, 1):
+            mm(A(banksH[b], 0, 128), E("qw", b), E("sw", b), A(lc, 192, 320), A(ls, 192, 320), deps=[sent], arrive=("arr%d" % t, came))
+            act(A("HR", K * b, K * b + K), A(banksH[b], 0, K), Fn.Relu, 0.0, 0.03125)
+        for b in range(2):
+            act(A("GG", C * b, C * b + C), ind(A("HR", K * b, K * b + K), A("oH")), Fn.Copy)
+            tt(lane(xn, b, C), A("pT%d" % b, 0, C), A("GG", C * b, C * b + C), Op.add)
+        for b in range(2, 4):
+            tt(lane(xn, b, C), ind(A("HR", K * b, K * b + K), A("oH")), A("TF", C * (b - 2), C * (b - 1)), Op.add)
+
+    act(A("ER"), ind(A("cI"), oE), Fn.Copy)
+    act(A("OLR"), ind(A("ER"), A("oH")), Fn.Copy)
+    dma("G", hbm(T.ol[:]), (T.OLR[0:128:16, :], A("OLR")[1]), 0.0)
+    quant(A("qx2"), A("sx2"), A("xt2"))
+    mm(A("pH0", 0, H), A("qv"), A("sv"), A("qx2", 0, H), A("sx2", 0, H))
+    mm(A("pH1", 0, H), A("qv"), A("sv"), A("qx2", H, C), A("sx2", H, C))
+    dma("Y", hbm(T.oc[:]), byte(A("qx2")), 0.9)
+    for k in range(4):
+        dma("YS"[k % 2], hbm(T.osc[4 * k:4 * k + 4, :]), (T.sx2[32 * k:32 * k + 4, :], A("sx2")[1]), 0.0)
+    cp(A("YO", 0, H), A("pH0", 0, H))
+    act(A("YO", H, C), A("pH1", 0, H), Fn.Copy)
+    dma("Y", hbm(T.y[:, 0:H]), A("YO", 0, H), 0.5)
+    dma("S", hbm(T.y[:, H:C]), A("YO", H, C), 0.5)
+    _emit(ops, queue, T)

@@ -10,7 +10,7 @@ BIG = 2.0 ** 96
 KEYS = 2.0 ** 18
 NV = [5, 6]
 NX = 132
-HOP, WAKE, LOAD, SLACK, TRIES = 3.5, 0.08, 2.0, 0.02, 1500
+HOP, WAKE, LOAD, SLACK, TRIES = 3.5, 0.17, 2.0, 0.02, 1500
 F32, BF, I32, U16, CODE, PLANE = "float32", "bfloat16", "int32", "uint16", "float8_e4m3fn_x4", "uint8"
 
 _SB = {
@@ -20,18 +20,19 @@ _SB = {
     "qx0": (C + 128, CODE), "sx0": (C + 128, PLANE), "qx1": (C + 128, CODE), "sx1": (C + 128, PLANE), "qx2": (C, CODE), "sx2": (C, PLANE),
     "lc0": (384, CODE), "ls0": (384, PLANE), "lc1": (384, CODE), "ls1": (384, PLANE), "rc": (64, CODE), "rs": (256, PLANE),
     "cI": (C + 2, F32), "cJ": (C, BF), "cP": (8, I32), "cPf": (8, F32), "cK": (32, F32), "cD": (32, F32), "cTK": (C + 2, F32), "cIT": (C + 2, F32),
-    "cRev": (H + 2, BF), "cTY": (H, F32), "mask": (C, BF), "c16": (C, BF), "c2": (H, BF), "cj1": (20, F32), "ckk": (8, F32), "cb": (64, I32),
+    "cRev": (H + 2, BF), "cTY": (H, F32), "mask": (C, BF), "c16": (C, BF), "c2": (H, BF), "mask2": (C, BF), "cL": (H, BF), "cjw": (20, F32),
+    "cj1": (20, F32), "ckk": (8, F32), "cb": (64, I32),
     "oU": (8, U16), "oX": (2, U16), "oY": (2, U16), "oD": (30, U16), "oA": (64, U16), "oH": (20, U16), "oS": (20, U16),
     "SW": (C + 8, F32), "KB": (NB * ROW, BF), "OS": (NB * ROW, F32), "JK": (NB * H, BF), "JK2": (NB * H, BF), "CS": (NB * H, BF),
     "TR": (C + 32, F32), "TQ": (C + 32, F32), "TB": (2 * C + 32, BF),
-    "ACC": (32, F32), "I1": (40, I32), "SC": (16, F32), "PQ": (C, F32), "SG": (H + 2, BF), "LAB": (H, BF),
+    "ACC": (32, F32), "I1": (40, I32), "SC": (16, F32), "PQ": (C, F32), "SG": (H + 2, BF), "LAB": (H + NX, BF),
     "TH": (4 * C, BF), "TF": (2 * C, BF), "TMP": (4 * K, BF), "HR": (4 * K, F32), "GG": (2 * C, F32),
     "ER": (K, F32), "OLR": (C, F32), "YO": (C, F32),
 }
 _ROWS = {
     "rf": (F32, {"MN": C + 32, "DT": 32, "M1": H, "POS": H, "KEY": H + 2, "KEYN": H + 2, "DG": C, "DS": C, "NG": H, "PM": H, "DP": H,
                  "GM": 40, "EF": 8, "QM": K, "QS": K, "SS": 32, "KR": 40, "RM": H + 2, "FS": H, "BS": H, "HT": 40}),
-    "rb": (BF, {"UP": C + 2, "PK": C, "PKM": H, "NPB": H, "Y": H, "G1": H, "EQ": H, "W": H + 2, "F1": H, "NK": H, "KZ": C, "XL": C + 2,
+    "rb": (BF, {"UP": C + 2, "PK": C, "PKM": H, "NPB": H, "Y": H, "G1": H, "EQ": C, "W": C, "F1": C, "NK": H, "KZ": C, "XL": C + 2,
                 "ZZ": C, "LW": C, "NP": NX, "CNP": NX, "DL": C + 32, "LM": H, "LS": H, "RR": H, "GT": H, "NM": H + 2, "NL": H,
                 "CUT": H + 2, "NC": H, "NBK": H, "CN": H, "HM": C, "HS": C, "J3": H, "J4": H, "J5": H}),
 }
@@ -291,7 +292,7 @@ def rank_program(g, core, T, topo):
     issue("G", lambda: g.affine_select(T.cTY[:], T.cI[:, 0:H], [[-1, H]], Op.is_ge, -1000.0, K - 1, 0), [A("cI")], [A("cTY")], 0.55)
     for o, v in ((A("ft"), 0.0), (A("et"), 0.0), (A("SW", C, C + 8), -BIG), (A("MN", 0, 16), 0.0), (A("MN", C + 16, C + 32), 0.0),
                  (A("KEY", 0, 1), float(C * 512 + C)), (A("UP", 0, 1), 1.0), (A("UP", C, C + 2), 0.0), (A("DL", 0, 17), 1.0),
-                 (A("DL", C + 15, C + 32), 0.0), (A("W", 0, 1), 0.0), (A("RM", 0, 1), BIG), (A("NM", H, H + 2), 1.0),
+                 (A("DL", C + 15, C + 32), 0.0), (A("F1", 1, C, 2), 0.0), (A("RM", 0, 1), BIG), (A("NM", H, H + 2), 1.0),
                  (A("CUT", 0, 1), 1.0), (A("KZ", 0, C, 2), 0.0), (A("SG", H, H + 2), 0.0)):
         fill(o, v)
     cp(A("oU"), A("cK", 0, 8))
@@ -308,6 +309,9 @@ def rank_program(g, core, T, topo):
     quant(A("lc1", 256, 384), A("ls1", 256, 384), A("ft"))
     ts(A("c16"), A("cJ"), 0.5, Op.is_gt)
     ts(A("mask"), A("cJ"), r16, Op.is_equal)
+    act(A("mask2", 0, H), A("mask", 0, H), Fn.Copy)
+    act(A("mask2", H, C), A("mask", 0, H), Fn.Identity, 0.0, KEYS)
+    act(A("cL"), A("c16", 0, H), Fn.Identity, -KEYS, 2.0 * KEYS)
     ts(A("cj1"), A("cK", 0, 20), r16, Op.add, 1.0, Op.add)
     act(A("ckk", 0, 4), A("cj1", 0, 4), Fn.Identity, -0.5, 1.0)
     act(A("ckk", 4, 8), A("cj1", 0, 4), Fn.Identity, -1.0 - H, 1.0)
@@ -323,6 +327,8 @@ def rank_program(g, core, T, topo):
     act(A("cIT", C, C + 2), A("cI", 0, 2), Fn.Identity, 0.0, 0.0)
     act(A("cRev"), A("cI", 0, H + 2), Fn.Identity, float(H), -1.0)
     act(A("c2"), A("cI", 0, H), Fn.Identity, -float(H), 2.0)
+    act(A("LAB", H, H + NX), A("cI", 1, NX + 1), Fn.Copy)
+    act(A("cjw"), A("cj1"), Fn.Identity, H - 1.0, 1.0)
     E = lambda n, b: A(n, 128 * b, 128 * b + 128)
     for b in range(4):
         quant(E("qe", b), E("se", b), A("et", 3 - b, 515 - b))
@@ -359,7 +365,6 @@ def rank_program(g, core, T, topo):
         tt(A("DL", 17, C + 15, 2), A("pS", 2, C, 2), M(0, H - 1), Op.is_gt)
         tt(A("DL", 18, C + 16, 2), A("pS", 1, C - 1, 2), M(1, H), Op.is_lt)
         tt(A("SS"), dealt("TB", "DL", C), A("cb", 32, 64), Op.add)
-        cp(A("oS"), A("SS", 0, 20))
         tt(A("POS"), A("cI", 2, C + 2, 2), A("UP", 2, C + 1, 2), Op.subtract)
         tt(A("PK"), A("UP", 0, C), A("UP", 1, C + 1), Op.is_gt)
         tt(A("PKM"), A("PK", 0, C, 2), A("PK", 1, C, 2), Op.add)
@@ -375,8 +380,10 @@ def rank_program(g, core, T, topo):
         act(sc(12), sc(0), Fn.Sign, 0.5 - K, 1.0)
         act(sc(10), sc(12), Fn.Identity, -0.5, -0.5)
         act(sc(11), sc(10), Fn.Identity, 0.0, -(K + 0.5))
-        ts(A("GM", 0, 20), A("cj1"), sc(1), Op.is_gt)
-        ts(A("GM", 20, 40), A("cj1"), sc(1), Op.min)
+        ts(A("GM", 0, 20), A("cj1"), sc(1), Op.is_le)
+        tt(A("GM", 20, 40), A("GM", 0, 20), A("cjw"), Op.mult)
+        tt(A("HT", 0, 20), A("SS", 0, 20), A("GM", 20, 40), Op.max)
+        cp(A("oS"), A("HT", 0, 20))
         for c in range(NB):
             act(A("JK", H * c, H * c + H), M(H, C), Fn.Sign, top(16 + c), -1.0, A("ACC", c, c + 1))
         ts(oN, A("ACC", 0, NB), -1.0, Op.mult, float(H), Op.add)
@@ -387,10 +394,10 @@ def rank_program(g, core, T, topo):
             act(A("KB", ROW * c, cut(c)), M(16 * c + 1, H + 1), Fn.Sign, top(c), -1.0)
             scan(A("OS", cut(c), ROW * c + ROW), A("KB", cut(c), ROW * c + ROW), A("KEY", 0, 16 * c + 16), 0.0, Op.mult, Op.max)
             scan(rev("OS", ROW * c, cut(c)), rev("KB", ROW * c, cut(c)), rev("KEYN", 16 * c + 1, H + 1), -1.0, Op.min, Op.max)
-        tt(A("DG"), ind(A("OS"), A("oD", 0, 20)), mask(C), Op.mult)
-        own16(A("DS"), A("DG"), C)
-        ts(A("KR", 0, NB), A("DS", H + 15, C, 16), 1.0, Op.add, KEYS, Op.mult)
-        tt(A("I1", 0, NB), A("DS", 15, H, 16), A("KR", 0, NB), Op.min)
+        tt(A("DG"), ind(A("OS"), A("oD", 0, 20)), A("mask2"), Op.mult)
+        scan(A("DS", 0, H), A("cL"), A("DG", 0, H), 0.0, Op.min, Op.add)
+        own16(A("DS", H, C), A("DG", H, C), H)
+        tt(A("I1", 0, NB), A("DS", 15, H, 16), A("DS", H + 15, C, 16), Op.min)
         ts(A("I1", NB, 2 * NB), A("I1", 0, NB), 511, Op.bitwise_and)
         cp(oQ, A("I1", NB, 2 * NB))
         tt(A("NG"), ind(A("SW"), oQ), A("M1"), Op.subtract)
@@ -407,19 +414,20 @@ def rank_program(g, core, T, topo):
         act(A("Y"), ind(A("cTY"), oG), Fn.Copy)
         act(A("G1"), ind(A("cI"), oG), Fn.Copy)
         red(sc(2), A("Y"), Op.max)
-        ts(A("EQ"), A("Y"), sc(2), Op.is_equal)
+        ts(A("EQ", 0, C, 2), A("Y"), sc(2), Op.is_equal)
+        ts(A("EQ", 1, C, 2), A("G1"), sc(2), Op.subtract, -1024.0, Op.mult)
+        ts(A("F1", 0, C, 2), A("G1"), sc(2), Op.subtract, 1024.0, Op.mult)
         ts(sc(3), sc(2), sc(10), Op.mult, sc(11), Op.add)
-        act(sc(4), sc(2), Fn.Identity, -1.0, 1.0)
-        cumsum(A("W", 1, H + 1), A("EQ"))
-        ts(A("F1"), A("W", 1, H + 1), sc(3), Op.is_lt, sc(4), Op.add)
-        tt(KP, A("G1"), A("F1"), Op.is_le)
+        scan(A("W"), A("EQ"), A("F1"), 0.0, Op.add, Op.add)
+        ts(KP, A("W", 0, C, 2), sc(3), Op.is_lt)
         act(A("XL", 0, C, 2), A("PK", 1, C, 2), Fn.Identity, 0.0, -0.5)
         cumsum(A("XL", 1, C, 2), KP, sc(7))
         scan(A("ZZ"), A("KZ"), A("XL", 0, C), 0.0, Op.mult, Op.add)
         for c in range(4):
             act(A("JK2", H * c, H * c + H), A("ZZ", 1, C, 2), Fn.Sign, A("ckk", c, c + 1), -1.0, A("ACC", 20 + c, 21 + c))
         tt(A("EF", 0, 4), A("ACC", 20, 24), A("ckk", 4, 8), Op.max)
-        ts(oE, A("EF", 0, 4), float(H), Op.add)
+        for c in range(4):
+            ts(A("oA", 30 + c, 31 + c), A("ACC", 20 + c, 21 + c), A("ckk", 4 + c, 5 + c), Op.max, float(H), Op.add)
         act(A("EF", 4, 8), A("EF", 0, 4), Fn.Identity, float(H), 1.0)
         act(A("PQ", 0, C, 2), ind(A("cIT"), oQ), Fn.Copy)
         act(A("PQ", 1, C, 2), ind(A("cIT"), oQ), Fn.Copy)
@@ -453,12 +461,12 @@ def rank_program(g, core, T, topo):
             scan(A("KB", ROW * (NB - 1 - c), cut(NB - 1 - c)), A("KB", cut(c), ROW * c + ROW), A("cRev", 0, 16 * c + 16), 0.0, Op.mult, Op.max)
         tt(A("LM"), ind(A("KB"), A("oD", 20, 30)), mask(H), Op.mult)
         own16(A("LS"), A("LM"), H)
-        tt(A("KR", NB, 2 * NB), A("DS", 15, H, 16), A("KR", 0, NB), Op.is_gt)
+        tt(A("KR", NB, 2 * NB), A("DS", 15, H, 16), A("DS", H + 15, C, 16), Op.is_gt)
         act(A("KR", 2 * NB, 3 * NB), A("KR", NB, 2 * NB), Fn.Identity, 0.0, float(H))
         tt(A("KR", 3 * NB, 4 * NB), A("LS", 15, H, 16), A("KR", 2 * NB, 3 * NB), Op.max)
         cp(oL, A("KR", 3 * NB, 4 * NB))
         act(sc(5), sc(2), Fn.Identity, K - 0.5, -1.0)
-        act(A("J5"), A("W", 1, H + 1), Fn.Sign, sc(5), -1.0, sc(6))
+        act(A("J5"), A("W", 1, C, 2), Fn.Sign, sc(5), -1.0, sc(6))
         ts(A("RR"), A("c2"), sc(6), Op.is_equal, -2.0 * BIG, Op.mult)
         scan(A("RM", 1, H + 1), A("RR"), A("M1"), BIG, Op.add, Op.max)
         tt(A("GT"), A("M1"), A("RM", 0, H), Op.is_gt)
@@ -469,17 +477,16 @@ def rank_program(g, core, T, topo):
         tt(A("CUT", 1, H + 1), A("FS"), A("BS"), Op.is_equal)
         cumsum(rev("SG", 0, H), A("CUT", 0, H))
         act(A("NC"), A("CUT", 0, H), Fn.Identity, 1.0, -1.0)
+        ts(A("XL", 1, C, 2), A("XL", 1, C, 2), sc(1), Op.max)
         tt(A("XL", 2, C + 2, 2), ind(A("SG"), oL), A("GT"), Op.mult)
         scan(A("LW"), A("KZ"), A("XL", 1, C + 1), 0.0, Op.mult, Op.max)
         ts(A("NL"), A("LW", 1, C, 2), 0.0, Op.is_equal)
         scan(rev("NBK", 0, H), rev("NL", 0, H), rev("LW", 1, C, 2), 0.0, Op.mult, Op.add)
         tt(A("CN"), A("NBK"), A("CUT", 0, H), Op.mult)
-        scan(A("LAB"), A("NC"), A("CN"), 0.0, Op.mult, Op.add)
+        scan(A("LAB", 0, H), A("NC"), A("CN"), 0.0, Op.mult, Op.add)
         tt(A("HM"), ind(A("LAB"), A("oS")), mask(C), Op.mult)
         own16(A("HS"), A("HM"), C)
-        tt(A("HT", 0, 20), A("HS", 15, C, 16), A("GM", 0, 20), Op.mult)
-        tt(A("HT", 20, 40), A("HT", 0, 20), A("GM", 20, 40), Op.max)
-        ts(A("oH"), A("HT", 20, 40), 1.0, Op.subtract)
+        ts(A("oH"), A("HS", 15, C, 16), 1.0, Op.subtract)
         xn = "xt%d" % (t + 1)
         for b in (2, 3, 0, 1):
             mm(A(banksH[b], 0, 128), E("qw", b), E("sw", b), A(lc, 192, 320), A(ls, 192, 320), deps=[sent], arrive=("arr%d" % t, came))

@@ -7,10 +7,17 @@ H = C // 2
 NB = H // 16
 ROW = H + 16
 BIG = 2.0 ** 96
-KEYS = 2.0 ** 18
-NV = [5, 6]
-NX = 132
-HOP, WAKE, LOAD, SLACK, TRIES = 3.5, 0.17, 2.0, 0.02, 1500
+FAR = 2.0 ** 98
+UNIT = 2.0 ** -18
+AT, WF = 48, 432
+NV = [6, 6]
+NE = 0
+NF = 2
+NFA = 2
+HS_ON = "V"
+Y_ON = "S"
+SOFT = False
+HOP, WAKE, LOAD, SLACK, TRIES = 3.0, 0.17, 2.0, 0.02, 1500
 F32, BF, I32, U16, CODE, PLANE = "float32", "bfloat16", "int32", "uint16", "float8_e4m3fn_x4", "uint8"
 
 _SB = {
@@ -19,22 +26,21 @@ _SB = {
     "qw": (512, CODE), "sw": (512, PLANE), "qe": (512, CODE), "se": (512, PLANE),
     "qx0": (C + 128, CODE), "sx0": (C + 128, PLANE), "qx1": (C + 128, CODE), "sx1": (C + 128, PLANE), "qx2": (C, CODE), "sx2": (C, PLANE),
     "lc0": (384, CODE), "ls0": (384, PLANE), "lc1": (384, CODE), "ls1": (384, PLANE), "rc": (64, CODE), "rs": (256, PLANE),
-    "cI": (C + 2, F32), "cJ": (C, BF), "cP": (8, I32), "cPf": (8, F32), "cK": (32, F32), "cD": (32, F32), "cTK": (C + 2, F32), "cIT": (C + 2, F32),
-    "cRev": (H + 2, BF), "cTY": (H, F32), "mask": (C, BF), "c16": (C, BF), "c2": (H, BF), "mask2": (C, BF), "cL": (H, BF), "cjw": (20, F32),
-    "cj1": (20, F32), "ckk": (8, F32), "cb": (64, I32),
-    "oU": (8, U16), "oX": (2, U16), "oY": (2, U16), "oD": (30, U16), "oA": (64, U16), "oH": (20, U16), "oS": (20, U16),
-    "SW": (C + 8, F32), "KB": (NB * ROW, BF), "OS": (NB * ROW, F32), "JK": (NB * H, BF), "JK2": (NB * H, BF), "CS": (NB * H, BF),
-    "TR": (C + 32, F32), "TQ": (C + 32, F32), "TB": (2 * C + 32, BF),
-    "ACC": (32, F32), "I1": (40, I32), "SC": (16, F32), "PQ": (C, F32), "SG": (H + 2, BF), "LAB": (H + NX, BF),
-    "TH": (4 * C, BF), "TF": (2 * C, BF), "TMP": (4 * K, BF), "HR": (4 * K, F32), "GG": (2 * C, F32),
+    "cI": (C + 16, F32), "cJ": (C, BF), "cP": (8, I32), "cPf": (8, F32), "cK": (32, F32), "cTK": (C + 16, F32),
+    "cRev": (H + 2, BF), "cTY": (C + 16, BF), "mask": (C, BF), "cM": (C, BF), "cR": (C, BF), "cC": (C, BF), "c16": (C, BF), "c01": (C, BF),
+    "cPn": (H, F32), "cj": (20, F32), "cm2": (NB, F32), "cb": (20, F32), "ck": (16, F32),
+    "oU": (8, U16), "oA": (80, U16), "oH": (20, U16), "oS": (20, U16),
+    "SW": (C + 8, F32), "KB": (NB * ROW, BF), "JK": (NB * H, BF), "JK2": (NB * H, BF), "CS": (NB * H, BF),
+    "ACC": (32, F32), "I1": (20, I32), "SC": (16, F32), "LAB": (H + K, BF), "FA": (4 * WF, BF), "EC": (WF, F32),
+    "TH": (4 * C, BF), "TF": (2 * C, BF), "TMP": (4 * C, BF), "HR": (4 * K, F32), "GG": (2 * C, F32),
     "ER": (K, F32), "OLR": (C, F32), "YO": (C, F32),
 }
 _ROWS = {
-    "rf": (F32, {"MN": C + 32, "DT": 32, "M1": H, "POS": H, "KEY": H + 2, "KEYN": H + 2, "DG": C, "DS": C, "NG": H, "PM": H, "DP": H,
-                 "GM": 40, "EF": 8, "QM": K, "QS": K, "SS": 32, "KR": 40, "RM": H + 2, "FS": H, "BS": H, "HT": 40}),
-    "rb": (BF, {"UP": C + 2, "PK": C, "PKM": H, "NPB": H, "Y": H, "G1": H, "EQ": C, "W": C, "F1": C, "NK": H, "KZ": C, "XL": C + 2,
-                "ZZ": C, "LW": C, "NP": NX, "CNP": NX, "DL": C + 32, "LM": H, "LS": H, "RR": H, "GT": H, "NM": H + 2, "NL": H,
-                "CUT": H + 2, "NC": H, "NBK": H, "CN": H, "HM": C, "HS": C, "J3": H, "J4": H, "J5": H}),
+    "rf": (F32, {"MN": C + 32, "X1": C, "DT": C, "US": H, "POS": H, "KEY": H + 2, "KEYN": H + 2, "LR": C, "X2": C, "DS": H, "NG": H, "X3": H,
+                 "DP": H, "SM": 120, "FS": H + 2, "BS": H, "HT": 20, "PF": 24}),
+    "rb": (BF, {"UP": C + 2, "DL": C, "X4": C, "D4": C, "X5": H, "D5": H, "LL": H, "X6": H, "D6": H, "PN": 2 * K + 2, "X7": 2 * K, "D7": 2 * K,
+                "Y": H, "MU": H, "OUT": H, "LE": H, "LT": H, "UU": H, "CK": H + 2, "CK2": H, "NM": H, "NA": H, "AN": H + 2, "KP": H, "LP": H, "W0": H,
+                "W1": H, "SD": H, "NS": H, "GO": H, "HO": H, "LB": H + 2, "XP": H, "Z": H, "O": H, "HM": C, "X8": C, "HS": C}),
 }
 _AT = {}
 for _b, (_d, _rows) in _ROWS.items():
@@ -102,7 +108,8 @@ def _play(ops, after, way):
         end = max(end, done)
         order.append(best)
         for j in after[best]:
-            ready[j] = max(ready[j], done + WAKE)
+            if ops[j]["deps"][best]:
+                ready[j] = max(ready[j], done + WAKE)
             left[j] -= 1
             if not left[j]:
                 free[ops[j]["q"]].append(j)
@@ -114,7 +121,7 @@ def _order(ops):
     if key not in _ORDERS:
         way, after = [0.0] * len(ops), [[] for o in ops]
         for i in reversed(range(len(ops))):
-            way[i] = ops[i]["cost"] + ops[i]["lat"] + max([way[j] + WAKE for j in after[i]], default=0.0)
+            way[i] = ops[i]["cost"] + ops[i]["lat"] + max([way[j] + WAKE * ops[j]["deps"][i] for j in after[i]], default=0.0)
             for d in ops[i]["deps"]:
                 after[d].append(i)
         best, seed = _play(ops, after, way), 1
@@ -142,8 +149,8 @@ def _emit(ops, queue, T):
     for i in _order(ops):
         o = ops[i]
         deps = {}
-        for d in o["deps"]:
-            if mark[d]:
+        for d, hard in o["deps"].items():
+            if mark[d] and hard:
                 deps[mark[d][0]] = max(deps.get(mark[d][0], 0), mark[d][1])
         for s, n in sorted(deps.items(), key=lambda e: -len(clocks.get(e, {}))):
             need(o["q"], s, n)
@@ -177,37 +184,40 @@ def rank_program(g, core, T, topo):
 
     def A(name, a=0, b=None, s=1):
         buf, a, b = place(name, a, b)
-        return (T[buf][:, a:b:s] if s != 1 else T[buf][:, a:b], [(buf, a, b)], len(range(a, b, s)), False)
+        return (T[buf][:, a:b:s] if s != 1 else T[buf][:, a:b], [(buf, a, b, s)], len(range(a, b, s)), False)
 
     def rev(name, a, b, s=1):
         buf, a, b = place(name, a, b)
-        return (T[buf][:, b - 1:(a - 1 if a else None):-s], [(buf, a, b)], len(range(a, b, s)), False)
-
-    def lane(name, b, n):
-        return (T[name][:, b:4 * n:4], [(name, b, b + 1)], n, False)
+        last = range(a, b, s)[-1]
+        return (T[buf][:, last:(a - 1 if a else None):-s], [(buf, a, b, s)], len(range(a, b, s)), False)
 
     def ind(win, off):
         return (win[0].indirect(off[0]), win[1] + off[1], 16 * off[2], True)
 
+    def meet(x, y):
+        return x[1] < y[2] and y[1] < x[2] and (x[3] != y[3] or (x[1] - y[1]) % x[3] == 0)
+
     def issue(q, fn, reads, writes, cost, sem="", inc=1, lat=0.0, deps=(), arrive=None, more=()):
         acc = [(x, False) for o in reads if isinstance(o, tuple) for x in o[1]] + [(x, True) for o in writes for x in o[1]]
-        deps = set(deps)
-        for (name, a, b), wr in acc:
-            for (a2, b2, wr2, i) in hist.get(name, []):
-                if (name[0] == "p" and ops[i]["q"] != q) or ((wr or wr2) and a < b2 and a2 < b):
-                    deps.add(i)
+        deps = {d: True for d in deps}
+        for x, wr in acc:
+            for (y, wr2, i) in hist.get(x[0], []):
+                same = ops[i]["q"] == q
+                if (x[0][0] == "p" and not same) or ((wr or wr2) and meet(x, y)):
+                    deps[i] = deps.get(i, False) or not (SOFT and same and wr and q in "VS" and ops[i]["sem"] == "s" + q and sem == "")
         ops.append({"q": q, "fn": fn, "deps": deps, "cost": cost, "lat": lat, "sem": "s" + q if sem == "" else sem, "inc": inc,
                     "arrive": arrive, "more": dict(more)})
-        for (name, a, b), wr in acc:
-            old = [h for h in hist.get(name, []) if not (wr and a <= h[0] and h[1] <= b and name[0] != "p")]
-            hist[name] = old + [(a, b, wr, len(ops) - 1)]
+        for x, wr in acc:
+            old = [h for h in hist.get(x[0], []) if not (wr and x[1] <= h[0][1] and h[0][2] <= x[2] and x[0][0] != "p" and
+                                                         (x[3] == 1 or x[3] == h[0][3] and meet(x, h[0])))]
+            hist[x[0]] = old + [(x, wr, len(ops) - 1)]
         return len(ops) - 1
 
     def ap(o):
         return o[0] if isinstance(o, tuple) else o
 
     def time(a, per):
-        return 0.07 + 0.0015 * a[2] if a[3] else max(64, a[2] * per) * 0.001
+        return 0.06 + 0.0015 * a[2] if a[3] else max(64, a[2] * per) * 0.001
 
     def narrow(*o):
         return 0.5 if all(_SB.get(x[1][0][0], (0, F32))[1] in (BF, U16) for x in o) else 1.0
@@ -221,11 +231,11 @@ def rank_program(g, core, T, topo):
         else:
             issue("V", lambda: g.vector.tensor_scalar(out[0], a[0], ap(s1), ap(s2), o1, o2), [a, s1, s2], [out], time(a, narrow(out, a)))
 
-    def cp(out, a):
-        issue("V", lambda: g.vector.tensor_copy(out[0], a[0]), [a], [out], time(a, narrow(out, a)))
-
-    def turn(out, a):
-        issue("V", lambda: g.vector.transpose(out[0], a[0]), [a], [out], time(a, narrow(out, a)))
+    def cp(out, a, q="V"):
+        if q == "S":
+            issue("S", lambda: g.scalar.activation(out[0], a[0], Fn.Copy), [a], [out], time(a, 1))
+        else:
+            issue("V", lambda: g.vector.tensor_copy(out[0], a[0]), [a], [out], time(a, narrow(out, a)))
 
     def scan(out, d0, d1, init, o0, o1):
         issue("V", lambda: g.vector.tensor_tensor_scan(out[0], d0[0], d1[0], ap(init), o0, o1), [d0, d1, init], [out], time(d0, narrow(out, d0, d1)))
@@ -233,16 +243,12 @@ def rank_program(g, core, T, topo):
     def cumsum(out, d, init=0.0):
         scan(out, d, d, init, Op.add, Op.max)
 
-    def own16(out, d, n):
-        scan(out, A("c16", 0, n), d, 0.0, Op.mult, Op.add)
+    def carry(out, d):
+        scan(out, A("cR", 0, d[2]), d, 0.0, Op.add, Op.min)
 
-    def dealt(buf, row, n, at=0):
-        turn(A(buf, 0, n), A(row, at + 16, at + n + 16))
-        turn(A(buf, n, 2 * n + 32), A(row, at, at + n + 32))
-        return ind(A(buf, 0, 2 * n + 32), A("oX") if n == C else A("oY", 0, 1))
-
-    def red(out, a, op):
-        issue("V", lambda: g.vector.tensor_reduce(out[0], a[0], AxisListType.X, op), [a], [out], time(a, 1))
+    def deal(out, tmp, row):
+        scan(tmp, row, A("cM", 0, row[2]), FAR, Op.min, Op.max)
+        carry(out, tmp)
 
     def fill(out, v):
         issue("V", lambda: g.vector.memset(out[0], v), [], [out], time(out, narrow(out)))
@@ -258,7 +264,8 @@ def rank_program(g, core, T, topo):
         issue("T", lambda: g.tensor.matmul_mx(out[0], wq[0], ws[0], xq[0], xs[0], True, True), [wq, ws, xq, xs], [out], 0.0006 * (out[2] + 16), **k)
 
     def iota(out, pattern, base, cm):
-        if _SB[out[1][0][0]][1] == I32:
+        buf = out[1][0][0]
+        if _SB[buf][1] == I32:
             issue("G", lambda: g.iota(out[0], pattern, base, cm), [], [out], 0.16 + 0.002 * out[2])
         else:
             issue("G", lambda: g.iota(out[0], pattern, base, cm, allow_small_or_imprecise_dtypes=True), [], [out], 0.16 + 0.002 * out[2])
@@ -282,164 +289,172 @@ def rank_program(g, core, T, topo):
     dma("Y", A("sw"), hbm(T.ws[:]), 0.5, [first])
     dma("Y", A("vt"), hbm(T.v[:]), 0.7, [first])
     iota(A("cK"), [[16, 32]], 0, 0)
-    for i, cm in enumerate((1, 16, 17)):
-        iota(A("cP", i, i + 1), [[0, 1]], 0, cm)
+    iota(A("cP", 0, 1), [[0, 1]], 0, 1)
     iota(A("cJ"), [[0, 20], [1, 16]], 0, 0)
-    iota(A("cI"), [[1, C + 2]], 0, 0)
-    iota(A("cD", 0, 20), [[-H, 2], [ROW, NB]], H, 0)
-    iota(A("cD", 20, 30), [[-H, NB]], ROW * (NB - 1), 0)
-    iota(A("cD", 30, 32), [[256, 2]], 0, 0)
-    issue("G", lambda: g.affine_select(T.cTY[:], T.cI[:, 0:H], [[-1, H]], Op.is_ge, -1000.0, K - 1, 0), [A("cI")], [A("cTY")], 0.55)
-    for o, v in ((A("ft"), 0.0), (A("et"), 0.0), (A("SW", C, C + 8), -BIG), (A("MN", 0, 16), 0.0), (A("MN", C + 16, C + 32), 0.0),
-                 (A("KEY", 0, 1), float(C * 512 + C)), (A("UP", 0, 1), 1.0), (A("UP", C, C + 2), 0.0), (A("DL", 0, 17), 1.0),
-                 (A("DL", C + 15, C + 32), 0.0), (A("F1", 1, C, 2), 0.0), (A("RM", 0, 1), BIG), (A("NM", H, H + 2), 1.0),
-                 (A("CUT", 0, 1), 1.0), (A("KZ", 0, C, 2), 0.0), (A("SG", H, H + 2), 0.0)):
+    iota(A("cI"), [[1, C + 16]], 0, 0)
+    for b in range(4):
+        iota(A("FA", WF * b, WF * b + WF), [[0, WF]], 0, 0)
+    iota(A("c01"), [[0, H], [1, 2]], 0, 0)
+    iota(A("EC"), [[1, WF]], -AT - C, 0)
+    for o, v in ((A("ft"), 0.0), (A("et"), 0.0), (A("SW", C, C + 8), -BIG), (A("MN", 0, 16), 0.0),
+                 (A("KEY", 0, 1), (C * 512 + C) * UNIT), (A("UP", 0, 1), 1.0), (A("DL", 0, 1), 1.0), (A("DL", C - 1, C), 0.0),
+                 (A("PN", K, K + 1), 0.0), (A("CK", 0, 1), -K - 1.0), (A("LB", 0, 1), 0.0), (A("AN", 0, 1), 0.0), (A("FS", 0, 1), 4.0)):
         fill(o, v)
     cp(A("oU"), A("cK", 0, 8))
-    ts(A("cP", 3, 4), A("cP", 0, 1), 15, Op.bitwise_and)
-    ts(A("cP", 4, 5), A("cP", 1, 2), 255, Op.bitwise_and)
-    ts(A("cP", 5, 6), A("cP", 2, 3), 4, Op.arith_shift_right, 1, Op.bitwise_and)
-    cp(A("cPf", 0, 6), A("cP", 0, 6))
-    r16 = A("cPf", 3, 4)
-    act(A("cPf", 6, 7), A("cPf", 5, 6), Fn.Identity, A("cPf", 4, 5), float(C + 16))
-    ts(A("oX"), A("cD", 30, 32), A("cPf", 6, 7), Op.add, float(2 * C), Op.min)
-    act(A("cPf", 7, 8), A("cPf", 5, 6), Fn.Identity, A("cPf", 4, 5), float(H + 16))
-    ts(A("oY", 0, 1), A("cPf", 7, 8), float(C), Op.min)
+    ts(A("cP", 1, 2), A("cP", 0, 1), 15, Op.bitwise_and)
+    ts(A("cP", 2, 3), A("cP", 0, 1), 1, Op.bitwise_and)
+    cp(A("cPf", 0, 3), A("cP", 0, 3))
+    r16, odd = A("cPf", 1, 2), A("cPf", 2, 3)
     quant(A("lc0", 256, 384), A("ls0", 256, 384), A("ft"))
     quant(A("lc1", 256, 384), A("ls1", 256, 384), A("ft"))
-    ts(A("c16"), A("cJ"), 0.5, Op.is_gt)
+    ts(A("cR"), A("cJ"), 0.5, Op.is_lt, 2 * FAR, Op.mult)
     ts(A("mask"), A("cJ"), r16, Op.is_equal)
-    act(A("mask2", 0, H), A("mask", 0, H), Fn.Copy)
-    act(A("mask2", H, C), A("mask", 0, H), Fn.Identity, 0.0, KEYS)
-    act(A("cL"), A("c16", 0, H), Fn.Identity, -KEYS, 2.0 * KEYS)
-    ts(A("cj1"), A("cK", 0, 20), r16, Op.add, 1.0, Op.add)
-    act(A("ckk", 0, 4), A("cj1", 0, 4), Fn.Identity, -0.5, 1.0)
-    act(A("ckk", 4, 8), A("cj1", 0, 4), Fn.Identity, -1.0 - H, 1.0)
-    ts(A("cb", 0, 32), A("cK"), r16, Op.add, 1.0, Op.subtract)
+    act(A("cM"), A("mask"), Fn.Identity, FAR, -2 * FAR)
+    act(A("cC", 0, C, 2), A("mask", 0, H), Fn.Identity, 4.0, -3.0)
+    act(A("cC", 1, C, 2), A("mask", 0, H), Fn.Identity, 4.0, -4.0)
+    if HS_ON == "V":
+        ts(A("c16"), A("cJ"), 0.5, Op.is_gt)
+    ts(A("cj"), A("cK", 0, 20), r16, Op.add)
+    act(A("cm2"), A("cj", 0, NB), Fn.Identity, 0.0, 2.0)
+    act(A("cPf", 3, 4), odd, Fn.Identity, -1.0, 0.5)
+    act(A("cb"), A("cj"), Fn.Identity, A("cPf", 3, 4), 0.5)
+    act(A("cPf", 4, 5), odd, Fn.Identity, C - 1.0, 1.0)
+    act(A("cPf", 5, 6), odd, Fn.Identity, AT + 1.0, -1.0)
+    act(A("ck", 0, 4), A("cj", 0, 4), Fn.Identity, -0.5, 1.0)
+    act(A("ck", 4, 8), A("cj", 0, 4), Fn.Identity, A("cPf", 5, 6), 1.0)
+    act(A("ck", 8, 12), A("cj", 0, 4), Fn.Identity, float(H), 1.0)
     ts(A("et", 3, 515, 4), A("cI", 0, 128), A("cPf", 0, 1), Op.is_equal)
     quant(A("qu0"), A("su0"), A("ut"))
-    ts(A("cb", 32, 64), A("cb", 0, 32), 1, Op.arith_shift_right)
     cp(word(A("qu")), ind(word(A("qu0")), A("oU")))
-    cp(A("su"), ind(A("su0"), A("oU")))
-    ts(A("oD"), A("cD", 0, 30), r16, Op.add)
-    act(A("cTK"), A("cI"), Fn.Identity, 0.0, 512.0)
-    act(A("cIT", 0, C), A("cI", 0, C), Fn.Identity, 512.0, 1.0)
-    act(A("cIT", C, C + 2), A("cI", 0, 2), Fn.Identity, 0.0, 0.0)
+    cp(A("su"), ind(A("su0"), A("oU")), "S")
+    act(A("cTK"), A("cI"), Fn.Identity, 0.0, 512.0 * UNIT)
+    act(A("cPn"), A("cI", 2, C + 2, 2), Fn.Identity, 0.0, UNIT)
     act(A("cRev"), A("cI", 0, H + 2), Fn.Identity, float(H), -1.0)
-    act(A("c2"), A("cI", 0, H), Fn.Identity, -float(H), 2.0)
-    act(A("LAB", H, H + NX), A("cI", 1, NX + 1), Fn.Copy)
-    act(A("cjw"), A("cj1"), Fn.Identity, H - 1.0, 1.0)
+    act(A("cTY", 0, K), A("cI", 0, K), Fn.Identity, -1.0, -1.0)
+    fill(A("cTY", K, C + 16), 1.0)
     E = lambda n, b: A(n, 128 * b, 128 * b + 128)
     for b in range(4):
         quant(E("qe", b), E("se", b), A("et", 3 - b, 515 - b))
     quant(A("qv"), A("sv"), A("vt"))
 
-    oN, oQ, oG, oE, oB, oL = A("oA", 0, 10), A("oA", 10, 20), A("oA", 20, 30), A("oA", 30, 34), A("oA", 34, 38), A("oA", 38, 48)
-    mask = lambda n: A("mask", 0, n)
+    oN, oQ, oG, oP, oB, oL, oL2, oE = [A("oA", NB * i, NB * i + (NB if i < 7 else 4)) for i in range(8)]
     banksH = ["pH0", "pH1", "pH2", "pS"]
     M = lambda a, b: A("MN", 16 + a, 16 + b)
-    top = lambda c: A("DT", c, c + 1)
-    per = lambda c: A("DP", 16 * c + 15, 16 * c + 16)
-    cut = lambda c: ROW * c + H - 16 * c
+    end = lambda name, c, n=1: A(name, 16 * c + 15, 16 * (c + n), 16)
     sc = lambda i: A("SC", i, i + 1)
-    KP = A("KZ", 1, C, 2)
+    sm = lambda i: A("SM", NB * i, NB * i + NB)
+    lane = lambda name, b, n: A(name, b, 4 * n, 4)
+    CK = A("CK", 1, H + 1)
 
     for t in range(R):
         qx, sxp, lc, ls, nv = "qx%d" % t, "sx%d" % t, "lc%d" % t, "ls%d" % t, NV[t]
         quant(A(qx, 0, C), A(sxp, 0, C), A("xt%d" % t))
-        mm(A("pS", 0, C), A("qu"), A("su"), A(qx, 0, C), A(sxp, 0, C))
+        for bank in ("pH0", "pS"):
+            mm(A(bank, 0, C), A("qu"), A("su"), A(qx, 0, C), A(sxp, 0, C))
         for b in range(4):
             mm(A("pT%d" % b, 0, C), E("qe", b), E("se", b), A(qx, 0, C), A(sxp, 0, C))
         for b in range(4):
             act(A("TH", C * b, C * b + C), A("pT%d" % b, 0, C), Fn.Copy, 0.0, 0.5)
+            cp(A("FA", WF * b + AT + C, WF * b + WF), A("pT%d" % b, 0, K), "S")
         for b in range(2):
-            act(A("TF", C * b, C * b + C), A("pT%d" % (2 + b), 0, C), Fn.Copy)
-        mm(A("pH0", 0, H), A("qu"), A("su"), A(qx, H, C), A(sxp, H, C))
-        cp(A("SW", 0, H), A("pS", 0, H))
-        act(A("SW", H, C), A("pH0", 0, H), Fn.Copy)
-        tt(M(0, H), A("pS", 0, C, 2), A("SW", 1, C, 2), Op.max)
+            cp(A("TF", C * b, C * b + C), A("pT%d" % (2 + b), 0, C), "S")
+        cp(A("SW", 0, C, 2), A("pH0", 0, C, 2), "S")
+        cp(A("SW", 1, C, 2), A("pH0", 1, C, 2), "S")
         tt(M(H, C), A("pS", 1, C, 2), A("SW", 2, C + 1, 2), Op.min)
-        cp(A("DT", 16, 32), dealt("TQ", "MN", H, H))
-        cp(A("DT", 0, 16), dealt("TR", "MN", H))
-        tt(A("UP", 1, C), A("pS", 1, C), A("SW", 0, C - 1), Op.is_gt)
-        tt(A("DL", 17, C + 15, 2), A("pS", 2, C, 2), M(0, H - 1), Op.is_gt)
-        tt(A("DL", 18, C + 16, 2), A("pS", 1, C - 1, 2), M(1, H), Op.is_lt)
-        tt(A("SS"), dealt("TB", "DL", C), A("cb", 32, 64), Op.add)
-        tt(A("POS"), A("cI", 2, C + 2, 2), A("UP", 2, C + 1, 2), Op.subtract)
-        tt(A("PK"), A("UP", 0, C), A("UP", 1, C + 1), Op.is_gt)
-        tt(A("PKM"), A("PK", 0, C, 2), A("PK", 1, C, 2), Op.add)
-        act(A("NPB"), A("PKM"), Fn.Identity, -BIG, BIG)
-        tt(A("M1"), M(0, H), A("NPB"), Op.add)
-        act(A("J3"), A("PKM"), Fn.Identity, 0.0, 1.0, sc(0))
-        act(sc(7), sc(0), Fn.Relu, float(K), -1.0)
-        act(sc(8), sc(0), Fn.Identity, K + 0.5, -1.0)
-        act(A("NP"), A("PK", 0, NX), Fn.Identity, 1.0, -1.0)
-        cumsum(A("CNP"), A("NP"))
-        act(A("J4", 0, NX), A("CNP"), Fn.Sign, sc(8), -1.0, sc(9))
-        act(sc(1), sc(9), Fn.Identity, NX / 2.0, 0.5)
-        act(sc(12), sc(0), Fn.Sign, 0.5 - K, 1.0)
-        act(sc(10), sc(12), Fn.Identity, -0.5, -0.5)
-        act(sc(11), sc(10), Fn.Identity, 0.0, -(K + 0.5))
-        ts(A("GM", 0, 20), A("cj1"), sc(1), Op.is_le)
-        tt(A("GM", 20, 40), A("GM", 0, 20), A("cjw"), Op.mult)
-        tt(A("HT", 0, 20), A("SS", 0, 20), A("GM", 20, 40), Op.max)
-        cp(A("oS"), A("HT", 0, 20))
+        tt(M(0, H), A("pS", 1, C, 2), A("SW", 0, C, 2), Op.max)
+        deal(A("DT", H, C), A("X1", H, C), M(H, C))
+        deal(A("DT", 0, H), A("X1", 0, H), M(0, H))
+        tt(A("UP", 1, C, 2), A("pS", 1, C, 2), A("SW", 0, C, 2), Op.is_gt)
+        tt(A("UP", 2, C + 1, 2), A("pS", 1, C, 2), A("SW", 2, C + 1, 2), Op.is_lt)
+        act(A("US"), A("UP", 2, C + 1, 2), Fn.Identity, 0.0, -UNIT)
+        scan(A("POS"), A("cPn"), A("US"), 0.0, Op.max, Op.add)
+        deal(A("D5"), A("X5"), A("UP", 1, C, 2))
+        tt(sm(0), end("D5", 0, NB), A("cm2"), Op.add)
+        cp(oP, sm(0))
+        tt(A("DL", 1, C - 1, 2), A("pS", 2, C, 2), M(0, H - 1), Op.is_gt)
+        tt(A("DL", 2, C, 2), A("pS", 1, C - 1, 2), M(1, H), Op.is_lt)
+        deal(A("D4"), A("X4"), A("DL"))
+        tt(A("HT"), end("D4", 0, 20), A("cb"), Op.add)
+        tt(A("PN", 0, K), A("UP", 0, K), A("UP", 1, K + 1), Op.is_le)
+        cumsum(A("PN", K + 1, 2 * K + 1), A("PN", 0, K))
+        deal(A("D7"), A("X7"), A("PN", 0, 2 * K))
+        act(A("PF", 0, 4), end("D7", 0, 4), Fn.Identity, 0.0, A("cPf", 4, 5))
+        tt(A("PF", 4, 8), A("PF", 0, 4), A("ck", 4, 8), Op.add)
         for c in range(NB):
-            act(A("JK", H * c, H * c + H), M(H, C), Fn.Sign, top(16 + c), -1.0, A("ACC", c, c + 1))
+            act(A("JK", H * c, H * c + H), M(H, C), Fn.Sign, end("DT", NB + c), -1.0, A("ACC", c, c + 1))
         ts(oN, A("ACC", 0, NB), -1.0, Op.mult, float(H), Op.add)
         tt(A("KEY", 1, H + 1), ind(A("cTK"), oN), A("POS"), Op.add)
-        act(A("KEYN", 1, H + 1), A("KEY", 1, H + 1), Fn.Identity, -1.0, 1.0 / KEYS)
+        act(A("KEYN", 1, H + 1), A("KEY", 1, H + 1), Fn.Identity, -1.0, 1.0)
         for c in range(NB):
-            act(A("KB", cut(c), ROW * c + ROW), M(-1, 16 * c + 15), Fn.Sign, top(c), -1.0)
-            act(A("KB", ROW * c, cut(c)), M(16 * c + 1, H + 1), Fn.Sign, top(c), -1.0)
-            scan(A("OS", cut(c), ROW * c + ROW), A("KB", cut(c), ROW * c + ROW), A("KEY", 0, 16 * c + 16), 0.0, Op.mult, Op.max)
-            scan(rev("OS", ROW * c, cut(c)), rev("KB", ROW * c, cut(c)), rev("KEYN", 16 * c + 1, H + 1), -1.0, Op.min, Op.max)
-        tt(A("DG"), ind(A("OS"), A("oD", 0, 20)), A("mask2"), Op.mult)
-        scan(A("DS", 0, H), A("cL"), A("DG", 0, H), 0.0, Op.min, Op.add)
-        own16(A("DS", H, C), A("DG", H, C), H)
-        tt(A("I1", 0, NB), A("DS", 15, H, 16), A("DS", H + 15, C, 16), Op.min)
+            act(A("KB", ROW * c, ROW * c + H + 2), M(-1, H + 1), Fn.Sign, end("DT", c), -1.0)
+        for c in range(NB):
+            d = NB - 1 - c
+            scan(A("LR", 1, 32 * d + 32, 2), A("KB", ROW * d, ROW * d + 16 * d + 16), A("KEY", 0, 16 * d + 16), 0.0, Op.mult, Op.max)
+            scan(rev("LR", 32 * c, C, 2), rev("KB", ROW * c + 16 * c + 2, ROW * c + H + 2), rev("KEYN", 16 * c + 1, H + 1), -1.0, Op.min, Op.max)
+        for d in reversed(range(NB)):
+            scan(A("LL", 0, 16 * d + 16), A("KB", ROW * d, ROW * d + 16 * d + 16), A("cRev", 0, 16 * d + 16), 0.0, Op.mult, Op.max)
+        scan(A("X2"), A("LR"), A("cC"), 4.0, Op.min, Op.add)
+        carry(A("DS"), A("X2", 1, C, 2))
+        ts(A("I1", 0, NB), end("DS", 0, NB), 1.0 / UNIT, Op.mult)
         ts(A("I1", NB, 2 * NB), A("I1", 0, NB), 511, Op.bitwise_and)
-        cp(oQ, A("I1", NB, 2 * NB))
-        tt(A("NG"), ind(A("SW"), oQ), A("M1"), Op.subtract)
-        tt(A("PM"), A("NG"), mask(H), Op.mult)
-        own16(A("DP"), A("PM"), H)
-        for c in range(nv, NB):
-            act(A("JK", H * c, H * c + H), A("NG"), Fn.Sign, per(c), -1.0)
-            act(A("JK2", H * c, H * c + H), A("JK", H * c, H * c + H), Fn.Relu, 0.0, 1.0, A("ACC", 10 + c, 11 + c))
-        for c in range(nv):
-            ts(A("JK", H * c, H * c + H), A("NG"), per(c), Op.is_lt)
-            cumsum(A("CS", H * c, H * c + H), A("JK", H * c, H * c + H))
-        cp(A("oA", 20, 20 + nv), A("CS", H - 1, nv * H, H))
-        cp(A("oA", 20 + nv, 30), A("ACC", 10 + nv, 20))
-        act(A("Y"), ind(A("cTY"), oG), Fn.Copy)
-        act(A("G1"), ind(A("cI"), oG), Fn.Copy)
-        red(sc(2), A("Y"), Op.max)
-        ts(A("EQ", 0, C, 2), A("Y"), sc(2), Op.is_equal)
-        ts(A("EQ", 1, C, 2), A("G1"), sc(2), Op.subtract, -1024.0, Op.mult)
-        ts(A("F1", 0, C, 2), A("G1"), sc(2), Op.subtract, 1024.0, Op.mult)
-        ts(sc(3), sc(2), sc(10), Op.mult, sc(11), Op.add)
-        scan(A("W"), A("EQ"), A("F1"), 0.0, Op.add, Op.add)
-        ts(KP, A("W", 0, C, 2), sc(3), Op.is_lt)
-        act(A("XL", 0, C, 2), A("PK", 1, C, 2), Fn.Identity, 0.0, -0.5)
-        cumsum(A("XL", 1, C, 2), KP, sc(7))
-        scan(A("ZZ"), A("KZ"), A("XL", 0, C), 0.0, Op.mult, Op.add)
-        for c in range(4):
-            act(A("JK2", H * c, H * c + H), A("ZZ", 1, C, 2), Fn.Sign, A("ckk", c, c + 1), -1.0, A("ACC", 20 + c, 21 + c))
-        tt(A("EF", 0, 4), A("ACC", 20, 24), A("ckk", 4, 8), Op.max)
-        for c in range(4):
-            ts(A("oA", 30 + c, 31 + c), A("ACC", 20 + c, 21 + c), A("ckk", 4 + c, 5 + c), Op.max, float(H), Op.add)
-        act(A("EF", 4, 8), A("EF", 0, 4), Fn.Identity, float(H), 1.0)
-        act(A("PQ", 0, C, 2), ind(A("cIT"), oQ), Fn.Copy)
-        act(A("PQ", 1, C, 2), ind(A("cIT"), oQ), Fn.Copy)
-        tt(A("PQ", 0, NX), A("PQ", 0, NX), A("PK", 0, NX), Op.mult)
-        tt(A("QM"), ind(A("PQ"), oE), mask(K), Op.mult)
-        own16(A("QS"), A("QM"), K)
-        tt(A("I1", 20, 24), A("QS", 15, K, 16), A("EF", 4, 8), Op.max)
-        ts(A("I1", 24, 28), A("I1", 20, 24), 511, Op.bitwise_and)
-        cp(oB, A("I1", 24, 28))
+        q = A("I1", NB, 2 * NB)
+        cp(oQ, q)
+        tt(sm(1), q, sm(0), Op.subtract)
+        act(sm(10), sm(1), Fn.Square)
+        act(sm(2), sm(10), Fn.Relu, 96.0, -96.0)
+        act(sm(3), end("DS", 0, NB), Fn.Identity, (C - 1) * 512.0, -1.0 / UNIT)
+        tt(sm(4), sm(3), sm(0), Op.max)
+        tt(sm(5), sm(4), q, Op.min)
+        cp(oB, sm(5))
         for b in range(4):
-            act(A("TMP", K * b, K * b + K), ind(A("TH", C * b, C * b + C), oE), Fn.Copy)
-            tt(lane("ft", b, K), ind(A("TH", C * b, C * b + C), oB), A("TMP", K * b, K * b + K), Op.add)
+            cp(A("TMP", C * b, C * b + C, 2), ind(A("TH", C * b, C * b + C), oP), "S")
+            if b < NFA:
+                tt(A("FA", WF * b + AT + 1, WF * b + AT + C, 2), ind(A("TH", C * b, C * b + C), oB), A("TMP", C * b, C * b + C, 2), Op.add)
+            else:
+                cp(A("TMP", C * b + 1, C * b + C, 2), ind(A("TH", C * b, C * b + C), oB), "S")
+                scan(A("FA", WF * b + AT, WF * b + AT + C), A("c01"), A("TMP", C * b, C * b + C), 0.0, Op.mult, Op.add)
+        tt(A("NG"), ind(A("SW"), oQ), M(0, H), Op.subtract)
+        deal(A("DP"), A("X3"), A("NG"))
+        for c in range(nv, NB):
+            act(A("JK", H * c, H * c + H), A("NG"), Fn.Sign, end("DP", c), -1.0)
+            act(A("JK2", H * c, H * c + H), A("JK", H * c, H * c + H), Fn.Relu, A("SM", 2 * NB + c, 2 * NB + c + 1), 1.0, A("ACC", 10 + c, 11 + c))
+        for c in range(nv):
+            ts(A("JK", H * c, H * c + H), A("NG"), end("DP", c), Op.is_lt)
+            cumsum(A("CS", H * c, H * c + H), A("JK", H * c, H * c + H), A("SM", 2 * NB + c, 2 * NB + c + 1))
+        if nv:
+            cp(A("oA", 20, 20 + nv), A("CS", H - 1, nv * H, H))
+        if nv < NB:
+            ts(A("oA", 20 + nv, 30), A("ACC", 10 + nv, 20), float(C), Op.min)
+        cp(A("Y"), ind(A("cTY"), oG), Y_ON)
+        scan(A("MU"), A("Y"), A("Y"), 0.0, Op.min, Op.min)
+        mu = A("MU", H - 1, H)
+        act(A("OUT"), A("Y"), Fn.Relu, 0.0, 1.0, sc(0))
+        act(A("LE"), A("OUT"), Fn.Identity, 1.0, -1.0)
+        ts(A("LT"), A("Y"), mu, Op.is_gt)
+        scan(A("UU"), A("LT"), A("OUT"), mu, Op.add, Op.subtract)
+        scan(CK, A("LE"), A("UU"), -K - 1.0, Op.add, Op.min)
+        act(sc(1), sc(0), Fn.Relu, float(K - H), 1.0)
+        act(sc(3), sc(1), Fn.Identity, -float(K), -1.0)
+        act(A("PF", 8, 12), A("ck", 0, 4), Fn.Identity, sc(3), 1.0)
+        act(A("PF", 12, 16), end("D7", 4, 4), Fn.Sign, sc(1), -1.0)
+        tt(A("PF", 16, 20), A("PF", 12, 16), A("PF", 4, 8), Op.mult)
+        tt(A("PF", 20, 24), A("PF", 12, 16), A("ck", 8, 12), Op.mult)
+        tt(A("HT", 0, 4), A("HT", 0, 4), A("PF", 20, 24), Op.max)
+        cp(A("oS"), A("HT"))
+        act(sc(2), sc(1), Fn.Identity, float(K), 1.0)
+        act(A("LAB", H, H + K), A("cI", 0, K), Fn.Identity, sc(3), 1.0)
+        for c in range(4):
+            bias = A("PF", 8 + c, 9 + c)
+            if c < NE:
+                ts(A("JK", H * c, H * c + H), CK, bias, Op.is_lt, 2.0, Op.mult)
+                cumsum(A("CS", H * c, H * c + H), A("JK", H * c, H * c + H))
+                got = A("CS", H * c + H - 1, H * c + H)
+            else:
+                got = A("ACC", 20 + c, 21 + c)
+                act(A("JK2", H * c, H * c + H), CK, Fn.Sign, bias, -1.0, got)
+            ts(A("oA", 70 + c, 71 + c), got, float(AT + 1 if c < NE else H + AT + 1), Op.add, A("PF", 16 + c, 17 + c), Op.max)
+        for b in range(4):
+            cp(lane("ft", b, K), ind(A("FA", WF * b, WF * b + WF), oE), "V" if b < NF else "S")
         quant(A(qx, C, C + 128), A(sxp, C, C + 128), A("ft"))
         other = T.cores[rank ^ STEP[t]]
         direct = topo.may_write(core, other)
@@ -457,36 +472,39 @@ def rank_program(g, core, T, topo):
         came = len(topo.engines(other, core)) if direct else sum(len(topo.engines(c, core)) for c in _relays(T, topo, other, core))
         sent = issue("G", lambda moves=moves, t=t: g.remote_dma_fused(moves, local_sem=T.sem["sent%d" % t]), [A(qx), A(sxp)], [], 0.3, None,
                      lat=HOP if direct else 2 * HOP, more={"sent%d" % t: 2 * half, "arr%d" % t: came})
-        for c in range(NB):
-            scan(A("KB", ROW * (NB - 1 - c), cut(NB - 1 - c)), A("KB", cut(c), ROW * c + ROW), A("cRev", 0, 16 * c + 16), 0.0, Op.mult, Op.max)
-        tt(A("LM"), ind(A("KB"), A("oD", 20, 30)), mask(H), Op.mult)
-        own16(A("LS"), A("LM"), H)
-        tt(A("KR", NB, 2 * NB), A("DS", 15, H, 16), A("DS", H + 15, C, 16), Op.is_gt)
-        act(A("KR", 2 * NB, 3 * NB), A("KR", NB, 2 * NB), Fn.Identity, 0.0, float(H))
-        tt(A("KR", 3 * NB, 4 * NB), A("LS", 15, H, 16), A("KR", 2 * NB, 3 * NB), Op.max)
-        cp(oL, A("KR", 3 * NB, 4 * NB))
-        act(sc(5), sc(2), Fn.Identity, K - 0.5, -1.0)
-        act(A("J5"), A("W", 1, C, 2), Fn.Sign, sc(5), -1.0, sc(6))
-        ts(A("RR"), A("c2"), sc(6), Op.is_equal, -2.0 * BIG, Op.mult)
-        scan(A("RM", 1, H + 1), A("RR"), A("M1"), BIG, Op.add, Op.max)
-        tt(A("GT"), A("M1"), A("RM", 0, H), Op.is_gt)
-        act(A("NK"), KP, Fn.Identity, 1.0, -1.0)
-        tt(A("NM", 0, H), A("NK"), A("GT"), Op.is_gt)
-        scan(A("FS"), A("NM", 0, H), A("KEY", 1, H + 1), 4.0 * KEYS, Op.mult, Op.max)
-        scan(rev("BS", 0, H), rev("NM", 1, H + 1), rev("KEY", 1, H + 1), 0.0, Op.mult, Op.max)
-        tt(A("CUT", 1, H + 1), A("FS"), A("BS"), Op.is_equal)
-        cumsum(rev("SG", 0, H), A("CUT", 0, H))
-        act(A("NC"), A("CUT", 0, H), Fn.Identity, 1.0, -1.0)
-        ts(A("XL", 1, C, 2), A("XL", 1, C, 2), sc(1), Op.max)
-        tt(A("XL", 2, C + 2, 2), ind(A("SG"), oL), A("GT"), Op.mult)
-        scan(A("LW"), A("KZ"), A("XL", 1, C + 1), 0.0, Op.mult, Op.max)
-        ts(A("NL"), A("LW", 1, C, 2), 0.0, Op.is_equal)
-        scan(rev("NBK", 0, H), rev("NL", 0, H), rev("LW", 1, C, 2), 0.0, Op.mult, Op.add)
-        tt(A("CN"), A("NBK"), A("CUT", 0, H), Op.mult)
-        scan(A("LAB", 0, H), A("NC"), A("CN"), 0.0, Op.mult, Op.add)
-        tt(A("HM"), ind(A("LAB"), A("oS")), mask(C), Op.mult)
-        own16(A("HS"), A("HM"), C)
-        ts(A("oH"), A("HS", 15, C, 16), 1.0, Op.subtract)
+        deal(A("D6"), A("X6"), A("LL"))
+        ts(oL, end("D6", 0, NB), -1.0, Op.mult, float(H), Op.add)
+        act(sm(6), end("D6", 0, NB), Fn.Identity, float(H), -1.0)
+        act(sm(7), sm(1), Fn.Sign, 0.5, 1.0)
+        tt(sm(8), sm(7), A("cj", 0, NB), Op.mult)
+        tt(sm(9), sm(8), sm(6), Op.max)
+        cp(oL2, sm(9))
+        scan(A("CK2"), A("LE"), A("UU"), -K - 1.0, Op.add, Op.min)
+        tt(A("NM"), ind(A("CK"), oL), A("CK2"), Op.is_ge)
+        tt(A("NA"), ind(A("CK"), oL2), A("CK2"), Op.is_ge)
+        scan(A("FS", 1, H + 1), A("NM"), A("KEY", 1, H + 1), 4.0, Op.mult, Op.max)
+        scan(rev("BS", 0, H), rev("KEY", 1, H + 1), rev("NM", 0, H), 0.0, Op.max, Op.mult)
+        tt(A("SD"), A("FS", 0, H), A("BS"), Op.is_gt)
+        act(A("NS"), A("SD"), Fn.Identity, 1.0, -1.0)
+        act(A("AN", 1, H + 1), A("NA"), Fn.Identity, 1.0, -1.0)
+        scan(A("KP"), CK, A("CK", 0, H), 0.0, Op.min, Op.subtract)
+        act(A("W0"), A("NA"), Fn.Identity, -384.0, 128.0)
+        act(A("W1"), A("KP"), Fn.Identity, 256.0, 128.0)
+        scan(A("LP"), A("W0"), A("W1"), 0.0, Op.min, Op.add)
+        scan(A("GO"), A("SD"), A("NA"), 0.0, Op.max, Op.min)
+        scan(A("HO"), A("AN", 0, H), A("NS"), 0.0, Op.max, Op.min)
+        scan(rev("LB", 1, H + 1), rev("CK", 1, H + 1), rev("GO", 0, H), 0.0, Op.min, Op.add)
+        tt(A("XP"), ind(A("LB"), oL2), A("LP"), Op.max)
+        scan(rev("Z", 0, H), rev("GO", 0, H), rev("XP", 0, H), 0.0, Op.mult, Op.min)
+        scan(A("O"), A("HO"), A("Z"), 0.0, Op.mult, Op.min)
+        scan(A("LAB", 0, H), A("LB", 1, H + 1), A("O"), -200.0, Op.max, Op.min)
+        if HS_ON == "V":
+            tt(A("HM"), ind(A("LAB"), A("oS")), A("mask"), Op.mult)
+            scan(A("HS"), A("c16"), A("HM"), 0.0, Op.mult, Op.add)
+        else:
+            cp(A("HM"), ind(A("LAB"), A("oS")), "S")
+            deal(A("HS"), A("X8"), A("HM"))
+        ts(A("oH"), end("HS", 0, 20), sc(2), Op.add)
         xn = "xt%d" % (t + 1)
         for b in (2, 3, 0, 1):
             mm(A(banksH[b], 0, 128), E("qw", b), E("sw", b), A(lc, 192, 320), A(ls, 192, 320), deps=[sent], arrive=("arr%d" % t, came))
@@ -497,7 +515,8 @@ def rank_program(g, core, T, topo):
         for b in range(2, 4):
             tt(lane(xn, b, C), ind(A("HR", K * b, K * b + K), A("oH")), A("TF", C * (b - 2), C * (b - 1)), Op.add)
 
-    act(A("ER"), ind(A("cI"), oE), Fn.Copy)
+    scan(A("EC", AT + 1, AT + C, 2), A("cI", 0, C, 2), A("UP", 1, C, 2), 0.0, Op.max, Op.add)
+    act(A("ER"), ind(A("EC"), oE), Fn.Copy)
     act(A("OLR"), ind(A("ER"), A("oH")), Fn.Copy)
     dma("G", hbm(T.ol[:]), (T.OLR[0:128:16, :], A("OLR")[1]), 0.0)
     quant(A("qx2"), A("sx2"), A("xt2"))

@@ -8,13 +8,15 @@ NB = H // 16
 ROW = H + 16
 BIG = 2.0 ** 96
 FAR = 2.0 ** 98
+DROP = 192.0
 UNIT = 2.0 ** -18
 AT, WF = 48, 432
 NV = [6, 6]
-NE = 0
+NR = 1
+NE = 2
 NF = 2
 NFA = 2
-HS_ON = "V"
+HS_ON = "S"
 Y_ON = "S"
 SOFT = False
 HOP, WAKE, LOAD, SLACK, TRIES = 3.0, 0.17, 2.0, 0.02, 1500
@@ -26,8 +28,9 @@ _SB = {
     "qw": (512, CODE), "sw": (512, PLANE), "qe": (512, CODE), "se": (512, PLANE),
     "qx0": (C + 128, CODE), "sx0": (C + 128, PLANE), "qx1": (C + 128, CODE), "sx1": (C + 128, PLANE), "qx2": (C, CODE), "sx2": (C, PLANE),
     "lc0": (384, CODE), "ls0": (384, PLANE), "lc1": (384, CODE), "ls1": (384, PLANE), "rc": (64, CODE), "rs": (256, PLANE),
-    "cI": (C + 16, F32), "cJ": (C, BF), "cP": (8, I32), "cPf": (8, F32), "cK": (32, F32), "cTK": (C + 16, F32),
-    "cRev": (H + 2, BF), "cTY": (C + 16, BF), "mask": (C, BF), "cM": (C, BF), "cR": (C, BF), "cC": (C, BF), "c16": (C, BF), "c01": (C, BF),
+    "cI": (C + 16, F32), "cJ": (C + 16, BF), "cP": (8, I32), "cPf": (16, F32), "cK": (32, F32), "cTK": (C + 16, F32),
+    "cRev": (H + 2, BF), "cTY": (C + 16, BF), "mask": (C + 16, BF), "cM": (H, BF), "cR": (H, BF), "cRn": (H, BF), "cC": (H, BF),
+    "cN": (C, BF), "cH": (C, BF), "cHn": (C, BF), "c01": (C, BF),
     "cPn": (H, F32), "cj": (20, F32), "cm2": (NB, F32), "cb": (20, F32), "ck": (16, F32),
     "oU": (8, U16), "oA": (80, U16), "oH": (20, U16), "oS": (20, U16),
     "SW": (C + 8, F32), "KB": (NB * ROW, BF), "JK": (NB * H, BF), "JK2": (NB * H, BF), "CS": (NB * H, BF),
@@ -36,11 +39,11 @@ _SB = {
     "ER": (K, F32), "OLR": (C, F32), "YO": (C, F32),
 }
 _ROWS = {
-    "rf": (F32, {"MN": C + 32, "X1": C, "DT": C, "US": H, "POS": H, "KEY": H + 2, "KEYN": H + 2, "LR": C, "X2": C, "DS": H, "NG": H, "X3": H,
+    "rf": (F32, {"MN": C + 32, "X1": H, "XN": C + 2, "DT": C, "US": H, "POS": H, "KEY": H + 2, "KEYN": H + 2, "LR": 2 * C, "DS": C, "NG": H, "X3": H,
                  "DP": H, "SM": 120, "FS": H + 2, "BS": H, "HT": 20, "PF": 24}),
-    "rb": (BF, {"UP": C + 2, "DL": C, "X4": C, "D4": C, "X5": H, "D5": H, "LL": H, "X6": H, "D6": H, "PN": 2 * K + 2, "X7": 2 * K, "D7": 2 * K,
+    "rb": (BF, {"UP": C + 2, "DL": C, "D4": C, "D5": H, "LL": C, "D6": H, "PN": 2 * K + 2, "D7": 2 * K,
                 "Y": H, "MU": H, "OUT": H, "LE": H, "LT": H, "UU": H, "CK": H + 2, "CK2": H, "NM": H, "NA": H, "AN": H + 2, "KP": H, "LP": H, "W0": H,
-                "W1": H, "SD": H, "NS": H, "GO": H, "HO": H, "LB": H + 2, "XP": H, "Z": H, "O": H, "HM": C, "X8": C, "HS": C}),
+                "W1": H, "SD": H, "NS": H, "GO": H, "HO": H, "LB": H + 2, "XP": H, "Z": H, "O": H, "HM": C, "HS": C}),
 }
 _AT = {}
 for _b, (_d, _rows) in _ROWS.items():
@@ -250,6 +253,9 @@ def rank_program(g, core, T, topo):
         scan(tmp, row, A("cM", 0, row[2]), FAR, Op.min, Op.max)
         carry(out, tmp)
 
+    def hold(out, row):
+        scan(out, A("cH", 0, row[2]), row, 0.0, Op.add, Op.min)
+
     def fill(out, v):
         issue("V", lambda: g.vector.memset(out[0], v), [], [out], time(out, narrow(out)))
 
@@ -290,7 +296,7 @@ def rank_program(g, core, T, topo):
     dma("Y", A("vt"), hbm(T.v[:]), 0.7, [first])
     iota(A("cK"), [[16, 32]], 0, 0)
     iota(A("cP", 0, 1), [[0, 1]], 0, 1)
-    iota(A("cJ"), [[0, 20], [1, 16]], 0, 0)
+    iota(A("cJ"), [[0, 21], [1, 16]], 0, 0)
     iota(A("cI"), [[1, C + 16]], 0, 0)
     for b in range(4):
         iota(A("FA", WF * b, WF * b + WF), [[0, WF]], 0, 0)
@@ -307,19 +313,35 @@ def rank_program(g, core, T, topo):
     r16, odd = A("cPf", 1, 2), A("cPf", 2, 3)
     quant(A("lc0", 256, 384), A("ls0", 256, 384), A("ft"))
     quant(A("lc1", 256, 384), A("ls1", 256, 384), A("ft"))
-    ts(A("cR"), A("cJ"), 0.5, Op.is_lt, 2 * FAR, Op.mult)
+    ts(A("cR"), A("cJ", 0, H), 0.5, Op.is_lt, 2 * FAR, Op.mult)
+    act(A("cRn"), A("cR"), Fn.Identity, 0.0, -1.0)
     ts(A("mask"), A("cJ"), r16, Op.is_equal)
-    act(A("cM"), A("mask"), Fn.Identity, FAR, -2 * FAR)
-    act(A("cC", 0, C, 2), A("mask", 0, H), Fn.Identity, 4.0, -3.0)
-    act(A("cC", 1, C, 2), A("mask", 0, H), Fn.Identity, 4.0, -4.0)
-    if HS_ON == "V":
-        ts(A("c16"), A("cJ"), 0.5, Op.is_gt)
+    act(A("cM"), A("mask", 0, H), Fn.Identity, FAR, -2 * FAR)
+    act(A("cN", 1, C, 2), A("mask", 0, H), Fn.Identity, FAR, -2 * FAR)
+    act(A("cN", 0, C, 2), A("mask", 15, H + 15), Fn.Identity, FAR, -2 * FAR)
+    fill(A("cN", 0, 1), FAR)
+    act(A("XN", C, C + 1), A("mask", 15, 16), Fn.Identity, FAR, -FAR - BIG)
+    act(A("HM"), A("mask", 15, C + 15), Fn.Identity, 0.0, -DROP / 1024.0)
+    act(A("HS"), A("mask", 0, C), Fn.Identity, 0.0, 1024.0)
+    scan(A("cH"), A("HM"), A("HS"), 0.0, Op.mult, Op.add)
+    act(A("cHn"), A("cH"), Fn.Identity, 0.0, -1.0)
+    act(A("cC", 0, H, 2), A("cH", 0, H // 2), Fn.Identity, 0.0, 3.0 / DROP)
+    cp(A("cC", 1, H, 2), A("mask", 0, H // 2), "S")
+    col = lambda i: A("cPf", i, i + 1)
+    act(col(6), A("mask", 15, 16), Fn.Identity, DROP, -DROP)
+    act(col(7), col(6), Fn.Identity, 0.0, 3.0 / DROP)
+    act(col(8), col(6), Fn.Identity, float(H), -1.0)
+    act(col(9), col(6), Fn.Identity, float(K), -1.0)
+    act(col(10), col(6), Fn.Identity, 0.0, -1.0)
+    act(col(11), col(6), Fn.Identity, (C - 1) * 512.0, -3.0 / DROP / UNIT)
     ts(A("cj"), A("cK", 0, 20), r16, Op.add)
-    act(A("cm2"), A("cj", 0, NB), Fn.Identity, 0.0, 2.0)
-    act(A("cPf", 3, 4), odd, Fn.Identity, -1.0, 0.5)
-    act(A("cb"), A("cj"), Fn.Identity, A("cPf", 3, 4), 0.5)
-    act(A("cPf", 4, 5), odd, Fn.Identity, C - 1.0, 1.0)
-    act(A("cPf", 5, 6), odd, Fn.Identity, AT + 1.0, -1.0)
+    act(A("cm2"), A("cj", 0, NB), Fn.Identity, col(6), 2.0)
+    ts(col(3), odd, 0.5, Op.mult, col(6), Op.add)
+    ts(A("cb"), A("cj"), 2.0, Op.subtract, 0.5, Op.mult)
+    act(A("cb"), A("cb"), Fn.Identity, col(3), 1.0)
+    act(col(4), odd, Fn.Identity, C - 1.0, 1.0)
+    act(col(12), col(4), Fn.Identity, 0.0, col(6))
+    act(col(5), odd, Fn.Identity, AT + 1.0, -1.0)
     act(A("ck", 0, 4), A("cj", 0, 4), Fn.Identity, -0.5, 1.0)
     act(A("ck", 4, 8), A("cj", 0, 4), Fn.Identity, A("cPf", 5, 6), 1.0)
     act(A("ck", 8, 12), A("cj", 0, 4), Fn.Identity, float(H), 1.0)
@@ -344,12 +366,13 @@ def rank_program(g, core, T, topo):
     sc = lambda i: A("SC", i, i + 1)
     sm = lambda i: A("SM", NB * i, NB * i + NB)
     lane = lambda name, b, n: A(name, b, 4 * n, 4)
+    part = lambda c: C * (2 * c // NB)
     CK = A("CK", 1, H + 1)
 
     for t in range(R):
         qx, sxp, lc, ls, nv = "qx%d" % t, "sx%d" % t, "lc%d" % t, "ls%d" % t, NV[t]
         quant(A(qx, 0, C), A(sxp, 0, C), A("xt%d" % t))
-        for bank in ("pH0", "pS"):
+        for bank in ("pS", "pH0"):
             mm(A(bank, 0, C), A("qu"), A("su"), A(qx, 0, C), A(sxp, 0, C))
         for b in range(4):
             mm(A("pT%d" % b, 0, C), E("qe", b), E("se", b), A(qx, 0, C), A(sxp, 0, C))
@@ -362,47 +385,54 @@ def rank_program(g, core, T, topo):
         cp(A("SW", 1, C, 2), A("pH0", 1, C, 2), "S")
         tt(M(H, C), A("pS", 1, C, 2), A("SW", 2, C + 1, 2), Op.min)
         tt(M(0, H), A("pS", 1, C, 2), A("SW", 0, C, 2), Op.max)
-        deal(A("DT", H, C), A("X1", H, C), M(H, C))
-        deal(A("DT", 0, H), A("X1", 0, H), M(0, H))
+        scan(A("XN", 0, C), A("pS", 0, C), A("cN"), FAR, Op.min, Op.max)
+        carry(A("DT", H, C), A("XN", 2, C + 1, 2))
+        deal(A("DT", 0, H), A("X1"), M(0, H))
         tt(A("UP", 1, C, 2), A("pS", 1, C, 2), A("SW", 0, C, 2), Op.is_gt)
         tt(A("UP", 2, C + 1, 2), A("pS", 1, C, 2), A("SW", 2, C + 1, 2), Op.is_lt)
         act(A("US"), A("UP", 2, C + 1, 2), Fn.Identity, 0.0, -UNIT)
         scan(A("POS"), A("cPn"), A("US"), 0.0, Op.max, Op.add)
-        deal(A("D5"), A("X5"), A("UP", 1, C, 2))
+        hold(A("D5"), A("UP", 1, C, 2))
         tt(sm(0), end("D5", 0, NB), A("cm2"), Op.add)
         cp(oP, sm(0))
         tt(A("DL", 1, C - 1, 2), A("pS", 2, C, 2), M(0, H - 1), Op.is_gt)
         tt(A("DL", 2, C, 2), A("pS", 1, C - 1, 2), M(1, H), Op.is_lt)
-        deal(A("D4"), A("X4"), A("DL"))
+        hold(A("D4"), A("DL"))
         tt(A("HT"), end("D4", 0, 20), A("cb"), Op.add)
         tt(A("PN", 0, K), A("UP", 0, K), A("UP", 1, K + 1), Op.is_le)
         cumsum(A("PN", K + 1, 2 * K + 1), A("PN", 0, K))
-        deal(A("D7"), A("X7"), A("PN", 0, 2 * K))
-        act(A("PF", 0, 4), end("D7", 0, 4), Fn.Identity, 0.0, A("cPf", 4, 5))
+        hold(A("D7"), A("PN", 0, 2 * K))
+        act(A("PF", 0, 4), end("D7", 0, 4), Fn.Identity, col(12), col(4))
         tt(A("PF", 4, 8), A("PF", 0, 4), A("ck", 4, 8), Op.add)
-        for c in range(NB):
+        for c in range(NR, NB):
             act(A("JK", H * c, H * c + H), M(H, C), Fn.Sign, end("DT", NB + c), -1.0, A("ACC", c, c + 1))
-        ts(oN, A("ACC", 0, NB), -1.0, Op.mult, float(H), Op.add)
+        ts(A("oA", NR, NB), A("ACC", NR, NB), -1.0, Op.mult, float(H), Op.add)
+        for c in range(NR):
+            ts(A("JK", H * c, H * c + H), M(H, C), end("DT", NB + c), Op.is_lt)
+            ts(A("JK2", H * c, H * c + H), M(H, C), end("DT", NB + c), Op.is_le)
+            scan(A("CS", H * c, H * c + H), A("JK", H * c, H * c + H), A("JK2", H * c, H * c + H), -float(H), Op.add, Op.add)
+        if NR:
+            ts(A("oA", 0, NR), A("CS", H - 1, NR * H, H), -1.0, Op.mult, float(H), Op.add)
         tt(A("KEY", 1, H + 1), ind(A("cTK"), oN), A("POS"), Op.add)
         act(A("KEYN", 1, H + 1), A("KEY", 1, H + 1), Fn.Identity, -1.0, 1.0)
         for c in range(NB):
             act(A("KB", ROW * c, ROW * c + H + 2), M(-1, H + 1), Fn.Sign, end("DT", c), -1.0)
         for c in range(NB):
             d = NB - 1 - c
-            scan(A("LR", 1, 32 * d + 32, 2), A("KB", ROW * d, ROW * d + 16 * d + 16), A("KEY", 0, 16 * d + 16), 0.0, Op.mult, Op.max)
-            scan(rev("LR", 32 * c, C, 2), rev("KB", ROW * c + 16 * c + 2, ROW * c + H + 2), rev("KEYN", 16 * c + 1, H + 1), -1.0, Op.min, Op.max)
+            scan(A("LR", part(d) + 1, part(d) + 32 * d + 32, 2), A("KB", ROW * d, ROW * d + 16 * d + 16), A("KEY", 0, 16 * d + 16), 0.0, Op.mult, Op.max)
+            scan(rev("LR", part(c) + 32 * c, part(c) + C, 2), rev("KB", ROW * c + 16 * c + 2, ROW * c + H + 2), rev("KEYN", 16 * c + 1, H + 1), -1.0, Op.min, Op.max)
         for d in reversed(range(NB)):
-            scan(A("LL", 0, 16 * d + 16), A("KB", ROW * d, ROW * d + 16 * d + 16), A("cRev", 0, 16 * d + 16), 0.0, Op.mult, Op.max)
-        scan(A("X2"), A("LR"), A("cC"), 4.0, Op.min, Op.add)
-        carry(A("DS"), A("X2", 1, C, 2))
-        ts(A("I1", 0, NB), end("DS", 0, NB), 1.0 / UNIT, Op.mult)
+            scan(A("LL", part(d) // 2, part(d) // 2 + 16 * d + 16), A("KB", ROW * d, ROW * d + 16 * d + 16), A("cRev", 0, 16 * d + 16), 0.0, Op.mult, Op.max)
+        for i in range(2):
+            scan(A("DS", H * i, H * i + H), A("cC", 0, H), A("LR", (C + H) * i, (C + H) * i + H), 0.0, Op.add, Op.min)
+        ts(A("I1", 0, NB), A("DS", 31, C, 32), col(7), Op.add, 1.0 / UNIT, Op.mult)
         ts(A("I1", NB, 2 * NB), A("I1", 0, NB), 511, Op.bitwise_and)
         q = A("I1", NB, 2 * NB)
         cp(oQ, q)
         tt(sm(1), q, sm(0), Op.subtract)
         act(sm(10), sm(1), Fn.Square)
         act(sm(2), sm(10), Fn.Relu, 96.0, -96.0)
-        act(sm(3), end("DS", 0, NB), Fn.Identity, (C - 1) * 512.0, -1.0 / UNIT)
+        act(sm(3), A("DS", 31, C, 32), Fn.Identity, col(11), -1.0 / UNIT)
         tt(sm(4), sm(3), sm(0), Op.max)
         tt(sm(5), sm(4), q, Op.min)
         cp(oB, sm(5))
@@ -414,7 +444,8 @@ def rank_program(g, core, T, topo):
                 cp(A("TMP", C * b + 1, C * b + C, 2), ind(A("TH", C * b, C * b + C), oB), "S")
                 scan(A("FA", WF * b + AT, WF * b + AT + C), A("c01"), A("TMP", C * b, C * b + C), 0.0, Op.mult, Op.add)
         tt(A("NG"), ind(A("SW"), oQ), M(0, H), Op.subtract)
-        deal(A("DP"), A("X3"), A("NG"))
+        tt(A("X3"), ind(A("SW"), oQ), A("X1"), Op.subtract)
+        scan(A("DP"), A("cRn"), A("X3"), 0.0, Op.add, Op.max)
         for c in range(nv, NB):
             act(A("JK", H * c, H * c + H), A("NG"), Fn.Sign, end("DP", c), -1.0)
             act(A("JK2", H * c, H * c + H), A("JK", H * c, H * c + H), Fn.Relu, A("SM", 2 * NB + c, 2 * NB + c + 1), 1.0, A("ACC", 10 + c, 11 + c))
@@ -435,13 +466,14 @@ def rank_program(g, core, T, topo):
         scan(CK, A("LE"), A("UU"), -K - 1.0, Op.add, Op.min)
         act(sc(1), sc(0), Fn.Relu, float(K - H), 1.0)
         act(sc(3), sc(1), Fn.Identity, -float(K), -1.0)
+        act(sc(4), sc(1), Fn.Identity, col(10), 1.0)
         act(A("PF", 8, 12), A("ck", 0, 4), Fn.Identity, sc(3), 1.0)
-        act(A("PF", 12, 16), end("D7", 4, 4), Fn.Sign, sc(1), -1.0)
+        act(A("PF", 12, 16), end("D7", 4, 4), Fn.Sign, sc(4), -1.0)
         tt(A("PF", 16, 20), A("PF", 12, 16), A("PF", 4, 8), Op.mult)
         tt(A("PF", 20, 24), A("PF", 12, 16), A("ck", 8, 12), Op.mult)
         tt(A("HT", 0, 4), A("HT", 0, 4), A("PF", 20, 24), Op.max)
         cp(A("oS"), A("HT"))
-        act(sc(2), sc(1), Fn.Identity, float(K), 1.0)
+        act(sc(2), sc(1), Fn.Identity, col(9), 1.0)
         act(A("LAB", H, H + K), A("cI", 0, K), Fn.Identity, sc(3), 1.0)
         for c in range(4):
             bias = A("PF", 8 + c, 9 + c)
@@ -472,13 +504,13 @@ def rank_program(g, core, T, topo):
         came = len(topo.engines(other, core)) if direct else sum(len(topo.engines(c, core)) for c in _relays(T, topo, other, core))
         sent = issue("G", lambda moves=moves, t=t: g.remote_dma_fused(moves, local_sem=T.sem["sent%d" % t]), [A(qx), A(sxp)], [], 0.3, None,
                      lat=HOP if direct else 2 * HOP, more={"sent%d" % t: 2 * half, "arr%d" % t: came})
-        deal(A("D6"), A("X6"), A("LL"))
-        ts(oL, end("D6", 0, NB), -1.0, Op.mult, float(H), Op.add)
-        act(sm(6), end("D6", 0, NB), Fn.Identity, float(H), -1.0)
-        act(sm(7), sm(1), Fn.Sign, 0.5, 1.0)
-        tt(sm(8), sm(7), A("cj", 0, NB), Op.mult)
-        tt(sm(9), sm(8), sm(6), Op.max)
-        cp(oL2, sm(9))
+        for i in range(2):
+            hold(A("D6", H // 2 * i, H // 2 * (i + 1)), A("LL", 3 * H // 2 * i, 3 * H // 2 * i + H // 2))
+        act(sm(6), end("D6", 0, NB), Fn.Identity, col(8), -1.0)
+        act(sm(9), sm(1), Fn.Sign, 0.5, 1.0)
+        tt(sm(8), sm(9), A("cj", 0, NB), Op.mult)
+        tt(sm(7), sm(8), sm(6), Op.max)
+        cp(A("oA", 5 * NB, 7 * NB), A("SM", 6 * NB, 8 * NB))
         scan(A("CK2"), A("LE"), A("UU"), -K - 1.0, Op.add, Op.min)
         tt(A("NM"), ind(A("CK"), oL), A("CK2"), Op.is_ge)
         tt(A("NA"), ind(A("CK"), oL2), A("CK2"), Op.is_ge)
@@ -498,12 +530,8 @@ def rank_program(g, core, T, topo):
         scan(rev("Z", 0, H), rev("GO", 0, H), rev("XP", 0, H), 0.0, Op.mult, Op.min)
         scan(A("O"), A("HO"), A("Z"), 0.0, Op.mult, Op.min)
         scan(A("LAB", 0, H), A("LB", 1, H + 1), A("O"), -200.0, Op.max, Op.min)
-        if HS_ON == "V":
-            tt(A("HM"), ind(A("LAB"), A("oS")), A("mask"), Op.mult)
-            scan(A("HS"), A("c16"), A("HM"), 0.0, Op.mult, Op.add)
-        else:
-            cp(A("HM"), ind(A("LAB"), A("oS")), "S")
-            deal(A("HS"), A("X8"), A("HM"))
+        cp(A("HM"), ind(A("LAB"), A("oS")), HS_ON)
+        scan(A("HS"), A("cHn"), A("HM"), 0.0, Op.add, Op.max)
         ts(A("oH"), end("HS", 0, 20), sc(2), Op.add)
         xn = "xt%d" % (t + 1)
         for b in (2, 3, 0, 1):

@@ -16,23 +16,26 @@ NR = 1
 NE = 2
 NF = 2
 NFA = 2
-HS_ON = "S"
+HS_ON = "BS"
 Y_ON = "S"
 SOFT = False
-HOP, WAKE, LOAD, SLACK, TRIES = 3.0, 0.17, 2.0, 0.02, 1500
+CASES, MOVES, SIZE = ((0.17, 1.4),), 8, 400.0
+BULK, HOP, WAKE, LOAD, SLACK, TRIES = 3.2, 1.7, 0.19, 2.0, 0.02, 6000
 F32, BF, I32, U16, CODE, PLANE = "float32", "bfloat16", "int32", "uint16", "float8_e4m3fn_x4", "uint8"
 
 _SB = {
     "xt0": (4 * C, BF), "xt1": (4 * C, BF), "xt2": (4 * C, BF), "ut": (512, BF), "vt": (512, BF), "et": (516, BF), "ft": (512, BF),
     "qu0": (128, CODE), "su0": (128, PLANE), "qu": (128, CODE), "su": (128, PLANE), "qv": (128, CODE), "sv": (128, PLANE),
     "qw": (512, CODE), "sw": (512, PLANE), "qe": (512, CODE), "se": (512, PLANE),
-    "qx0": (C + 128, CODE), "sx0": (C + 128, PLANE), "qx1": (C + 128, CODE), "sx1": (C + 128, PLANE), "qx2": (C, CODE), "sx2": (C, PLANE),
-    "lc0": (384, CODE), "ls0": (384, PLANE), "lc1": (384, CODE), "ls1": (384, PLANE), "rc": (64, CODE), "rs": (256, PLANE),
+    "qx0": (C, CODE), "sx0": (C, PLANE), "qx1": (C, CODE), "sx1": (C, PLANE), "qx2": (C, CODE), "sx2": (C, PLANE), "qf": (128, CODE), "sf": (128, PLANE),
+    "lc0": (C, CODE), "ls0": (C, PLANE), "lc1": (C, CODE), "ls1": (C, PLANE), "rc": (C, CODE), "rs": (C, PLANE),
+    "lp0": (NB, U16), "lp1": (NB, U16), "rp": (NB, U16), "lq0": (NB, U16), "lq1": (NB, U16), "rq": (NB, U16),
+    "lk0": (4, U16), "lk1": (4, U16), "rk": (4, U16),
     "cI": (C + 16, F32), "cJ": (C + 16, BF), "cP": (8, I32), "cPf": (16, F32), "cK": (32, F32), "cTK": (C + 16, F32),
     "cRev": (H + 2, BF), "cTY": (C + 16, BF), "mask": (C + 16, BF), "cM": (H, BF), "cR": (H, BF), "cRn": (H, BF), "cC": (H, BF),
     "cN": (C, BF), "cH": (C, BF), "cHn": (C, BF), "c01": (C, BF),
     "cPn": (H, F32), "cj": (20, F32), "cm2": (NB, F32), "cb": (20, F32), "ck": (16, F32),
-    "oU": (8, U16), "oA": (80, U16), "oH": (20, U16), "oS": (20, U16),
+    "oU": (8, U16), "oA0": (80, U16), "oA1": (80, U16), "oH": (20, U16), "oS": (20, U16),
     "SW": (C + 8, F32), "KB": (NB * ROW, BF), "JK": (NB * H, BF), "JK2": (NB * H, BF), "CS": (NB * H, BF),
     "ACC": (32, F32), "I1": (20, I32), "SC": (16, F32), "LAB": (H + K, BF), "FA": (4 * WF, BF), "EC": (WF, F32),
     "TH": (4 * C, BF), "TF": (2 * C, BF), "TMP": (4 * C, BF), "HR": (4 * K, F32), "GG": (2 * C, F32),
@@ -55,8 +58,8 @@ for _b, (_d, _rows) in _ROWS.items():
 SCRATCH = {n: ("sbuf", [128, w], d) for n, (w, d) in _SB.items()}
 for _n in ("pS", "pT0", "pT1", "pT2", "pT3", "pH0", "pH1", "pH2"):
     SCRATCH[_n] = ("psum", [128, 512], F32)
-NDMA = 14
-SEMAPHORES = ["sV", "sS", "sT", "sG", "arr0", "arr1", "sent0", "sent1", "rin", "rout"] + ["d%d" % i for i in range(NDMA)]
+NDMA = 16
+SEMAPHORES = ["sV", "sS", "sT", "sG", "sent", "rout"] + ["in" + n for n in "cspqe"] + [n + t for n in "cspqe" for t in "01"] + ["d%d" % i for i in range(NDMA)]
 _ORDERS = {}
 
 
@@ -68,24 +71,31 @@ def _bits(engines):
     return sum(1 << e for e in engines)
 
 
+def _parcels(T, t):
+    codes = lambda n, i: T[n][:, H * i:H * i + H].bitcast(dt.uint8)
+    lists = T["oA%d" % t]
+    return [("c", [(codes("qx%d" % t, i), codes("rc", i), codes("lc%d" % t, i), i) for i in range(2)]),
+            ("s", [(T["sx%d" % t][:], T.rs[:], T["ls%d" % t][:], 0)]),
+            ("p", [(lists[:, 3 * NB:4 * NB], T.rp[:], T["lp%d" % t][:], 1)]),
+            ("q", [(lists[:, 4 * NB:5 * NB], T.rq[:], T["lq%d" % t][:], 1)]),
+            ("e", [(lists[:, 7 * NB:7 * NB + 4], T.rk[:], T["lk%d" % t][:], 0)])]
+
+
 def _relay_program(g, core, T, topo):
     for r, src in enumerate(T.cores):
         for t in range(R):
             dst = T.cores[r ^ STEP[t]]
-            if topo.may_write(src, dst):
+            if topo.may_write(src, dst) or core not in _relays(T, topo, src, dst):
                 continue
-            rel = _relays(T, topo, src, dst)
-            if core not in rel:
-                continue
-            n = len(topo.engines(src, core)) // 2
             rid, pid = topo.addr(dst, core)
-            m = topo.mask(core, dst)
-            g.wait_ge(T.sem.rin, n)
-            if core == rel[0]:
-                g.remote_dma(T["lc%d" % t][:, 192:256].bitcast(dt.uint8), T.rc[:].bitcast(dt.uint8), T.sem["arr%d" % t], T.sem.rout, pid, rid, m)
-            else:
-                g.remote_dma(T["ls%d" % t][:, 192:256], T.rs[:, 192:256], T.sem["arr%d" % t], T.sem.rout, pid, rid, m)
-            g.wait_ge(T.sem.rout, len(topo.engines(core, dst)))
+            calls = 0
+            for name, pieces in _parcels(T, t):
+                for _, mid, land, i in pieces:
+                    if _relays(T, topo, src, dst)[i] == core:
+                        g.wait_ge(T.sem["in" + name], len(topo.engines(src, core)) // len(pieces))
+                        g.remote_dma(land, mid, T.sem[name + str(t)], T.sem.rout, pid, rid, topo.mask(core, dst))
+                        calls += 1
+            g.wait_ge(T.sem.rout, calls * len(topo.engines(core, dst)))
 
 
 def _play(ops, after, way):
@@ -119,6 +129,15 @@ def _play(ops, after, way):
     return end, order
 
 
+def _replay(ops, order, wake, late):
+    now, done = {}, [0.0] * len(ops)
+    for i in order:
+        o = ops[i]
+        now[o["q"]] = max([now.get(o["q"], 0.0)] + [done[d] + wake for d in o["deps"]]) + o["cost"]
+        done[i] = now[o["q"]] + o["lat"] * (late if o["sem"] is None else 1.0)
+    return max(done)
+
+
 def _order(ops):
     key = tuple((o["q"], o["cost"], o["lat"]) for o in ops)
     if key not in _ORDERS:
@@ -127,13 +146,14 @@ def _order(ops):
             way[i] = ops[i]["cost"] + ops[i]["lat"] + max([way[j] + WAKE * ops[j]["deps"][i] for j in after[i]], default=0.0)
             for d in ops[i]["deps"]:
                 after[d].append(i)
-        best, seed = _play(ops, after, way), 1
+        worth = lambda got: (got[0] + sum(_replay(ops, got[1], *case) for case in CASES), got[1])
+        best, seed = worth(_play(ops, after, way)), 1
         for n in range(TRIES):
             new = list(way)
-            for m in range(6):
+            for m in range(MOVES):
                 seed = (seed * 6364136223846793005 + 1442695040888963407) % 2 ** 64
-                new[(seed >> 33) % len(ops)] += ((seed >> 20) % 1001 - 500) / 250.0
-            got = _play(ops, after, new)
+                new[(seed >> 33) % len(ops)] += ((seed >> 20) % 1001 - 500) / SIZE
+            got = worth(_play(ops, after, new))
             if got[0] <= best[0]:
                 best, way = got, new
         _ORDERS[key] = best[1]
@@ -157,8 +177,8 @@ def _emit(ops, queue, T):
                 deps[mark[d][0]] = max(deps.get(mark[d][0], 0), mark[d][1])
         for s, n in sorted(deps.items(), key=lambda e: -len(clocks.get(e, {}))):
             need(o["q"], s, n)
-        if o["arrive"]:
-            need(o["q"], *o["arrive"])
+        for s, n in o["arrive"]:
+            need(o["q"], s, n)
         call = o["fn"]()
         mark[i] = None
         if o["sem"]:
@@ -166,7 +186,8 @@ def _emit(ops, queue, T):
             call.then_inc(T.sem[o["sem"]], o["inc"])
             mark[i] = (o["sem"], count[o["sem"]])
             clocks[mark[i]] = dict(known[o["q"]], **{o["sem"]: count[o["sem"]]})
-        count.update(o["more"])
+        for s, n in o["more"].items():
+            count[s] = max(count.get(s, 0), n)
     for s, n in count.items():
         need("G", s, n)
 
@@ -200,7 +221,7 @@ def rank_program(g, core, T, topo):
     def meet(x, y):
         return x[1] < y[2] and y[1] < x[2] and (x[3] != y[3] or (x[1] - y[1]) % x[3] == 0)
 
-    def issue(q, fn, reads, writes, cost, sem="", inc=1, lat=0.0, deps=(), arrive=None, more=()):
+    def issue(q, fn, reads, writes, cost, sem="", inc=1, lat=0.0, deps=(), arrive=(), more=()):
         acc = [(x, False) for o in reads if isinstance(o, tuple) for x in o[1]] + [(x, True) for o in writes for x in o[1]]
         deps = {d: True for d in deps}
         for x, wr in acc:
@@ -225,8 +246,8 @@ def rank_program(g, core, T, topo):
     def narrow(*o):
         return 0.5 if all(_SB.get(x[1][0][0], (0, F32))[1] in (BF, U16) for x in o) else 1.0
 
-    def tt(out, a, b, op):
-        issue("V", lambda: g.vector.tensor_tensor(out[0], a[0], b[0], op), [a, b], [out], time(a, 1 if a[1][0][0][0] == "p" else 2))
+    def tt(out, a, b, op, **k):
+        issue("V", lambda: g.vector.tensor_tensor(out[0], a[0], b[0], op), [a, b], [out], time(a, 1 if a[1][0][0][0] == "p" else 2), **k)
 
     def ts(out, a, s1, o1, s2=None, o2=None):
         if o2 is None:
@@ -234,11 +255,11 @@ def rank_program(g, core, T, topo):
         else:
             issue("V", lambda: g.vector.tensor_scalar(out[0], a[0], ap(s1), ap(s2), o1, o2), [a, s1, s2], [out], time(a, narrow(out, a)))
 
-    def cp(out, a, q="V"):
+    def cp(out, a, q="V", **k):
         if q == "S":
-            issue("S", lambda: g.scalar.activation(out[0], a[0], Fn.Copy), [a], [out], time(a, 1))
+            issue("S", lambda: g.scalar.activation(out[0], a[0], Fn.Copy), [a], [out], time(a, 1), **k)
         else:
-            issue("V", lambda: g.vector.tensor_copy(out[0], a[0]), [a], [out], time(a, narrow(out, a)))
+            issue("V", lambda: g.vector.tensor_copy(out[0], a[0]), [a], [out], time(a, narrow(out, a)), **k)
 
     def scan(out, d0, d1, init, o0, o1):
         issue("V", lambda: g.vector.tensor_tensor_scan(out[0], d0[0], d1[0], ap(init), o0, o1), [d0, d1, init], [out], time(d0, narrow(out, d0, d1)))
@@ -290,7 +311,8 @@ def rank_program(g, core, T, topo):
         return (o[0].bitcast(dt.uint32),) + o[1:]
 
     dma("S", A("ut"), hbm(T.u[:]), 0.7)
-    first = dma("Y", A("xt0"), hbm(T.x[:]), 1.8)
+    dma("Y", A("xt0", 0, 2 * C), hbm(T.x[:, 0:2 * C]), 1.2)
+    first = dma("Y", A("xt0", 2 * C, 4 * C), hbm(T.x[:, 2 * C:4 * C]), 1.8)
     dma("Y", byte(A("qw")), hbm(T.wc[:]), 1.5, [first])
     dma("Y", A("sw"), hbm(T.ws[:]), 0.5, [first])
     dma("Y", A("vt"), hbm(T.v[:]), 0.7, [first])
@@ -298,10 +320,8 @@ def rank_program(g, core, T, topo):
     iota(A("cP", 0, 1), [[0, 1]], 0, 1)
     iota(A("cJ"), [[0, 21], [1, 16]], 0, 0)
     iota(A("cI"), [[1, C + 16]], 0, 0)
-    for b in range(4):
-        iota(A("FA", WF * b, WF * b + WF), [[0, WF]], 0, 0)
     iota(A("c01"), [[0, H], [1, 2]], 0, 0)
-    iota(A("EC"), [[1, WF]], -AT - C, 0)
+    iota(A("EC", AT + C, WF), [[1, K]], 0, 0)
     for o, v in ((A("ft"), 0.0), (A("et"), 0.0), (A("SW", C, C + 8), -BIG), (A("MN", 0, 16), 0.0),
                  (A("KEY", 0, 1), (C * 512 + C) * UNIT), (A("UP", 0, 1), 1.0), (A("DL", 0, 1), 1.0), (A("DL", C - 1, C), 0.0),
                  (A("PN", K, K + 1), 0.0), (A("CK", 0, 1), -K - 1.0), (A("LB", 0, 1), 0.0), (A("AN", 0, 1), 0.0), (A("FS", 0, 1), 4.0)):
@@ -311,8 +331,6 @@ def rank_program(g, core, T, topo):
     ts(A("cP", 2, 3), A("cP", 0, 1), 1, Op.bitwise_and)
     cp(A("cPf", 0, 3), A("cP", 0, 3))
     r16, odd = A("cPf", 1, 2), A("cPf", 2, 3)
-    quant(A("lc0", 256, 384), A("ls0", 256, 384), A("ft"))
-    quant(A("lc1", 256, 384), A("ls1", 256, 384), A("ft"))
     ts(A("cR"), A("cJ", 0, H), 0.5, Op.is_lt, 2 * FAR, Op.mult)
     act(A("cRn"), A("cR"), Fn.Identity, 0.0, -1.0)
     ts(A("mask"), A("cJ"), r16, Op.is_equal)
@@ -359,7 +377,26 @@ def rank_program(g, core, T, topo):
         quant(E("qe", b), E("se", b), A("et", 3 - b, 515 - b))
     quant(A("qv"), A("sv"), A("vt"))
 
-    oN, oQ, oG, oP, oB, oL, oL2, oE = [A("oA", NB * i, NB * i + (NB if i < 7 else 4)) for i in range(8)]
+    total = [0]
+
+    def send(t, n, reads, hop):
+        name, pieces = _parcels(T, t)[n]
+        other = T.cores[rank ^ STEP[t]]
+        direct = topo.may_write(core, other)
+        moves, came = [], 0
+        for i, (src, mid, land, rel) in enumerate(pieces):
+            to = other if direct else _relays(T, topo, core, other)[rel]
+            eng = topo.engines(core, to)
+            share = len(eng) // len(pieces)
+            moves.append(RemoteDMATransfer(dst_ids=[DstId(rid=topo.addr(to, core)[0], pnc=topo.addr(to, core)[1])],
+                                           dma_engine_mask=_bits(eng[share * i:share * i + share]), src=src, dst=land if direct else mid,
+                                           remote_sem=T.sem[name + str(t) if direct else "in" + name]))
+            total[0] += share
+            came += share if direct else len(topo.engines(_relays(T, topo, other, core)[rel], core))
+        sent = issue("G", lambda: g.remote_dma_fused(moves, local_sem=T.sem.sent), reads, [], 0.3, None, lat=hop if direct else 2 * hop,
+                     more={"sent": total[0], name + str(t): came})
+        return {"deps": [sent], "arrive": [(name + str(t), came)]}
+
     banksH = ["pH0", "pH1", "pH2", "pS"]
     M = lambda a, b: A("MN", 16 + a, 16 + b)
     end = lambda name, c, n=1: A(name, 16 * c + 15, 16 * (c + n), 16)
@@ -371,16 +408,22 @@ def rank_program(g, core, T, topo):
 
     for t in range(R):
         qx, sxp, lc, ls, nv = "qx%d" % t, "sx%d" % t, "lc%d" % t, "ls%d" % t, NV[t]
-        quant(A(qx, 0, C), A(sxp, 0, C), A("xt%d" % t))
+        oA = "oA%d" % t
+        oN, oQ, oG, oP, oB, oL, oL2, oE = [A(oA, NB * i, NB * i + (NB if i < 7 else 4)) for i in range(8)]
+        for a, b in ((0, H), (H, C)) if t == 0 else ((0, C),):
+            quant(A(qx, a, b), A(sxp, a, b), A("xt%d" % t, 4 * a, 4 * b))
+        got = [send(t, 0, [A(qx)], BULK), send(t, 1, [A(sxp)], HOP)]
+        both = {k: got[0][k] + got[1][k] for k in got[0]}
         for bank in ("pS", "pH0"):
             mm(A(bank, 0, C), A("qu"), A("su"), A(qx, 0, C), A(sxp, 0, C))
         for b in range(4):
             mm(A("pT%d" % b, 0, C), E("qe", b), E("se", b), A(qx, 0, C), A(sxp, 0, C))
-        for b in range(4):
-            act(A("TH", C * b, C * b + C), A("pT%d" % b, 0, C), Fn.Copy, 0.0, 0.5)
-            cp(A("FA", WF * b + AT + C, WF * b + WF), A("pT%d" % b, 0, K), "S")
         for b in range(2):
             cp(A("TF", C * b, C * b + C), A("pT%d" % (2 + b), 0, C), "S")
+        for b, bank in enumerate(("pH1", "pH2", "pT2", "pT3")):
+            mm(A(bank, 0, C), E("qe", b), E("se", b), A(lc), A(ls), **both)
+            act(A("TH", C * b, C * b + C), A(bank, 0, C), Fn.Copy, 0.0, 0.5)
+            cp(A("FA", WF * b + AT + C, WF * b + WF), A(bank, 0, K), "S")
         cp(A("SW", 0, C, 2), A("pH0", 0, C, 2), "S")
         cp(A("SW", 1, C, 2), A("pH0", 1, C, 2), "S")
         tt(M(H, C), A("pS", 1, C, 2), A("SW", 2, C + 1, 2), Op.min)
@@ -406,13 +449,13 @@ def rank_program(g, core, T, topo):
         tt(A("PF", 4, 8), A("PF", 0, 4), A("ck", 4, 8), Op.add)
         for c in range(NR, NB):
             act(A("JK", H * c, H * c + H), M(H, C), Fn.Sign, end("DT", NB + c), -1.0, A("ACC", c, c + 1))
-        ts(A("oA", NR, NB), A("ACC", NR, NB), -1.0, Op.mult, float(H), Op.add)
+        ts(A(oA, NR, NB), A("ACC", NR, NB), -1.0, Op.mult, float(H), Op.add)
         for c in range(NR):
             ts(A("JK", H * c, H * c + H), M(H, C), end("DT", NB + c), Op.is_lt)
             ts(A("JK2", H * c, H * c + H), M(H, C), end("DT", NB + c), Op.is_le)
             scan(A("CS", H * c, H * c + H), A("JK", H * c, H * c + H), A("JK2", H * c, H * c + H), -float(H), Op.add, Op.add)
         if NR:
-            ts(A("oA", 0, NR), A("CS", H - 1, NR * H, H), -1.0, Op.mult, float(H), Op.add)
+            ts(A(oA, 0, NR), A("CS", H - 1, NR * H, H), -1.0, Op.mult, float(H), Op.add)
         tt(A("KEY", 1, H + 1), ind(A("cTK"), oN), A("POS"), Op.add)
         act(A("KEYN", 1, H + 1), A("KEY", 1, H + 1), Fn.Identity, -1.0, 1.0)
         for c in range(NB):
@@ -436,12 +479,14 @@ def rank_program(g, core, T, topo):
         tt(sm(4), sm(3), sm(0), Op.max)
         tt(sm(5), sm(4), q, Op.min)
         cp(oB, sm(5))
+        gotp, got = send(t, 2, [oP], HOP), send(t, 3, [oB], HOP)
+        oP, oB = A("lp%d" % t), A("lq%d" % t)
         for b in range(4):
-            cp(A("TMP", C * b, C * b + C, 2), ind(A("TH", C * b, C * b + C), oP), "S")
+            cp(A("TMP", C * b, C * b + C, 2), ind(A("TH", C * b, C * b + C), oP), "S", **gotp)
             if b < NFA:
-                tt(A("FA", WF * b + AT + 1, WF * b + AT + C, 2), ind(A("TH", C * b, C * b + C), oB), A("TMP", C * b, C * b + C, 2), Op.add)
+                tt(A("FA", WF * b + AT + 1, WF * b + AT + C, 2), ind(A("TH", C * b, C * b + C), oB), A("TMP", C * b, C * b + C, 2), Op.add, **got)
             else:
-                cp(A("TMP", C * b + 1, C * b + C, 2), ind(A("TH", C * b, C * b + C), oB), "S")
+                cp(A("TMP", C * b + 1, C * b + C, 2), ind(A("TH", C * b, C * b + C), oB), "S", **got)
                 scan(A("FA", WF * b + AT, WF * b + AT + C), A("c01"), A("TMP", C * b, C * b + C), 0.0, Op.mult, Op.add)
         tt(A("NG"), ind(A("SW"), oQ), M(0, H), Op.subtract)
         tt(A("X3"), ind(A("SW"), oQ), A("X1"), Op.subtract)
@@ -453,9 +498,9 @@ def rank_program(g, core, T, topo):
             ts(A("JK", H * c, H * c + H), A("NG"), end("DP", c), Op.is_lt)
             cumsum(A("CS", H * c, H * c + H), A("JK", H * c, H * c + H), A("SM", 2 * NB + c, 2 * NB + c + 1))
         if nv:
-            cp(A("oA", 20, 20 + nv), A("CS", H - 1, nv * H, H))
+            cp(A(oA, 20, 20 + nv), A("CS", H - 1, nv * H, H))
         if nv < NB:
-            ts(A("oA", 20 + nv, 30), A("ACC", 10 + nv, 20), float(C), Op.min)
+            ts(A(oA, 20 + nv, 30), A("ACC", 10 + nv, 20), float(C), Op.min)
         cp(A("Y"), ind(A("cTY"), oG), Y_ON)
         scan(A("MU"), A("Y"), A("Y"), 0.0, Op.min, Op.min)
         mu = A("MU", H - 1, H)
@@ -484,33 +529,18 @@ def rank_program(g, core, T, topo):
             else:
                 got = A("ACC", 20 + c, 21 + c)
                 act(A("JK2", H * c, H * c + H), CK, Fn.Sign, bias, -1.0, got)
-            ts(A("oA", 70 + c, 71 + c), got, float(AT + 1 if c < NE else H + AT + 1), Op.add, A("PF", 16 + c, 17 + c), Op.max)
+            ts(A(oA, 70 + c, 71 + c), got, float(AT + 1 if c < NE else H + AT + 1), Op.add, A("PF", 16 + c, 17 + c), Op.max)
+        got = send(t, 4, [oE], HOP)
         for b in range(4):
-            cp(lane("ft", b, K), ind(A("FA", WF * b, WF * b + WF), oE), "V" if b < NF else "S")
-        quant(A(qx, C, C + 128), A(sxp, C, C + 128), A("ft"))
-        other = T.cores[rank ^ STEP[t]]
-        direct = topo.may_write(core, other)
-        to = [other, other] if direct else _relays(T, topo, core, other)
-        eng = topo.engines(core, to[0])
-        half = len(eng) // 2
-        ids = [DstId(rid=topo.addr(d, core)[0], pnc=topo.addr(d, core)[1]) for d in to]
-        rsem = T.sem["arr%d" % t] if direct else T.sem.rin
-        moves = [
-            RemoteDMATransfer(dst_ids=[ids[0]], dma_engine_mask=_bits(eng[:half]), remote_sem=rsem, src=T[qx][:, C:C + K].bitcast(dt.uint8),
-                              dst=(T[lc][:, 192:256] if direct else T.rc[:]).bitcast(dt.uint8)),
-            RemoteDMATransfer(dst_ids=[ids[1]], dma_engine_mask=_bits(eng[half:]), remote_sem=rsem, src=T[sxp][:, C + K - 256:C + K],
-                              dst=T[ls][:, 0:256] if direct else T.rs[:]),
-        ]
-        came = len(topo.engines(other, core)) if direct else sum(len(topo.engines(c, core)) for c in _relays(T, topo, other, core))
-        sent = issue("G", lambda moves=moves, t=t: g.remote_dma_fused(moves, local_sem=T.sem["sent%d" % t]), [A(qx), A(sxp)], [], 0.3, None,
-                     lat=HOP if direct else 2 * HOP, more={"sent%d" % t: 2 * half, "arr%d" % t: came})
+            cp(lane("ft", b, K), ind(A("FA", WF * b, WF * b + WF), A("lk%d" % t)), "V" if b < NF else "S", **got)
+        quant(A("qf"), A("sf"), A("ft"))
         for i in range(2):
             hold(A("D6", H // 2 * i, H // 2 * (i + 1)), A("LL", 3 * H // 2 * i, 3 * H // 2 * i + H // 2))
         act(sm(6), end("D6", 0, NB), Fn.Identity, col(8), -1.0)
         act(sm(9), sm(1), Fn.Sign, 0.5, 1.0)
         tt(sm(8), sm(9), A("cj", 0, NB), Op.mult)
         tt(sm(7), sm(8), sm(6), Op.max)
-        cp(A("oA", 5 * NB, 7 * NB), A("SM", 6 * NB, 8 * NB))
+        cp(A(oA, 5 * NB, 7 * NB), A("SM", 6 * NB, 8 * NB))
         scan(A("CK2"), A("LE"), A("UU"), -K - 1.0, Op.add, Op.min)
         tt(A("NM"), ind(A("CK"), oL), A("CK2"), Op.is_ge)
         tt(A("NA"), ind(A("CK"), oL2), A("CK2"), Op.is_ge)
@@ -530,12 +560,16 @@ def rank_program(g, core, T, topo):
         scan(rev("Z", 0, H), rev("GO", 0, H), rev("XP", 0, H), 0.0, Op.mult, Op.min)
         scan(A("O"), A("HO"), A("Z"), 0.0, Op.mult, Op.min)
         scan(A("LAB", 0, H), A("LB", 1, H + 1), A("O"), -200.0, Op.max, Op.min)
-        cp(A("HM"), ind(A("LAB"), A("oS")), HS_ON)
+        if HS_ON[t] in "SV":
+            cp(A("HM"), ind(A("LAB"), A("oS")), HS_ON[t])
+        else:
+            cp(A("HM", 0, H), ind(A("LAB"), A("oS", 0, NB)), "S")
+            cp(A("HM", H, C), ind(A("LAB"), A("oS", NB, 2 * NB)), "V")
         scan(A("HS"), A("cHn"), A("HM"), 0.0, Op.add, Op.max)
         ts(A("oH"), end("HS", 0, 20), sc(2), Op.add)
         xn = "xt%d" % (t + 1)
         for b in (2, 3, 0, 1):
-            mm(A(banksH[b], 0, 128), E("qw", b), E("sw", b), A(lc, 192, 320), A(ls, 192, 320), deps=[sent], arrive=("arr%d" % t, came))
+            mm(A(banksH[b], 0, 128), E("qw", b), E("sw", b), A("qf"), A("sf"))
             act(A("HR", K * b, K * b + K), A(banksH[b], 0, K), Fn.Relu, 0.0, 0.03125)
         for b in range(2):
             act(A("GG", C * b, C * b + C), ind(A("HR", K * b, K * b + K), A("oH")), Fn.Copy)
@@ -546,7 +580,7 @@ def rank_program(g, core, T, topo):
     scan(A("EC", AT + 1, AT + C, 2), A("cI", 0, C, 2), A("UP", 1, C, 2), 0.0, Op.max, Op.add)
     act(A("ER"), ind(A("EC"), oE), Fn.Copy)
     act(A("OLR"), ind(A("ER"), A("oH")), Fn.Copy)
-    dma("G", hbm(T.ol[:]), (T.OLR[0:128:16, :], A("OLR")[1]), 0.0)
+    dma("Y", hbm(T.ol[:]), (T.OLR[0:128:16, :], A("OLR")[1]), 0.0)
     quant(A("qx2"), A("sx2"), A("xt2"))
     mm(A("pH0", 0, H), A("qv"), A("sv"), A("qx2", 0, H), A("sx2", 0, H))
     mm(A("pH1", 0, H), A("qv"), A("sv"), A("qx2", H, C), A("sx2", H, C))

@@ -1,5 +1,5 @@
 from concourse.bass import DstId, RemoteDMATransfer
-from concourse.mybir import dt, AluOpType, AxisListType, ActivationFunctionType
+from concourse.mybir import dt, AluOpType, ActivationFunctionType
 
 C, K, R = 320, 64, 2
 STEP = [1, 2]
@@ -11,42 +11,40 @@ FAR = 2.0 ** 98
 DROP = 192.0
 UNIT = 2.0 ** -18
 AT, WF = 48, 432
+NRS = [1, 1]
 NV = [6, 6]
-NR = 1
-NE = 2
-NF = 2
-NFA = 2
-HS_ON = "BS"
-Y_ON = "S"
-SOFT = False
-CASES, MOVES, SIZE = ((0.17, 1.4),), 8, 400.0
-BULK, HOP, WAKE, LOAD, SLACK, TRIES = 3.2, 1.7, 0.19, 2.0, 0.02, 6000
+NES = [0, 1]
+NFAS = [0, 2]
+NFS = [2, 2]
+HV = [H, K]
+BULK, HOP, WAKE, LOAD, CASES = 3.2, 1.7, 0.19, 1.0, ((0.17, 1.4),)
+TRIES, MOVES, SIZE, HEAT = 8000, 5, 350.0, 0.15
 F32, BF, I32, U16, CODE, PLANE = "float32", "bfloat16", "int32", "uint16", "float8_e4m3fn_x4", "uint8"
 
 _SB = {
     "xt0": (4 * C, BF), "xt1": (4 * C, BF), "xt2": (4 * C, BF), "ut": (512, BF), "vt": (512, BF), "et": (516, BF), "ft": (512, BF),
     "qu0": (128, CODE), "su0": (128, PLANE), "qu": (128, CODE), "su": (128, PLANE), "qv": (128, CODE), "sv": (128, PLANE),
-    "qw": (512, CODE), "sw": (512, PLANE), "qe": (512, CODE), "se": (512, PLANE),
-    "qx0": (C, CODE), "sx0": (C, PLANE), "qx1": (C, CODE), "sx1": (C, PLANE), "qx2": (C, CODE), "sx2": (C, PLANE), "qf": (128, CODE), "sf": (128, PLANE),
+    "qw": (512, CODE), "sw": (512, PLANE), "qe": (512, CODE), "se": (512, PLANE), "qf": (128, CODE), "sf": (128, PLANE),
+    "qx0": (C, CODE), "sx0": (C, PLANE), "qx1": (C, CODE), "sx1": (C, PLANE), "qx2": (C, CODE), "sx2": (C, PLANE),
     "lc0": (C, CODE), "ls0": (C, PLANE), "lc1": (C, CODE), "ls1": (C, PLANE), "rc": (C, CODE), "rs": (C, PLANE),
     "lp0": (NB, U16), "lp1": (NB, U16), "rp": (NB, U16), "lq0": (NB, U16), "lq1": (NB, U16), "rq": (NB, U16),
     "lk0": (4, U16), "lk1": (4, U16), "rk": (4, U16),
-    "cI": (C + 16, F32), "cJ": (C + 16, BF), "cP": (8, I32), "cPf": (16, F32), "cK": (32, F32), "cTK": (C + 16, F32),
-    "cRev": (H + 2, BF), "cTY": (C + 16, BF), "mask": (C + 16, BF), "cM": (H, BF), "cR": (H, BF), "cRn": (H, BF), "cC": (H, BF),
+    "cI": (C + 16, F32), "cJ": (H + 16, BF), "cP": (8, I32), "cPf": (16, F32), "cK": (32, F32), "cTK": (C + 16, F32),
+    "cRev": (H + 2, BF), "cTY": (C + 16, BF), "mask": (H + 16, BF), "cM": (H, BF), "cR": (H, BF), "cRn": (H, BF), "cC": (H, BF),
     "cN": (C, BF), "cH": (C, BF), "cHn": (C, BF), "c01": (C, BF),
-    "cPn": (H, F32), "cj": (20, F32), "cm2": (NB, F32), "cb": (20, F32), "ck": (16, F32),
+    "cPn": (H, F32), "cj": (20, F32), "cm2": (NB, F32), "cb": (20, F32), "ck": (8, F32),
     "oU": (8, U16), "oA0": (80, U16), "oA1": (80, U16), "oH": (20, U16), "oS": (20, U16),
     "SW": (C + 8, F32), "KB": (NB * ROW, BF), "JK": (NB * H, BF), "JK2": (NB * H, BF), "CS": (NB * H, BF),
-    "ACC": (32, F32), "I1": (20, I32), "SC": (16, F32), "LAB": (H + K, BF), "FA": (4 * WF, BF), "EC": (WF, F32),
+    "ACC": (32, F32), "I1": (20, I32), "SC": (16, F32), "LAB": (H, BF), "FA": (4 * WF, BF), "EC": (WF, F32),
     "TH": (4 * C, BF), "TF": (2 * C, BF), "TMP": (4 * C, BF), "HR": (4 * K, F32), "GG": (2 * C, F32),
     "ER": (K, F32), "OLR": (C, F32), "YO": (C, F32),
 }
 _ROWS = {
-    "rf": (F32, {"MN": C + 32, "X1": H, "XN": C + 2, "DT": C, "US": H, "POS": H, "KEY": H + 2, "KEYN": H + 2, "LR": 2 * C, "DS": C, "NG": H, "X3": H,
-                 "DP": H, "SM": 120, "FS": H + 2, "BS": H, "HT": 20, "PF": 24}),
-    "rb": (BF, {"UP": C + 2, "DL": C, "D4": C, "D5": H, "LL": C, "D6": H, "PN": 2 * K + 2, "D7": 2 * K,
-                "Y": H, "MU": H, "OUT": H, "LE": H, "LT": H, "UU": H, "CK": H + 2, "CK2": H, "NM": H, "NA": H, "AN": H + 2, "KP": H, "LP": H, "W0": H,
-                "W1": H, "SD": H, "NS": H, "GO": H, "HO": H, "LB": H + 2, "XP": H, "Z": H, "O": H, "HM": C, "HS": C}),
+    "rf": (F32, {"MN": C + 32, "X1": H, "XN": C + 2, "DT": C, "US": H, "POS": H, "KEY": H + 2, "KEYN": H + 2, "LR": 2 * C, "DS": C,
+                 "NG": H, "X3": H, "DP": H, "SM": 120, "FS": H + 2, "BS": H, "HT": 20, "PF": 20}),
+    "rb": (BF, {"UP": C + 2, "DL": C, "D4": C, "D5": H, "LL": C, "D6": H, "PN": 2 * K + 2, "D7": 2 * K, "Y": H, "MU": H, "OUT": H, "LE": H,
+                "LT": H, "UU": H, "CK": H + 2, "CK2": H, "NM": H, "NA": H, "N1": H, "N2": H, "N3": H, "AN": H + 2, "KP": H, "LP": H,
+                "W1": H, "SD": H, "NS": H, "GO": H, "HO": H, "LB": H, "XP": H, "Z": H, "O": H, "JN": H, "HM": C, "HS": C}),
 }
 _AT = {}
 for _b, (_d, _rows) in _ROWS.items():
@@ -59,7 +57,8 @@ SCRATCH = {n: ("sbuf", [128, w], d) for n, (w, d) in _SB.items()}
 for _n in ("pS", "pT0", "pT1", "pT2", "pT3", "pH0", "pH1", "pH2"):
     SCRATCH[_n] = ("psum", [128, 512], F32)
 NDMA = 16
-SEMAPHORES = ["sV", "sS", "sT", "sG", "sent", "rout"] + ["in" + n for n in "cspqe"] + [n + t for n in "cspqe" for t in "01"] + ["d%d" % i for i in range(NDMA)]
+SEMAPHORES = (["sV", "sS", "sT", "sG", "sent", "rout"] + ["in" + n for n in "cspqe"] + [n + t for n in "cspqe" for t in "01"]
+              + ["d%d" % i for i in range(NDMA)])
 _ORDERS = {}
 
 
@@ -98,64 +97,62 @@ def _relay_program(g, core, T, topo):
             g.wait_ge(T.sem.rout, calls * len(topo.engines(core, dst)))
 
 
-def _play(ops, after, way):
-    now, left, free = {}, [len(o["deps"]) for o in ops], {}
-    for i, o in enumerate(ops):
-        now[o["q"]] = 0.0
-        free.setdefault(o["q"], [])
-        if not o["deps"]:
-            free[o["q"]].append(i)
-    ready, order, end = [0.0] * len(ops), [], 0.0
-    while len(order) < len(ops):
-        q = min((q for q in free if free[q]), key=lambda q: max(now[q], min(ready[i] for i in free[q])))
-        best, t = max(free[q], key=lambda i: way[i]), now[q]
-        rb = ready[best]
-        if rb - t > 0.01:
-            fit = [i for i in free[q] if ready[i] < rb and
-                   max(ready[i], t) + ops[i]["cost"] + way[best] <= rb + max(way[best] + SLACK, ops[best]["cost"] + way[i])]
-            if fit:
-                best = max(fit, key=lambda i: way[i] - 8 * max(0.0, ready[i] - t))
-        free[q].remove(best)
-        now[q] = max(t, ready[best]) + ops[best]["cost"]
-        done = now[q] + ops[best]["lat"]
+def _fit(ops, before, after, rank, back):
+    left, ready, start, end = [len(b) for b in before], [0.0] * len(ops), [0.0] * len(ops), 0.0
+    free, taken = sorted((rank[i], i) for i in range(len(ops)) if not left[i]), {}
+    while free:
+        i = free.pop(0)[1]
+        cost, lat, line = ops[i]["cost"], ops[i]["lat"], taken.setdefault(ops[i]["q"], [])
+        t, lo, hi = ready[i] + (lat if back else 0.0), 0, len(line)
+        while lo < hi:
+            mid = (lo + hi) // 2
+            lo, hi = (mid + 1, hi) if line[mid][1] <= t else (lo, mid)
+        while lo < len(line) and line[lo][0] < t + cost - 1e-9:
+            t, lo = line[lo][1], lo + 1
+        line.insert(lo, (t, t + cost))
+        start[i], done = t, t + cost + (0.0 if back else lat)
         end = max(end, done)
-        order.append(best)
-        for j in after[best]:
-            if ops[j]["deps"][best]:
-                ready[j] = max(ready[j], done + WAKE)
+        for j in after[i]:
+            waits = ops[max(i, j)]["deps"][min(i, j)]
+            ready[j] = max(ready[j], done + WAKE if waits else t + cost - (ops[j]["lat"] if back else 0.0))
             left[j] -= 1
             if not left[j]:
-                free[ops[j]["q"]].append(j)
-    return end, order
+                free.append((rank[j], j))
+        free.sort()
+    return end, start
 
 
 def _replay(ops, order, wake, late):
     now, done = {}, [0.0] * len(ops)
     for i in order:
         o = ops[i]
-        now[o["q"]] = max([now.get(o["q"], 0.0)] + [done[d] + wake for d in o["deps"]]) + o["cost"]
-        done[i] = now[o["q"]] + o["lat"] * (late if o["sem"] is None else 1.0)
+        now[o["q"]] = max([now.get(o["q"], 0.0)] + [done[d] + wake for d, waits in o["deps"].items() if waits]) + o["cost"]
+        done[i] = now[o["q"]] + o["lat"] * (late if o["q"] == "G" else 1.0)
     return max(done)
 
 
 def _order(ops):
     key = tuple((o["q"], o["cost"], o["lat"]) for o in ops)
     if key not in _ORDERS:
-        way, after = [0.0] * len(ops), [[] for o in ops]
-        for i in reversed(range(len(ops))):
-            way[i] = ops[i]["cost"] + ops[i]["lat"] + max([way[j] + WAKE * ops[j]["deps"][i] for j in after[i]], default=0.0)
-            for d in ops[i]["deps"]:
+        n = len(ops)
+        before, after = [list(o["deps"]) for o in ops], [[] for o in ops]
+        for i in range(n):
+            for d in before[i]:
                 after[d].append(i)
-        worth = lambda got: (got[0] + sum(_replay(ops, got[1], *case) for case in CASES), got[1])
-        best, seed = worth(_play(ops, after, way)), 1
-        for n in range(TRIES):
-            new = list(way)
+        best, here, seed, rank = None, None, 1, [-float(i) for i in range(n)]
+        for turn in range(TRIES):
+            late = _fit(ops, after, before, rank, True)[1]
+            end, start = _fit(ops, before, after, [-late[i] - ops[i]["cost"] for i in range(n)], False)
+            order = sorted(range(n), key=lambda i: start[i])
+            worth = end + sum(_replay(ops, order, *case) for case in CASES)
+            if best is None or worth <= best[0]:
+                best = (worth, order)
+            if here is None or worth <= here[0] + HEAT * (1 - turn / TRIES) * (seed >> 40) / 2 ** 24:
+                here = (worth, start)
+            rank = [-here[1][i] - ops[i]["cost"] for i in range(n)]
             for m in range(MOVES):
                 seed = (seed * 6364136223846793005 + 1442695040888963407) % 2 ** 64
-                new[(seed >> 33) % len(ops)] += ((seed >> 20) % 1001 - 500) / SIZE
-            got = worth(_play(ops, after, new))
-            if got[0] <= best[0]:
-                best, way = got, new
+                rank[(seed >> 33) % n] += ((seed >> 20) % 1001 - 500) / SIZE
         _ORDERS[key] = best[1]
     return _ORDERS[key]
 
@@ -171,9 +168,12 @@ def _emit(ops, queue, T):
 
     for i in _order(ops):
         o = ops[i]
+        if o["fn"] is None:
+            mark[i] = mark[i - 1]
+            continue
         deps = {}
-        for d, hard in o["deps"].items():
-            if mark[d] and hard:
+        for d, waits in o["deps"].items():
+            if mark[d] and waits:
                 deps[mark[d][0]] = max(deps.get(mark[d][0], 0), mark[d][1])
         for s, n in sorted(deps.items(), key=lambda e: -len(clocks.get(e, {}))):
             need(o["q"], s, n)
@@ -199,7 +199,7 @@ def rank_program(g, core, T, topo):
         return
     Op, Fn = AluOpType, ActivationFunctionType
     queue = {"V": g.vector, "S": g.scalar, "T": g.tensor, "G": g, "Y": g.sync}
-    ops, hist, dmas = [], {}, [0]
+    ops, hist, dmas, total = [], {}, [0], [0]
 
     def place(name, a, b):
         buf, o, w = _AT.get(name, (name, 0, None))
@@ -221,14 +221,13 @@ def rank_program(g, core, T, topo):
     def meet(x, y):
         return x[1] < y[2] and y[1] < x[2] and (x[3] != y[3] or (x[1] - y[1]) % x[3] == 0)
 
-    def issue(q, fn, reads, writes, cost, sem="", inc=1, lat=0.0, deps=(), arrive=(), more=()):
+    def issue(q, fn, reads, writes, cost, sem="", inc=1, lat=0.0, deps=(), arrive=(), more=(), behind=()):
         acc = [(x, False) for o in reads if isinstance(o, tuple) for x in o[1]] + [(x, True) for o in writes for x in o[1]]
-        deps = {d: True for d in deps}
+        deps = dict([(d, False) for d in behind] + [(d, True) for d in deps])
         for x, wr in acc:
             for (y, wr2, i) in hist.get(x[0], []):
-                same = ops[i]["q"] == q
-                if (x[0][0] == "p" and not same) or ((wr or wr2) and meet(x, y)):
-                    deps[i] = deps.get(i, False) or not (SOFT and same and wr and q in "VS" and ops[i]["sem"] == "s" + q and sem == "")
+                if (x[0][0] == "p" and ops[i]["q"] != q) or ((wr or wr2) and meet(x, y)):
+                    deps[i] = True
         ops.append({"q": q, "fn": fn, "deps": deps, "cost": cost, "lat": lat, "sem": "s" + q if sem == "" else sem, "inc": inc,
                     "arrive": arrive, "more": dict(more)})
         for x, wr in acc:
@@ -270,10 +269,6 @@ def rank_program(g, core, T, topo):
     def carry(out, d):
         scan(out, A("cR", 0, d[2]), d, 0.0, Op.add, Op.min)
 
-    def deal(out, tmp, row):
-        scan(tmp, row, A("cM", 0, row[2]), FAR, Op.min, Op.max)
-        carry(out, tmp)
-
     def hold(out, row):
         scan(out, A("cH", 0, row[2]), row, 0.0, Op.add, Op.min)
 
@@ -291,93 +286,16 @@ def rank_program(g, core, T, topo):
         issue("T", lambda: g.tensor.matmul_mx(out[0], wq[0], ws[0], xq[0], xs[0], True, True), [wq, ws, xq, xs], [out], 0.0006 * (out[2] + 16), **k)
 
     def iota(out, pattern, base, cm):
-        buf = out[1][0][0]
-        if _SB[buf][1] == I32:
+        if _SB[out[1][0][0]][1] == I32:
             issue("G", lambda: g.iota(out[0], pattern, base, cm), [], [out], 0.16 + 0.002 * out[2])
         else:
             issue("G", lambda: g.iota(out[0], pattern, base, cm, allow_small_or_imprecise_dtypes=True), [], [out], 0.16 + 0.002 * out[2])
 
-    def dma(q, out, a, us, deps=()):
+    def dma(q, out, a, us, deps=(), last=None):
         dmas[0] += 1
-        return issue(q, lambda: queue[q].dma_start(out[0], a[0]), [a], [out], 0.1, "d%d" % (dmas[0] - 1), 16, LOAD + us, deps)
-
-    def hbm(x):
-        return (x, [], 0, False)
-
-    def byte(o):
-        return (o[0].bitcast(dt.uint8),) + o[1:]
-
-    def word(o):
-        return (o[0].bitcast(dt.uint32),) + o[1:]
-
-    dma("S", A("ut"), hbm(T.u[:]), 0.7)
-    dma("Y", A("xt0", 0, 2 * C), hbm(T.x[:, 0:2 * C]), 1.2)
-    first = dma("Y", A("xt0", 2 * C, 4 * C), hbm(T.x[:, 2 * C:4 * C]), 1.8)
-    dma("Y", byte(A("qw")), hbm(T.wc[:]), 1.5, [first])
-    dma("Y", A("sw"), hbm(T.ws[:]), 0.5, [first])
-    dma("Y", A("vt"), hbm(T.v[:]), 0.7, [first])
-    iota(A("cK"), [[16, 32]], 0, 0)
-    iota(A("cP", 0, 1), [[0, 1]], 0, 1)
-    iota(A("cJ"), [[0, 21], [1, 16]], 0, 0)
-    iota(A("cI"), [[1, C + 16]], 0, 0)
-    iota(A("c01"), [[0, H], [1, 2]], 0, 0)
-    iota(A("EC", AT + C, WF), [[1, K]], 0, 0)
-    for o, v in ((A("ft"), 0.0), (A("et"), 0.0), (A("SW", C, C + 8), -BIG), (A("MN", 0, 16), 0.0),
-                 (A("KEY", 0, 1), (C * 512 + C) * UNIT), (A("UP", 0, 1), 1.0), (A("DL", 0, 1), 1.0), (A("DL", C - 1, C), 0.0),
-                 (A("PN", K, K + 1), 0.0), (A("CK", 0, 1), -K - 1.0), (A("LB", 0, 1), 0.0), (A("AN", 0, 1), 0.0), (A("FS", 0, 1), 4.0)):
-        fill(o, v)
-    cp(A("oU"), A("cK", 0, 8))
-    ts(A("cP", 1, 2), A("cP", 0, 1), 15, Op.bitwise_and)
-    ts(A("cP", 2, 3), A("cP", 0, 1), 1, Op.bitwise_and)
-    cp(A("cPf", 0, 3), A("cP", 0, 3))
-    r16, odd = A("cPf", 1, 2), A("cPf", 2, 3)
-    ts(A("cR"), A("cJ", 0, H), 0.5, Op.is_lt, 2 * FAR, Op.mult)
-    act(A("cRn"), A("cR"), Fn.Identity, 0.0, -1.0)
-    ts(A("mask"), A("cJ"), r16, Op.is_equal)
-    act(A("cM"), A("mask", 0, H), Fn.Identity, FAR, -2 * FAR)
-    act(A("cN", 1, C, 2), A("mask", 0, H), Fn.Identity, FAR, -2 * FAR)
-    act(A("cN", 0, C, 2), A("mask", 15, H + 15), Fn.Identity, FAR, -2 * FAR)
-    fill(A("cN", 0, 1), FAR)
-    act(A("XN", C, C + 1), A("mask", 15, 16), Fn.Identity, FAR, -FAR - BIG)
-    act(A("HM"), A("mask", 15, C + 15), Fn.Identity, 0.0, -DROP / 1024.0)
-    act(A("HS"), A("mask", 0, C), Fn.Identity, 0.0, 1024.0)
-    scan(A("cH"), A("HM"), A("HS"), 0.0, Op.mult, Op.add)
-    act(A("cHn"), A("cH"), Fn.Identity, 0.0, -1.0)
-    act(A("cC", 0, H, 2), A("cH", 0, H // 2), Fn.Identity, 0.0, 3.0 / DROP)
-    cp(A("cC", 1, H, 2), A("mask", 0, H // 2), "S")
-    col = lambda i: A("cPf", i, i + 1)
-    act(col(6), A("mask", 15, 16), Fn.Identity, DROP, -DROP)
-    act(col(7), col(6), Fn.Identity, 0.0, 3.0 / DROP)
-    act(col(8), col(6), Fn.Identity, float(H), -1.0)
-    act(col(9), col(6), Fn.Identity, float(K), -1.0)
-    act(col(10), col(6), Fn.Identity, 0.0, -1.0)
-    act(col(11), col(6), Fn.Identity, (C - 1) * 512.0, -3.0 / DROP / UNIT)
-    ts(A("cj"), A("cK", 0, 20), r16, Op.add)
-    act(A("cm2"), A("cj", 0, NB), Fn.Identity, col(6), 2.0)
-    ts(col(3), odd, 0.5, Op.mult, col(6), Op.add)
-    ts(A("cb"), A("cj"), 2.0, Op.subtract, 0.5, Op.mult)
-    act(A("cb"), A("cb"), Fn.Identity, col(3), 1.0)
-    act(col(4), odd, Fn.Identity, C - 1.0, 1.0)
-    act(col(12), col(4), Fn.Identity, 0.0, col(6))
-    act(col(5), odd, Fn.Identity, AT + 1.0, -1.0)
-    act(A("ck", 0, 4), A("cj", 0, 4), Fn.Identity, -0.5, 1.0)
-    act(A("ck", 4, 8), A("cj", 0, 4), Fn.Identity, A("cPf", 5, 6), 1.0)
-    act(A("ck", 8, 12), A("cj", 0, 4), Fn.Identity, float(H), 1.0)
-    ts(A("et", 3, 515, 4), A("cI", 0, 128), A("cPf", 0, 1), Op.is_equal)
-    quant(A("qu0"), A("su0"), A("ut"))
-    cp(word(A("qu")), ind(word(A("qu0")), A("oU")))
-    cp(A("su"), ind(A("su0"), A("oU")), "S")
-    act(A("cTK"), A("cI"), Fn.Identity, 0.0, 512.0 * UNIT)
-    act(A("cPn"), A("cI", 2, C + 2, 2), Fn.Identity, 0.0, UNIT)
-    act(A("cRev"), A("cI", 0, H + 2), Fn.Identity, float(H), -1.0)
-    act(A("cTY", 0, K), A("cI", 0, K), Fn.Identity, -1.0, -1.0)
-    fill(A("cTY", K, C + 16), 1.0)
-    E = lambda n, b: A(n, 128 * b, 128 * b + 128)
-    for b in range(4):
-        quant(E("qe", b), E("se", b), A("et", 3 - b, 515 - b))
-    quant(A("qv"), A("sv"), A("vt"))
-
-    total = [0]
+        call = issue(q, lambda: queue[q].dma_start(out[0], a[0]), [a], [out], 0.1, "d%d" % (dmas[0] - 1), 16, LOAD / 2, deps,
+                     behind=[] if last is None else [last - 1])
+        return issue("D", None, [], [out], us, None, lat=LOAD / 2, deps=[call], behind=[] if last is None else [last])
 
     def send(t, n, reads, hop):
         name, pieces = _parcels(T, t)[n]
@@ -397,27 +315,102 @@ def rank_program(g, core, T, topo):
                      more={"sent": total[0], name + str(t): came})
         return {"deps": [sent], "arrive": [(name + str(t), came)]}
 
+    def hbm(x):
+        return (x, [], 0, False)
+
+    def byte(o):
+        return (o[0].bitcast(dt.uint8),) + o[1:]
+
+    def word(o):
+        return (o[0].bitcast(dt.uint32),) + o[1:]
+
+    first = dma("Y", A("ut"), hbm(T.u[:]), 0.6)
+    first = dma("Y", A("xt0", 0, 2 * C), hbm(T.x[:, 0:2 * C]), 0.7, last=first)
+    first = dma("Y", A("xt0", 2 * C, 4 * C), hbm(T.x[:, 2 * C:4 * C]), 0.7, last=first)
+    dma("Y", byte(A("qw")), hbm(T.wc[:]), 1.5, [first])
+    dma("Y", A("sw"), hbm(T.ws[:]), 0.5, [first])
+    dma("Y", A("vt"), hbm(T.v[:]), 0.7, [first])
+    iota(A("cK"), [[16, 32]], 0, 0)
+    iota(A("cP", 0, 1), [[0, 1]], 0, 1)
+    iota(A("cJ"), [[0, NB + 1], [1, 16]], 0, 0)
+    iota(A("cI"), [[1, C + 16]], 0, 0)
+    iota(A("cRev"), [[-1, H + 2]], H, 0)
+    iota(A("cTY", 0, K), [[-1, K]], -1, 0)
+    iota(A("c01"), [[0, H], [1, 2]], 0, 0)
+    iota(A("EC", AT + C, WF), [[1, K]], 0, 0)
+    for o, v in ((A("ft"), 0.0), (A("et"), 0.0), (A("SW", C, C + 8), -BIG), (A("MN", 0, 16), 0.0), (A("cTY", K, C + 16), 1.0),
+                 (A("KEY", 0, 1), (C * 512 + C) * UNIT), (A("UP", 0, 1), 1.0), (A("DL", 0, 1), 1.0), (A("DL", C - 1, C), 0.0),
+                 (A("PN", K, K + 1), 0.0), (A("CK", 0, 1), -K - 1.0), (A("AN", 0, 1), 0.0), (A("JN", K, H), 0.0), (A("FS", 0, 1), 1.0)):
+        fill(o, v)
+    col = lambda i: A("cPf", i, i + 1)
+    cp(A("oU"), A("cK", 0, 8))
+    ts(A("cP", 1, 2), A("cP", 0, 1), 15, Op.bitwise_and)
+    ts(A("cP", 2, 3), A("cP", 0, 1), 1, Op.bitwise_and)
+    cp(A("cPf", 0, 3), A("cP", 0, 3))
+    r16, odd = col(1), col(2)
+    ts(A("cR"), A("cJ", 0, H), 0.5, Op.is_lt, 2 * FAR, Op.mult)
+    act(A("cRn"), A("cR"), Fn.Identity, 0.0, -1.0)
+    ts(A("mask"), A("cJ"), r16, Op.is_equal)
+    act(A("cM"), A("mask", 0, H), Fn.Identity, FAR, -2 * FAR)
+    act(A("cN", 1, C, 2), A("mask", 0, H), Fn.Identity, FAR, -2 * FAR)
+    act(A("cN", 0, C, 2), A("mask", 15, H + 15), Fn.Identity, FAR, -2 * FAR)
+    act(A("XN", C, C + 1), A("mask", 15, 16), Fn.Identity, FAR, -FAR - BIG)
+    ts(A("HM", 0, H), A("mask", 15, H + 15), -DROP / 1024.0, Op.mult)
+    ts(A("HS", 0, H), A("mask", 0, H), 1024.0, Op.mult)
+    for i in range(2):
+        scan(A("cH", H * i, H * i + H), A("HM", 0, H), A("HS", 0, H), 0.0, Op.mult, Op.add)
+    ts(A("cHn"), A("cH"), -1.0, Op.mult)
+    act(A("cC", 0, H, 2), A("cH", 0, H // 2), Fn.Identity, 0.0, 3.0 / DROP)
+    cp(A("cC", 1, H, 2), A("mask", 0, H // 2), "S")
+    act(col(6), A("mask", 15, 16), Fn.Identity, DROP, -DROP)
+    act(col(7), col(6), Fn.Identity, 0.0, 3.0 / DROP)
+    act(col(8), col(6), Fn.Identity, float(H), -1.0)
+    act(col(9), col(6), Fn.Identity, float(K), -1.0)
+    act(col(10), col(6), Fn.Identity, 0.0, -1.0)
+    act(col(11), col(6), Fn.Identity, (C - 1) * 512.0, -3.0 / DROP / UNIT)
+    ts(A("cj"), A("cK", 0, 20), r16, Op.add)
+    act(A("cm2"), A("cj", 0, NB), Fn.Identity, col(6), 2.0)
+    ts(col(3), odd, 0.5, Op.mult, col(6), Op.add)
+    ts(A("cb"), A("cj"), 2.0, Op.subtract, 0.5, Op.mult)
+    act(A("cb"), A("cb"), Fn.Identity, col(3), 1.0)
+    act(col(4), odd, Fn.Identity, C - 1.0, 1.0)
+    act(col(12), col(4), Fn.Identity, 0.0, col(6))
+    act(col(5), odd, Fn.Identity, AT + 1.0, -1.0)
+    act(A("ck", 0, 4), A("cj", 0, 4), Fn.Identity, -0.5, 1.0)
+    act(A("ck", 4, 8), A("cj", 0, 4), Fn.Identity, col(5), 1.0)
+    ts(A("et", 3, 515, 4), A("cI", 0, 128), col(0), Op.is_equal)
+    quant(A("qu0"), A("su0"), A("ut"))
+    cp(word(A("qu")), ind(word(A("qu0")), A("oU")))
+    cp(A("su"), ind(A("su0"), A("oU")), "S")
+    act(A("cTK"), A("cI"), Fn.Identity, 0.0, 512.0 * UNIT)
+    act(A("cPn"), A("cI", 2, C + 2, 2), Fn.Identity, 0.0, UNIT)
+    E = lambda n, b: A(n, 128 * b, 128 * b + 128)
+    for b in range(4):
+        quant(E("qe", b), E("se", b), A("et", 3 - b, 515 - b))
+    quant(A("qv"), A("sv"), A("vt"))
+
     banksH = ["pH0", "pH1", "pH2", "pS"]
+    halves = ((0, H), (H, C))
     M = lambda a, b: A("MN", 16 + a, 16 + b)
     end = lambda name, c, n=1: A(name, 16 * c + 15, 16 * (c + n), 16)
+    row = lambda name, c: A(name, H * c, H * c + H)
     sc = lambda i: A("SC", i, i + 1)
     sm = lambda i: A("SM", NB * i, NB * i + NB)
-    lane = lambda name, b, n: A(name, b, 4 * n, 4)
     part = lambda c: C * (2 * c // NB)
     CK = A("CK", 1, H + 1)
 
     for t in range(R):
-        qx, sxp, lc, ls, nv = "qx%d" % t, "sx%d" % t, "lc%d" % t, "ls%d" % t, NV[t]
-        oA = "oA%d" % t
+        qx, sxp, lc, ls, oA = "qx%d" % t, "sx%d" % t, "lc%d" % t, "ls%d" % t, "oA%d" % t
+        nr, nv, ne = NRS[t], NV[t], NES[t]
         oN, oQ, oG, oP, oB, oL, oL2, oE = [A(oA, NB * i, NB * i + (NB if i < 7 else 4)) for i in range(8)]
-        for a, b in ((0, H), (H, C)) if t == 0 else ((0, C),):
+        for a, b in halves if t == 0 else ((0, C),):
             quant(A(qx, a, b), A(sxp, a, b), A("xt%d" % t, 4 * a, 4 * b))
         got = [send(t, 0, [A(qx)], BULK), send(t, 1, [A(sxp)], HOP)]
         both = {k: got[0][k] + got[1][k] for k in got[0]}
-        for bank in ("pS", "pH0"):
-            mm(A(bank, 0, C), A("qu"), A("su"), A(qx, 0, C), A(sxp, 0, C))
+        for bank in ("pH0", "pS"):
+            mm(A(bank, 0, C), A("qu"), A("su"), A(qx), A(sxp))
         for b in range(4):
-            mm(A("pT%d" % b, 0, C), E("qe", b), E("se", b), A(qx, 0, C), A(sxp, 0, C))
+            mm(A("pT%d" % b, 0, C), E("qe", b), E("se", b), A(qx), A(sxp))
         for b in range(2):
             cp(A("TF", C * b, C * b + C), A("pT%d" % (2 + b), 0, C), "S")
         for b, bank in enumerate(("pH1", "pH2", "pT2", "pT3")):
@@ -428,9 +421,12 @@ def rank_program(g, core, T, topo):
         cp(A("SW", 1, C, 2), A("pH0", 1, C, 2), "S")
         tt(M(H, C), A("pS", 1, C, 2), A("SW", 2, C + 1, 2), Op.min)
         tt(M(0, H), A("pS", 1, C, 2), A("SW", 0, C, 2), Op.max)
-        scan(A("XN", 0, C), A("pS", 0, C), A("cN"), FAR, Op.min, Op.max)
-        carry(A("DT", H, C), A("XN", 2, C + 1, 2))
-        deal(A("DT", 0, H), A("X1"), M(0, H))
+        for a, b in halves:
+            n = min(b + 1, C)
+            scan(A("XN", a + 1, n), A("pS", a + 1, n), A("cN", 1, n - a), FAR, Op.min, Op.max)
+            carry(A("DT", H + a // 2, H + b // 2), A("XN", a + 2, b + 1, 2))
+        scan(A("X1"), M(0, H), A("cM"), FAR, Op.min, Op.max)
+        carry(A("DT", 0, H), A("X1"))
         tt(A("UP", 1, C, 2), A("pS", 1, C, 2), A("SW", 0, C, 2), Op.is_gt)
         tt(A("UP", 2, C + 1, 2), A("pS", 1, C, 2), A("SW", 2, C + 1, 2), Op.is_lt)
         act(A("US"), A("UP", 2, C + 1, 2), Fn.Identity, 0.0, -UNIT)
@@ -442,32 +438,36 @@ def rank_program(g, core, T, topo):
         tt(A("DL", 2, C, 2), A("pS", 1, C - 1, 2), M(1, H), Op.is_lt)
         hold(A("D4"), A("DL"))
         tt(A("HT"), end("D4", 0, 20), A("cb"), Op.add)
+        cp(A("oS"), A("HT"))
         tt(A("PN", 0, K), A("UP", 0, K), A("UP", 1, K + 1), Op.is_le)
         cumsum(A("PN", K + 1, 2 * K + 1), A("PN", 0, K))
         hold(A("D7"), A("PN", 0, 2 * K))
         act(A("PF", 0, 4), end("D7", 0, 4), Fn.Identity, col(12), col(4))
         tt(A("PF", 4, 8), A("PF", 0, 4), A("ck", 4, 8), Op.add)
-        for c in range(NR, NB):
-            act(A("JK", H * c, H * c + H), M(H, C), Fn.Sign, end("DT", NB + c), -1.0, A("ACC", c, c + 1))
-        ts(A(oA, NR, NB), A("ACC", NR, NB), -1.0, Op.mult, float(H), Op.add)
-        for c in range(NR):
-            ts(A("JK", H * c, H * c + H), M(H, C), end("DT", NB + c), Op.is_lt)
-            ts(A("JK2", H * c, H * c + H), M(H, C), end("DT", NB + c), Op.is_le)
-            scan(A("CS", H * c, H * c + H), A("JK", H * c, H * c + H), A("JK2", H * c, H * c + H), -float(H), Op.add, Op.add)
-        if NR:
-            ts(A(oA, 0, NR), A("CS", H - 1, NR * H, H), -1.0, Op.mult, float(H), Op.add)
+        for c in range(nr, NB):
+            act(row("JK", c), M(H, C), Fn.Sign, end("DT", NB + c), -1.0, A("ACC", c, c + 1))
+        ts(A(oA, nr, NB), A("ACC", nr, NB), -1.0, Op.mult, float(H), Op.add)
+        for c in range(nr):
+            ts(row("JK", c), M(H, C), end("DT", NB + c), Op.is_lt)
+            ts(row("JK2", c), M(H, C), end("DT", NB + c), Op.is_le)
+            scan(row("CS", c), row("JK", c), row("JK2", c), -float(H), Op.add, Op.add)
+        if nr:
+            ts(A(oA, 0, nr), A("CS", H - 1, nr * H, H), -1.0, Op.mult, float(H), Op.add)
         tt(A("KEY", 1, H + 1), ind(A("cTK"), oN), A("POS"), Op.add)
         act(A("KEYN", 1, H + 1), A("KEY", 1, H + 1), Fn.Identity, -1.0, 1.0)
         for c in range(NB):
             act(A("KB", ROW * c, ROW * c + H + 2), M(-1, H + 1), Fn.Sign, end("DT", c), -1.0)
         for c in range(NB):
             d = NB - 1 - c
-            scan(A("LR", part(d) + 1, part(d) + 32 * d + 32, 2), A("KB", ROW * d, ROW * d + 16 * d + 16), A("KEY", 0, 16 * d + 16), 0.0, Op.mult, Op.max)
-            scan(rev("LR", part(c) + 32 * c, part(c) + C, 2), rev("KB", ROW * c + 16 * c + 2, ROW * c + H + 2), rev("KEYN", 16 * c + 1, H + 1), -1.0, Op.min, Op.max)
+            scan(A("LR", part(d) + 1, part(d) + 32 * d + 32, 2), A("KB", ROW * d, ROW * d + 16 * d + 16), A("KEY", 0, 16 * d + 16),
+                 0.0, Op.mult, Op.max)
+            scan(rev("LR", part(c) + 32 * c, part(c) + C, 2), rev("KB", ROW * c + 16 * c + 2, ROW * c + H + 2), rev("KEYN", 16 * c + 1, H + 1),
+                 -1.0, Op.min, Op.max)
         for d in reversed(range(NB)):
-            scan(A("LL", part(d) // 2, part(d) // 2 + 16 * d + 16), A("KB", ROW * d, ROW * d + 16 * d + 16), A("cRev", 0, 16 * d + 16), 0.0, Op.mult, Op.max)
+            scan(A("LL", part(d) // 2, part(d) // 2 + 16 * d + 16), A("KB", ROW * d, ROW * d + 16 * d + 16), A("cRev", 0, 16 * d + 16),
+                 0.0, Op.mult, Op.max)
         for i in range(2):
-            scan(A("DS", H * i, H * i + H), A("cC", 0, H), A("LR", (C + H) * i, (C + H) * i + H), 0.0, Op.add, Op.min)
+            scan(A("DS", H * i, H * i + H), A("cC"), A("LR", (C + H) * i, (C + H) * i + H), 0.0, Op.add, Op.min)
         ts(A("I1", 0, NB), A("DS", 31, C, 32), col(7), Op.add, 1.0 / UNIT, Op.mult)
         ts(A("I1", NB, 2 * NB), A("I1", 0, NB), 511, Op.bitwise_and)
         q = A("I1", NB, 2 * NB)
@@ -479,29 +479,27 @@ def rank_program(g, core, T, topo):
         tt(sm(4), sm(3), sm(0), Op.max)
         tt(sm(5), sm(4), q, Op.min)
         cp(oB, sm(5))
-        gotp, got = send(t, 2, [oP], HOP), send(t, 3, [oB], HOP)
-        oP, oB = A("lp%d" % t), A("lq%d" % t)
+        gotp, gotq = send(t, 2, [oP], HOP), send(t, 3, [oB], HOP)
         for b in range(4):
-            cp(A("TMP", C * b, C * b + C, 2), ind(A("TH", C * b, C * b + C), oP), "S", **gotp)
-            if b < NFA:
-                tt(A("FA", WF * b + AT + 1, WF * b + AT + C, 2), ind(A("TH", C * b, C * b + C), oB), A("TMP", C * b, C * b + C, 2), Op.add, **got)
+            pick = lambda name: ind(A("TH", C * b, C * b + C), A(name % t))
+            cp(A("TMP", C * b, C * b + C, 2), pick("lp%d"), "S", **gotp)
+            if b < NFAS[t]:
+                tt(A("FA", WF * b + AT + 1, WF * b + AT + C, 2), pick("lq%d"), A("TMP", C * b, C * b + C, 2), Op.add, **gotq)
             else:
-                cp(A("TMP", C * b + 1, C * b + C, 2), ind(A("TH", C * b, C * b + C), oB), "S", **got)
+                cp(A("TMP", C * b + 1, C * b + C, 2), pick("lq%d"), "S", **gotq)
                 scan(A("FA", WF * b + AT, WF * b + AT + C), A("c01"), A("TMP", C * b, C * b + C), 0.0, Op.mult, Op.add)
         tt(A("NG"), ind(A("SW"), oQ), M(0, H), Op.subtract)
         tt(A("X3"), ind(A("SW"), oQ), A("X1"), Op.subtract)
         scan(A("DP"), A("cRn"), A("X3"), 0.0, Op.add, Op.max)
         for c in range(nv, NB):
-            act(A("JK", H * c, H * c + H), A("NG"), Fn.Sign, end("DP", c), -1.0)
-            act(A("JK2", H * c, H * c + H), A("JK", H * c, H * c + H), Fn.Relu, A("SM", 2 * NB + c, 2 * NB + c + 1), 1.0, A("ACC", 10 + c, 11 + c))
+            act(row("JK", c), A("NG"), Fn.Sign, end("DP", c), -1.0)
+            act(row("JK2", c), row("JK", c), Fn.Relu, A("SM", 2 * NB + c, 2 * NB + c + 1), 1.0, A("ACC", NB + c, NB + c + 1))
         for c in range(nv):
-            ts(A("JK", H * c, H * c + H), A("NG"), end("DP", c), Op.is_lt)
-            cumsum(A("CS", H * c, H * c + H), A("JK", H * c, H * c + H), A("SM", 2 * NB + c, 2 * NB + c + 1))
-        if nv:
-            cp(A(oA, 20, 20 + nv), A("CS", H - 1, nv * H, H))
-        if nv < NB:
-            ts(A(oA, 20 + nv, 30), A("ACC", 10 + nv, 20), float(C), Op.min)
-        cp(A("Y"), ind(A("cTY"), oG), Y_ON)
+            ts(row("JK", c), A("NG"), end("DP", c), Op.is_lt)
+            cumsum(row("CS", c), row("JK", c), A("SM", 2 * NB + c, 2 * NB + c + 1))
+        cp(A(oA, 2 * NB, 2 * NB + nv), A("CS", H - 1, nv * H, H))
+        ts(A(oA, 2 * NB + nv, 3 * NB), A("ACC", NB + nv, 2 * NB), float(C), Op.min)
+        cp(A("Y"), ind(A("cTY"), oG), "S")
         scan(A("MU"), A("Y"), A("Y"), 0.0, Op.min, Op.min)
         mu = A("MU", H - 1, H)
         act(A("OUT"), A("Y"), Fn.Relu, 0.0, 1.0, sc(0))
@@ -510,29 +508,26 @@ def rank_program(g, core, T, topo):
         scan(A("UU"), A("LT"), A("OUT"), mu, Op.add, Op.subtract)
         scan(CK, A("LE"), A("UU"), -K - 1.0, Op.add, Op.min)
         act(sc(1), sc(0), Fn.Relu, float(K - H), 1.0)
+        act(sc(2), sc(1), Fn.Identity, col(9), 1.0)
         act(sc(3), sc(1), Fn.Identity, -float(K), -1.0)
         act(sc(4), sc(1), Fn.Identity, col(10), 1.0)
         act(A("PF", 8, 12), A("ck", 0, 4), Fn.Identity, sc(3), 1.0)
         act(A("PF", 12, 16), end("D7", 4, 4), Fn.Sign, sc(4), -1.0)
         tt(A("PF", 16, 20), A("PF", 12, 16), A("PF", 4, 8), Op.mult)
-        tt(A("PF", 20, 24), A("PF", 12, 16), A("ck", 8, 12), Op.mult)
-        tt(A("HT", 0, 4), A("HT", 0, 4), A("PF", 20, 24), Op.max)
-        cp(A("oS"), A("HT"))
-        act(sc(2), sc(1), Fn.Identity, col(9), 1.0)
-        act(A("LAB", H, H + K), A("cI", 0, K), Fn.Identity, sc(3), 1.0)
+        act(A("JN", 0, K), A("cI", 0, K), Fn.Identity, sc(3), 1.0)
         for c in range(4):
             bias = A("PF", 8 + c, 9 + c)
-            if c < NE:
-                ts(A("JK", H * c, H * c + H), CK, bias, Op.is_lt, 2.0, Op.mult)
-                cumsum(A("CS", H * c, H * c + H), A("JK", H * c, H * c + H))
-                got = A("CS", H * c + H - 1, H * c + H)
+            if c < ne:
+                ts(row("JK", c), CK, bias, Op.is_lt, 2.0, Op.mult)
+                cumsum(row("CS", c), row("JK", c))
+                twice = A("CS", H * c + H - 1, H * c + H)
             else:
-                got = A("ACC", 20 + c, 21 + c)
-                act(A("JK2", H * c, H * c + H), CK, Fn.Sign, bias, -1.0, got)
-            ts(A(oA, 70 + c, 71 + c), got, float(AT + 1 if c < NE else H + AT + 1), Op.add, A("PF", 16 + c, 17 + c), Op.max)
+                twice = A("ACC", 2 * NB + c, 2 * NB + c + 1)
+                act(row("JK2", c), CK, Fn.Sign, bias, -1.0, twice)
+            ts(A(oA, 7 * NB + c, 7 * NB + c + 1), twice, float(AT + 1 if c < ne else H + AT + 1), Op.add, A("PF", 16 + c, 17 + c), Op.max)
         got = send(t, 4, [oE], HOP)
         for b in range(4):
-            cp(lane("ft", b, K), ind(A("FA", WF * b, WF * b + WF), A("lk%d" % t)), "V" if b < NF else "S", **got)
+            cp(A("ft", b, 4 * K, 4), ind(A("FA", WF * b, WF * b + WF), A("lk%d" % t)), "V" if b < NFS[t] else "S", **got)
         quant(A("qf"), A("sf"), A("ft"))
         for i in range(2):
             hold(A("D6", H // 2 * i, H // 2 * (i + 1)), A("LL", 3 * H // 2 * i, 3 * H // 2 * i + H // 2))
@@ -543,52 +538,51 @@ def rank_program(g, core, T, topo):
         cp(A(oA, 5 * NB, 7 * NB), A("SM", 6 * NB, 8 * NB))
         scan(A("CK2"), A("LE"), A("UU"), -K - 1.0, Op.add, Op.min)
         tt(A("NM"), ind(A("CK"), oL), A("CK2"), Op.is_ge)
-        tt(A("NA"), ind(A("CK"), oL2), A("CK2"), Op.is_ge)
-        scan(A("FS", 1, H + 1), A("NM"), A("KEY", 1, H + 1), 4.0, Op.mult, Op.max)
-        scan(rev("BS", 0, H), rev("KEY", 1, H + 1), rev("NM", 0, H), 0.0, Op.max, Op.mult)
+        act(A("N1"), ind(A("CK"), oL2), Fn.Identity, -128.0, 1.0)
+        act(A("N2"), CK, Fn.Identity, -129.0, 1.0)
+        scan(A("N3"), A("N1"), A("N2"), 0.0, Op.min, Op.subtract)
+        act(A("NA"), A("N3"), Fn.Relu, 0.0, 128.0)
+        act(A("AN", 1, H + 1), A("N3"), Fn.Identity, 1.0, -1.0)
+        scan(A("FS", 1, H + 1), A("NM"), A("KEY", 1, H + 1), 1.0, Op.min, Op.max)
+        scan(rev("BS", 0, H), rev("KEY", 1, H + 1), rev("NM", 0, H), 0.0, Op.max, Op.min)
         tt(A("SD"), A("FS", 0, H), A("BS"), Op.is_gt)
         act(A("NS"), A("SD"), Fn.Identity, 1.0, -1.0)
-        act(A("AN", 1, H + 1), A("NA"), Fn.Identity, 1.0, -1.0)
         scan(A("KP"), CK, A("CK", 0, H), 0.0, Op.min, Op.subtract)
-        act(A("W0"), A("NA"), Fn.Identity, -384.0, 128.0)
-        act(A("W1"), A("KP"), Fn.Identity, 256.0, 128.0)
-        scan(A("LP"), A("W0"), A("W1"), 0.0, Op.min, Op.add)
+        act(A("W1"), A("KP"), Fn.Identity, 128.0, 128.0)
+        scan(A("LP"), A("NA"), A("W1"), 256.0, Op.min, Op.add)
+        scan(A("XP"), A("N1"), A("LP"), 0.0, Op.min, Op.add)
         scan(A("GO"), A("SD"), A("NA"), 0.0, Op.max, Op.min)
         scan(A("HO"), A("AN", 0, H), A("NS"), 0.0, Op.max, Op.min)
-        scan(rev("LB", 1, H + 1), rev("CK", 1, H + 1), rev("GO", 0, H), 0.0, Op.min, Op.add)
-        tt(A("XP"), ind(A("LB"), oL2), A("LP"), Op.max)
+        scan(rev("LB", 0, H), rev("CK", 1, H + 1), rev("GO", 0, H), 0.0, Op.min, Op.add)
         scan(rev("Z", 0, H), rev("GO", 0, H), rev("XP", 0, H), 0.0, Op.mult, Op.min)
         scan(A("O"), A("HO"), A("Z"), 0.0, Op.mult, Op.min)
-        scan(A("LAB", 0, H), A("LB", 1, H + 1), A("O"), -200.0, Op.max, Op.min)
-        if HS_ON[t] in "SV":
-            cp(A("HM"), ind(A("LAB"), A("oS")), HS_ON[t])
-        else:
-            cp(A("HM", 0, H), ind(A("LAB"), A("oS", 0, NB)), "S")
-            cp(A("HM", H, C), ind(A("LAB"), A("oS", NB, 2 * NB)), "V")
+        scan(A("LAB"), A("LB"), A("O"), -200.0, Op.max, Op.min)
+        tt(A("HM", 0, HV[t]), ind(A("LAB"), A("oS", 0, HV[t] // 16)), A("JN", 0, HV[t]), Op.min)
+        cp(A("HM", HV[t], C), ind(A("LAB"), A("oS", HV[t] // 16, 2 * NB)), "S")
         scan(A("HS"), A("cHn"), A("HM"), 0.0, Op.add, Op.max)
         ts(A("oH"), end("HS", 0, 20), sc(2), Op.add)
         xn = "xt%d" % (t + 1)
         for b in (2, 3, 0, 1):
             mm(A(banksH[b], 0, 128), E("qw", b), E("sw", b), A("qf"), A("sf"))
             act(A("HR", K * b, K * b + K), A(banksH[b], 0, K), Fn.Relu, 0.0, 0.03125)
-        for b in range(2):
-            act(A("GG", C * b, C * b + C), ind(A("HR", K * b, K * b + K), A("oH")), Fn.Copy)
-            tt(lane(xn, b, C), A("pT%d" % b, 0, C), A("GG", C * b, C * b + C), Op.add)
-        for b in range(2, 4):
-            tt(lane(xn, b, C), ind(A("HR", K * b, K * b + K), A("oH")), A("TF", C * (b - 2), C * (b - 1)), Op.add)
+        for lo, hi in ((0, C),) if t < R - 1 else halves:
+            pick = lambda b: ind(A("HR", K * b, K * b + K), A("oH", lo // 16, hi // 16))
+            for b in range(2):
+                cp(A("GG", C * b + lo, C * b + hi), pick(b), "S")
+                tt(A(xn, 4 * lo + b, 4 * hi, 4), A("pT%d" % b, lo, hi), A("GG", C * b + lo, C * b + hi), Op.add)
+            for b in range(2, 4):
+                tt(A(xn, 4 * lo + b, 4 * hi, 4), pick(b), A("TF", C * (b - 2) + lo, C * (b - 2) + hi), Op.add)
 
     scan(A("EC", AT + 1, AT + C, 2), A("cI", 0, C, 2), A("UP", 1, C, 2), 0.0, Op.max, Op.add)
-    act(A("ER"), ind(A("EC"), oE), Fn.Copy)
-    act(A("OLR"), ind(A("ER"), A("oH")), Fn.Copy)
-    dma("Y", hbm(T.ol[:]), (T.OLR[0:128:16, :], A("OLR")[1]), 0.0)
-    quant(A("qx2"), A("sx2"), A("xt2"))
-    mm(A("pH0", 0, H), A("qv"), A("sv"), A("qx2", 0, H), A("sx2", 0, H))
-    mm(A("pH1", 0, H), A("qv"), A("sv"), A("qx2", H, C), A("sx2", H, C))
-    dma("Y", hbm(T.oc[:]), byte(A("qx2")), 0.9)
+    cp(A("ER"), ind(A("EC"), oE), "S")
+    cp(A("OLR"), ind(A("ER"), A("oH")), "S")
+    dma("Y", hbm(T.ol[:]), (T.OLR[0:128:16, :], A("OLR")[1]), 0.05)
+    for (lo, hi), bank, q in zip(halves, ("pH0", "pH1"), "SV"):
+        quant(A("qx2", lo, hi), A("sx2", lo, hi), A("xt2", 4 * lo, 4 * hi))
+        mm(A(bank, 0, H), A("qv"), A("sv"), A("qx2", lo, hi), A("sx2", lo, hi))
+        dma("Y", hbm(T.oc[:, 4 * lo:4 * hi]), byte(A("qx2", lo, hi)), 0.6)
+        cp(A("YO", lo, hi), A(bank, 0, H), q)
+        dma("Y" if lo else "S", hbm(T.y[:, lo:hi]), A("YO", lo, hi), 0.6)
     for k in range(4):
-        dma("YS"[k % 2], hbm(T.osc[4 * k:4 * k + 4, :]), (T.sx2[32 * k:32 * k + 4, :], A("sx2")[1]), 0.0)
-    cp(A("YO", 0, H), A("pH0", 0, H))
-    act(A("YO", H, C), A("pH1", 0, H), Fn.Copy)
-    dma("Y", hbm(T.y[:, 0:H]), A("YO", 0, H), 0.5)
-    dma("S", hbm(T.y[:, H:C]), A("YO", H, C), 0.5)
+        dma("S", hbm(T.osc[4 * k:4 * k + 4, :]), (T.sx2[32 * k:32 * k + 4, :], A("sx2")[1]), 0.05)
     _emit(ops, queue, T)

from concourse.bass import DstId, RemoteDMATransfer
from concourse.mybir import dt, AluOpType, ActivationFunctionType

C, K, R = 320, 64, 2
STEP = [1, 2]
H = C // 2
NB = H // 16
ROW = H + 16
BIG = 2.0 ** 96
FAR = 2.0 ** 98
DROP = 192.0
UNIT = 2.0 ** -18
AT, WF = 48, 432
NRS = [1, 1]
NV = [6, 6]
NES = [0, 1]
NFAS = [0, 2]
NFS = [2, 2]
HV = [H, K]
BULK, HOP, WAKE, LOAD, CASES = 3.2, 1.7, 0.19, 1.0, ((0.17, 1.4),)
TRIES, MOVES, SIZE, HEAT = 8000, 5, 350.0, 0.15
F32, BF, I32, U16, CODE, PLANE = "float32", "bfloat16", "int32", "uint16", "float8_e4m3fn_x4", "uint8"

_SB = {
    "xt0": (4 * C, BF), "xt1": (4 * C, BF), "xt2": (4 * C, BF), "ut": (512, BF), "vt": (512, BF), "et": (516, BF), "ft": (512, BF),
    "qu0": (128, CODE), "su0": (128, PLANE), "qu": (128, CODE), "su": (128, PLANE), "qv": (128, CODE), "sv": (128, PLANE),
    "qw": (512, CODE), "sw": (512, PLANE), "qe": (512, CODE), "se": (512, PLANE), "qf": (128, CODE), "sf": (128, PLANE),
    "qx0": (C, CODE), "sx0": (C, PLANE), "qx1": (C, CODE), "sx1": (C, PLANE), "qx2": (C, CODE), "sx2": (C, PLANE),
    "lc0": (C, CODE), "ls0": (C, PLANE), "lc1": (C, CODE), "ls1": (C, PLANE), "rc": (C, CODE), "rs": (C, PLANE),
    "lp0": (NB, U16), "lp1": (NB, U16), "rp": (NB, U16), "lq0": (NB, U16), "lq1": (NB, U16), "rq": (NB, U16),
    "lk0": (4, U16), "lk1": (4, U16), "rk": (4, U16),
    "cI": (C + 16, F32), "cJ": (H + 16, BF), "cP": (8, I32), "cPf": (16, F32), "cK": (32, F32), "cTK": (C + 16, F32),
    "cRev": (H + 2, BF), "cTY": (C + 16, BF), "mask": (H + 16, BF), "cM": (H, BF), "cR": (H, BF), "cRn": (H, BF), "cC": (H, BF),
    "cN": (C, BF), "cH": (C, BF), "cHn": (C, BF), "c01": (C, BF),
    "cPn": (H, F32), "cj": (20, F32), "cm2": (NB, F32), "cb": (20, F32), "ck": (8, F32),
    "oU": (8, U16), "oA0": (80, U16), "oA1": (80, U16), "oH": (20, U16), "oS": (20, U16),
    "SW": (C + 8, F32), "KB": (NB * ROW, BF), "JK": (NB * H, BF), "JK2": (NB * H, BF), "CS": (NB * H, BF),
    "ACC": (32, F32), "I1": (20, I32), "SC": (16, F32), "LAB": (H, BF), "FA": (4 * WF, BF), "EC": (WF, F32),
    "TH": (4 * C, BF), "TF": (2 * C, BF), "TMP": (4 * C, BF), "HR": (4 * K, F32), "GG": (2 * C, F32),
    "ER": (K, F32), "OLR": (C, F32), "YO": (C, F32),
}
_ROWS = {
    "rf": (F32, {"MN": C + 32, "X1": H, "XN": C + 2, "DT": C, "US": H, "POS": H, "KEY": H + 2, "KEYN": H + 2, "LR": 2 * C, "DS": C,
                 "NG": H, "X3": H, "DP": H, "SM": 120, "FS": H + 2, "BS": H, "HT": 20, "PF": 20}),
    "rb": (BF, {"UP": C + 2, "DL": C, "D4": C, "D5": H, "LL": C, "D6": H, "PN": 2 * K + 2, "D7": 2 * K, "Y": H, "MU": H, "OUT": H, "LE": H,
                "LT": H, "UU": H, "CK": H + 2, "CK2": H, "NM": H, "NA": H, "N1": H, "N2": H, "N3": H, "AN": H + 2, "KP": H, "LP": H,
                "W1": H, "SD": H, "NS": H, "GO": H, "HO": H, "LB": H, "XP": H, "Z": H, "O": H, "JN": H, "HM": C, "HS": C}),
}
_AT = {}
for _b, (_d, _rows) in _ROWS.items():
    _o = 0
    for _n, _w in _rows.items():
        _AT[_n] = (_b, _o, _w)
        _o += (_w + 15) // 16 * 16
    _SB[_b] = (_o, _d)
SCRATCH = {n: ("sbuf", [128, w], d) for n, (w, d) in _SB.items()}
for _n in ("pS", "pT0", "pT1", "pT2", "pT3", "pH0", "pH1", "pH2"):
    SCRATCH[_n] = ("psum", [128, 512], F32)
NDMA = 16
SEMAPHORES = (["sV", "sS", "sT", "sG", "sent", "rout"] + ["in" + n for n in "cspqe"] + [n + t for n in "cspqe" for t in "01"]
              + ["d%d" % i for i in range(NDMA)])
_ORDERS = {}


def _relays(T, topo, src, dst):
    return [c for c in topo.cores_of(src) if T.rank_of(c) is None and topo.die(c) == topo.die(src) and topo.may_write(c, dst)][:2]


def _bits(engines):
    return sum(1 << e for e in engines)


def _parcels(T, t):
    codes = lambda n, i: T[n][:, H * i:H * i + H].bitcast(dt.uint8)
    lists = T["oA%d" % t]
    return [("c", [(codes("qx%d" % t, i), codes("rc", i), codes("lc%d" % t, i), i) for i in range(2)]),
            ("s", [(T["sx%d" % t][:], T.rs[:], T["ls%d" % t][:], 0)]),
            ("p", [(lists[:, 3 * NB:4 * NB], T.rp[:], T["lp%d" % t][:], 1)]),
            ("q", [(lists[:, 4 * NB:5 * NB], T.rq[:], T["lq%d" % t][:], 1)]),
            ("e", [(lists[:, 7 * NB:7 * NB + 4], T.rk[:], T["lk%d" % t][:], 0)])]


def _relay_program(g, core, T, topo):
    for r, src in enumerate(T.cores):
        for t in range(R):
            dst = T.cores[r ^ STEP[t]]
            if topo.may_write(src, dst) or core not in _relays(T, topo, src, dst):
                continue
            rid, pid = topo.addr(dst, core)
            calls = 0
            for name, pieces in _parcels(T, t):
                for _, mid, land, i in pieces:
                    if _relays(T, topo, src, dst)[i] == core:
                        g.wait_ge(T.sem["in" + name], len(topo.engines(src, core)) // len(pieces))
                        g.remote_dma(land, mid, T.sem[name + str(t)], T.sem.rout, pid, rid, topo.mask(core, dst))
                        calls += 1
            g.wait_ge(T.sem.rout, calls * len(topo.engines(core, dst)))


def _fit(ops, before, after, rank, back):
    left, ready, start, end = [len(b) for b in before], [0.0] * len(ops), [0.0] * len(ops), 0.0
    free, taken = sorted((rank[i], i) for i in range(len(ops)) if not left[i]), {}
    while free:
        i = free.pop(0)[1]
        cost, lat, line = ops[i]["cost"], ops[i]["lat"], taken.setdefault(ops[i]["q"], [])
        t, lo, hi = ready[i] + (lat if back else 0.0), 0, len(line)
        while lo < hi:
            mid = (lo + hi) // 2
            lo, hi = (mid + 1, hi) if line[mid][1] <= t else (lo, mid)
        while lo < len(line) and line[lo][0] < t + cost - 1e-9:
            t, lo = line[lo][1], lo + 1
        line.insert(lo, (t, t + cost))
        start[i], done = t, t + cost + (0.0 if back else lat)
        end = max(end, done)
        for j in after[i]:
            waits = ops[max(i, j)]["deps"][min(i, j)]
            ready[j] = max(ready[j], done + WAKE if waits else t + cost - (ops[j]["lat"] if back else 0.0))
            left[j] -= 1
            if not left[j]:
                free.append((rank[j], j))
        free.sort()
    return end, start


def _replay(ops, order, wake, late):
    now, done = {}, [0.0] * len(ops)
    for i in order:
        o = ops[i]
        now[o["q"]] = max([now.get(o["q"], 0.0)] + [done[d] + wake for d, waits in o["deps"].items() if waits]) + o["cost"]
        done[i] = now[o["q"]] + o["lat"] * (late if o["q"] == "G" else 1.0)
    return max(done)


def _order(ops):
    key = tuple((o["q"], o["cost"], o["lat"]) for o in ops)
    if key not in _ORDERS:
        n = len(ops)
        before, after = [list(o["deps"]) for o in ops], [[] for o in ops]
        for i in range(n):
            for d in before[i]:
                after[d].append(i)
        best, here, seed, rank = None, None, 1, [-float(i) for i in range(n)]
        for turn in range(TRIES):
            late = _fit(ops, after, before, rank, True)[1]
            end, start = _fit(ops, before, after, [-late[i] - ops[i]["cost"] for i in range(n)], False)
            order = sorted(range(n), key=lambda i: start[i])
            worth = end + sum(_replay(ops, order, *case) for case in CASES)
            if best is None or worth <= best[0]:
                best = (worth, order)
            if here is None or worth <= here[0] + HEAT * (1 - turn / TRIES) * (seed >> 40) / 2 ** 24:
                here = (worth, start)
            rank = [-here[1][i] - ops[i]["cost"] for i in range(n)]
            for m in range(MOVES):
                seed = (seed * 6364136223846793005 + 1442695040888963407) % 2 ** 64
                rank[(seed >> 33) % n] += ((seed >> 20) % 1001 - 500) / SIZE
        _ORDERS[key] = best[1]
    return _ORDERS[key]


def _emit(ops, queue, T):
    count, known, clocks, mark = {}, {q: {} for q in queue}, {}, {}

    def need(q, sem, n):
        if known[q].get(sem, 0) < n:
            queue[q].wait_ge(T.sem[sem], n)
            for s, v in clocks.get((sem, n), {sem: n}).items():
                known[q][s] = max(known[q].get(s, 0), v)

    for i in _order(ops):
        o = ops[i]
        if o["fn"] is None:
            mark[i] = mark[i - 1]
            continue
        deps = {}
        for d, waits in o["deps"].items():
            if mark[d] and waits:
                deps[mark[d][0]] = max(deps.get(mark[d][0], 0), mark[d][1])
        for s, n in sorted(deps.items(), key=lambda e: -len(clocks.get(e, {}))):
            need(o["q"], s, n)
        for s, n in o["arrive"]:
            need(o["q"], s, n)
        call = o["fn"]()
        mark[i] = None
        if o["sem"]:
            count[o["sem"]] = count.get(o["sem"], 0) + o["inc"]
            call.then_inc(T.sem[o["sem"]], o["inc"])
            mark[i] = (o["sem"], count[o["sem"]])
            clocks[mark[i]] = dict(known[o["q"]], **{o["sem"]: count[o["sem"]]})
        for s, n in o["more"].items():
            count[s] = max(count.get(s, 0), n)
    for s, n in count.items():
        need("G", s, n)


def rank_program(g, core, T, topo):
    rank = T.rank_of(core)
    if rank is None:
        _relay_program(g, core, T, topo)
        return
    Op, Fn = AluOpType, ActivationFunctionType
    queue = {"V": g.vector, "S": g.scalar, "T": g.tensor, "G": g, "Y": g.sync}
    ops, hist, dmas, total = [], {}, [0], [0]

    def place(name, a, b):
        buf, o, w = _AT.get(name, (name, 0, None))
        w = T[buf].shape[1] if w is None else w
        return buf, o + a, o + (w if b is None else b)

    def A(name, a=0, b=None, s=1):
        buf, a, b = place(name, a, b)
        return (T[buf][:, a:b:s] if s != 1 else T[buf][:, a:b], [(buf, a, b, s)], len(range(a, b, s)), False)

    def rev(name, a, b, s=1):
        buf, a, b = place(name, a, b)
        last = range(a, b, s)[-1]
        return (T[buf][:, last:(a - 1 if a else None):-s], [(buf, a, b, s)], len(range(a, b, s)), False)

    def ind(win, off):
        return (win[0].indirect(off[0]), win[1] + off[1], 16 * off[2], True)

    def meet(x, y):
        return x[1] < y[2] and y[1] < x[2] and (x[3] != y[3] or (x[1] - y[1]) % x[3] == 0)

    def issue(q, fn, reads, writes, cost, sem="", inc=1, lat=0.0, deps=(), arrive=(), more=(), behind=()):
        acc = [(x, False) for o in reads if isinstance(o, tuple) for x in o[1]] + [(x, True) for o in writes for x in o[1]]
        deps = dict([(d, False) for d in behind] + [(d, True) for d in deps])
        for x, wr in acc:
            for (y, wr2, i) in hist.get(x[0], []):
                if (x[0][0] == "p" and ops[i]["q"] != q) or ((wr or wr2) and meet(x, y)):
                    deps[i] = True
        ops.append({"q": q, "fn": fn, "deps": deps, "cost": cost, "lat": lat, "sem": "s" + q if sem == "" else sem, "inc": inc,
                    "arrive": arrive, "more": dict(more)})
        for x, wr in acc:
            old = [h for h in hist.get(x[0], []) if not (wr and x[1] <= h[0][1] and h[0][2] <= x[2] and x[0][0] != "p" and
                                                         (x[3] == 1 or x[3] == h[0][3] and meet(x, h[0])))]
            hist[x[0]] = old + [(x, wr, len(ops) - 1)]
        return len(ops) - 1

    def ap(o):
        return o[0] if isinstance(o, tuple) else o

    def time(a, per):
        return 0.06 + 0.0015 * a[2] if a[3] else max(64, a[2] * per) * 0.001

    def narrow(*o):
        return 0.5 if all(_SB.get(x[1][0][0], (0, F32))[1] in (BF, U16) for x in o) else 1.0

    def tt(out, a, b, op, **k):
        issue("V", lambda: g.vector.tensor_tensor(out[0], a[0], b[0], op), [a, b], [out], time(a, 1 if a[1][0][0][0] == "p" else 2), **k)

    def ts(out, a, s1, o1, s2=None, o2=None):
        if o2 is None:
            issue("V", lambda: g.vector.tensor_scalar(out[0], a[0], ap(s1), None, o1), [a, s1], [out], time(a, narrow(out, a)))
        else:
            issue("V", lambda: g.vector.tensor_scalar(out[0], a[0], ap(s1), ap(s2), o1, o2), [a, s1, s2], [out], time(a, narrow(out, a)))

    def cp(out, a, q="V", **k):
        if q == "S":
            issue("S", lambda: g.scalar.activation(out[0], a[0], Fn.Copy), [a], [out], time(a, 1), **k)
        else:
            issue("V", lambda: g.vector.tensor_copy(out[0], a[0]), [a], [out], time(a, narrow(out, a)), **k)

    def scan(out, d0, d1, init, o0, o1):
        issue("V", lambda: g.vector.tensor_tensor_scan(out[0], d0[0], d1[0], ap(init), o0, o1), [d0, d1, init], [out], time(d0, narrow(out, d0, d1)))

    def cumsum(out, d, init=0.0):
        scan(out, d, d, init, Op.add, Op.max)

    def carry(out, d):
        scan(out, A("cR", 0, d[2]), d, 0.0, Op.add, Op.min)

    def hold(out, row):
        scan(out, A("cH", 0, row[2]), row, 0.0, Op.add, Op.min)

    def fill(out, v):
        issue("V", lambda: g.vector.memset(out[0], v), [], [out], time(out, narrow(out)))

    def act(out, a, fn, bias=0.0, scale=1.0, acc=None):
        issue("S", lambda: g.scalar.activation(out[0], a[0], fn, bias=ap(bias), scale=ap(scale), accum_out=ap(acc)),
              [a, bias, scale], [out] + ([acc] if acc else []), time(a, 1) + (0.025 if acc else 0))

    def quant(q, s, a):
        issue("V", lambda: g.vector.quantize_mx(q[0], s[0], a[0]), [a], [q, s], 0.015 + 0.00027 * a[2])

    def mm(out, wq, ws, xq, xs, **k):
        issue("T", lambda: g.tensor.matmul_mx(out[0], wq[0], ws[0], xq[0], xs[0], True, True), [wq, ws, xq, xs], [out], 0.0006 * (out[2] + 16), **k)

    def iota(out, pattern, base, cm):
        if _SB[out[1][0][0]][1] == I32:
            issue("G", lambda: g.iota(out[0], pattern, base, cm), [], [out], 0.16 + 0.002 * out[2])
        else:
            issue("G", lambda: g.iota(out[0], pattern, base, cm, allow_small_or_imprecise_dtypes=True), [], [out], 0.16 + 0.002 * out[2])

    def dma(q, out, a, us, deps=(), last=None):
        dmas[0] += 1
        call = issue(q, lambda: queue[q].dma_start(out[0], a[0]), [a], [out], 0.1, "d%d" % (dmas[0] - 1), 16, LOAD / 2, deps,
                     behind=[] if last is None else [last - 1])
        return issue("D", None, [], [out], us, None, lat=LOAD / 2, deps=[call], behind=[] if last is None else [last])

    def send(t, n, reads, hop):
        name, pieces = _parcels(T, t)[n]
        other = T.cores[rank ^ STEP[t]]
        direct = topo.may_write(core, other)
        moves, came = [], 0
        for i, (src, mid, land, rel) in enumerate(pieces):
            to = other if direct else _relays(T, topo, core, other)[rel]
            eng = topo.engines(core, to)
            share = len(eng) // len(pieces)
            moves.append(RemoteDMATransfer(dst_ids=[DstId(rid=topo.addr(to, core)[0], pnc=topo.addr(to, core)[1])],
                                           dma_engine_mask=_bits(eng[share * i:share * i + share]), src=src, dst=land if direct else mid,
                                           remote_sem=T.sem[name + str(t) if direct else "in" + name]))
            total[0] += share
            came += share if direct else len(topo.engines(_relays(T, topo, other, core)[rel], core))
        sent = issue("G", lambda: g.remote_dma_fused(moves, local_sem=T.sem.sent), reads, [], 0.3, None, lat=hop if direct else 2 * hop,
                     more={"sent": total[0], name + str(t): came})
        return {"deps": [sent], "arrive": [(name + str(t), came)]}

    def hbm(x):
        return (x, [], 0, False)

    def byte(o):
        return (o[0].bitcast(dt.uint8),) + o[1:]

    def word(o):
        return (o[0].bitcast(dt.uint32),) + o[1:]

    first = dma("Y", A("ut"), hbm(T.u[:]), 0.6)
    first = dma("Y", A("xt0", 0, 2 * C), hbm(T.x[:, 0:2 * C]), 0.7, last=first)
    first = dma("Y", A("xt0", 2 * C, 4 * C), hbm(T.x[:, 2 * C:4 * C]), 0.7, last=first)
    dma("Y", byte(A("qw")), hbm(T.wc[:]), 1.5, [first])
    dma("Y", A("sw"), hbm(T.ws[:]), 0.5, [first])
    dma("Y", A("vt"), hbm(T.v[:]), 0.7, [first])
    iota(A("cK"), [[16, 32]], 0, 0)
    iota(A("cP", 0, 1), [[0, 1]], 0, 1)
    iota(A("cJ"), [[0, NB + 1], [1, 16]], 0, 0)
    iota(A("cI"), [[1, C + 16]], 0, 0)
    iota(A("cRev"), [[-1, H + 2]], H, 0)
    iota(A("cTY", 0, K), [[-1, K]], -1, 0)
    iota(A("c01"), [[0, H], [1, 2]], 0, 0)
    iota(A("EC", AT + C, WF), [[1, K]], 0, 0)
    for o, v in ((A("ft"), 0.0), (A("et"), 0.0), (A("SW", C, C + 8), -BIG), (A("MN", 0, 16), 0.0), (A("cTY", K, C + 16), 1.0),
                 (A("KEY", 0, 1), (C * 512 + C) * UNIT), (A("UP", 0, 1), 1.0), (A("DL", 0, 1), 1.0), (A("DL", C - 1, C), 0.0),
                 (A("PN", K, K + 1), 0.0), (A("CK", 0, 1), -K - 1.0), (A("AN", 0, 1), 0.0), (A("JN", K, H), 0.0), (A("FS", 0, 1), 1.0)):
        fill(o, v)
    col = lambda i: A("cPf", i, i + 1)
    cp(A("oU"), A("cK", 0, 8))
    ts(A("cP", 1, 2), A("cP", 0, 1), 15, Op.bitwise_and)
    ts(A("cP", 2, 3), A("cP", 0, 1), 1, Op.bitwise_and)
    cp(A("cPf", 0, 3), A("cP", 0, 3))
    r16, odd = col(1), col(2)
    ts(A("cR"), A("cJ", 0, H), 0.5, Op.is_lt, 2 * FAR, Op.mult)
    act(A("cRn"), A("cR"), Fn.Identity, 0.0, -1.0)
    ts(A("mask"), A("cJ"), r16, Op.is_equal)
    act(A("cM"), A("mask", 0, H), Fn.Identity, FAR, -2 * FAR)
    act(A("cN", 1, C, 2), A("mask", 0, H), Fn.Identity, FAR, -2 * FAR)
    act(A("cN", 0, C, 2), A("mask", 15, H + 15), Fn.Identity, FAR, -2 * FAR)
    act(A("XN", C, C + 1), A("mask", 15, 16), Fn.Identity, FAR, -FAR - BIG)
    ts(A("HM", 0, H), A("mask", 15, H + 15), -DROP / 1024.0, Op.mult)
    ts(A("HS", 0, H), A("mask", 0, H), 1024.0, Op.mult)
    for i in range(2):
        scan(A("cH", H * i, H * i + H), A("HM", 0, H), A("HS", 0, H), 0.0, Op.mult, Op.add)
    ts(A("cHn"), A("cH"), -1.0, Op.mult)
    act(A("cC", 0, H, 2), A("cH", 0, H // 2), Fn.Identity, 0.0, 3.0 / DROP)
    cp(A("cC", 1, H, 2), A("mask", 0, H // 2), "S")
    act(col(6), A("mask", 15, 16), Fn.Identity, DROP, -DROP)
    act(col(7), col(6), Fn.Identity, 0.0, 3.0 / DROP)
    act(col(8), col(6), Fn.Identity, float(H), -1.0)
    act(col(9), col(6), Fn.Identity, float(K), -1.0)
    act(col(10), col(6), Fn.Identity, 0.0, -1.0)
    act(col(11), col(6), Fn.Identity, (C - 1) * 512.0, -3.0 / DROP / UNIT)
    ts(A("cj"), A("cK", 0, 20), r16, Op.add)
    act(A("cm2"), A("cj", 0, NB), Fn.Identity, col(6), 2.0)
    ts(col(3), odd, 0.5, Op.mult, col(6), Op.add)
    ts(A("cb"), A("cj"), 2.0, Op.subtract, 0.5, Op.mult)
    act(A("cb"), A("cb"), Fn.Identity, col(3), 1.0)
    act(col(4), odd, Fn.Identity, C - 1.0, 1.0)
    act(col(12), col(4), Fn.Identity, 0.0, col(6))
    act(col(5), odd, Fn.Identity, AT + 1.0, -1.0)
    act(A("ck", 0, 4), A("cj", 0, 4), Fn.Identity, -0.5, 1.0)
    act(A("ck", 4, 8), A("cj", 0, 4), Fn.Identity, col(5), 1.0)
    ts(A("et", 3, 515, 4), A("cI", 0, 128), col(0), Op.is_equal)
    quant(A("qu0"), A("su0"), A("ut"))
    cp(word(A("qu")), ind(word(A("qu0")), A("oU")))
    cp(A("su"), ind(A("su0"), A("oU")), "S")
    act(A("cTK"), A("cI"), Fn.Identity, 0.0, 512.0 * UNIT)
    act(A("cPn"), A("cI", 2, C + 2, 2), Fn.Identity, 0.0, UNIT)
    E = lambda n, b: A(n, 128 * b, 128 * b + 128)
    for b in range(4):
        quant(E("qe", b), E("se", b), A("et", 3 - b, 515 - b))
    quant(A("qv"), A("sv"), A("vt"))

    banksH = ["pH0", "pH1", "pH2", "pS"]
    halves = ((0, H), (H, C))
    M = lambda a, b: A("MN", 16 + a, 16 + b)
    end = lambda name, c, n=1: A(name, 16 * c + 15, 16 * (c + n), 16)
    row = lambda name, c: A(name, H * c, H * c + H)
    sc = lambda i: A("SC", i, i + 1)
    sm = lambda i: A("SM", NB * i, NB * i + NB)
    part = lambda c: C * (2 * c // NB)
    CK = A("CK", 1, H + 1)

    for t in range(R):
        qx, sxp, lc, ls, oA = "qx%d" % t, "sx%d" % t, "lc%d" % t, "ls%d" % t, "oA%d" % t
        nr, nv, ne = NRS[t], NV[t], NES[t]
        oN, oQ, oG, oP, oB, oL, oL2, oE = [A(oA, NB * i, NB * i + (NB if i < 7 else 4)) for i in range(8)]
        for a, b in halves if t == 0 else ((0, C),):
            quant(A(qx, a, b), A(sxp, a, b), A("xt%d" % t, 4 * a, 4 * b))
        got = [send(t, 0, [A(qx)], BULK), send(t, 1, [A(sxp)], HOP)]
        both = {k: got[0][k] + got[1][k] for k in got[0]}
        for bank in ("pH0", "pS"):
            mm(A(bank, 0, C), A("qu"), A("su"), A(qx), A(sxp))
        for b in range(4):
            mm(A("pT%d" % b, 0, C), E("qe", b), E("se", b), A(qx), A(sxp))
        for b in range(2):
            cp(A("TF", C * b, C * b + C), A("pT%d" % (2 + b), 0, C), "S")
        for b, bank in enumerate(("pH1", "pH2", "pT2", "pT3")):
            mm(A(bank, 0, C), E("qe", b), E("se", b), A(lc), A(ls), **both)
            act(A("TH", C * b, C * b + C), A(bank, 0, C), Fn.Copy, 0.0, 0.5)
            cp(A("FA", WF * b + AT + C, WF * b + WF), A(bank, 0, K), "S")
        cp(A("SW", 0, C, 2), A("pH0", 0, C, 2), "S")
        cp(A("SW", 1, C, 2), A("pH0", 1, C, 2), "S")
        tt(M(H, C), A("pS", 1, C, 2), A("SW", 2, C + 1, 2), Op.min)
        tt(M(0, H), A("pS", 1, C, 2), A("SW", 0, C, 2), Op.max)
        for a, b in halves:
            n = min(b + 1, C)
            scan(A("XN", a + 1, n), A("pS", a + 1, n), A("cN", 1, n - a), FAR, Op.min, Op.max)
            carry(A("DT", H + a // 2, H + b // 2), A("XN", a + 2, b + 1, 2))
        scan(A("X1"), M(0, H), A("cM"), FAR, Op.min, Op.max)
        carry(A("DT", 0, H), A("X1"))
        tt(A("UP", 1, C, 2), A("pS", 1, C, 2), A("SW", 0, C, 2), Op.is_gt)
        tt(A("UP", 2, C + 1, 2), A("pS", 1, C, 2), A("SW", 2, C + 1, 2), Op.is_lt)
        act(A("US"), A("UP", 2, C + 1, 2), Fn.Identity, 0.0, -UNIT)
        scan(A("POS"), A("cPn"), A("US"), 0.0, Op.max, Op.add)
        hold(A("D5"), A("UP", 1, C, 2))
        tt(sm(0), end("D5", 0, NB), A("cm2"), Op.add)
        cp(oP, sm(0))
        tt(A("DL", 1, C - 1, 2), A("pS", 2, C, 2), M(0, H - 1), Op.is_gt)
        tt(A("DL", 2, C, 2), A("pS", 1, C - 1, 2), M(1, H), Op.is_lt)
        hold(A("D4"), A("DL"))
        tt(A("HT"), end("D4", 0, 20), A("cb"), Op.add)
        cp(A("oS"), A("HT"))
        tt(A("PN", 0, K), A("UP", 0, K), A("UP", 1, K + 1), Op.is_le)
        cumsum(A("PN", K + 1, 2 * K + 1), A("PN", 0, K))
        hold(A("D7"), A("PN", 0, 2 * K))
        act(A("PF", 0, 4), end("D7", 0, 4), Fn.Identity, col(12), col(4))
        tt(A("PF", 4, 8), A("PF", 0, 4), A("ck", 4, 8), Op.add)
        for c in range(nr, NB):
            act(row("JK", c), M(H, C), Fn.Sign, end("DT", NB + c), -1.0, A("ACC", c, c + 1))
        ts(A(oA, nr, NB), A("ACC", nr, NB), -1.0, Op.mult, float(H), Op.add)
        for c in range(nr):
            ts(row("JK", c), M(H, C), end("DT", NB + c), Op.is_lt)
            ts(row("JK2", c), M(H, C), end("DT", NB + c), Op.is_le)
            scan(row("CS", c), row("JK", c), row("JK2", c), -float(H), Op.add, Op.add)
        if nr:
            ts(A(oA, 0, nr), A("CS", H - 1, nr * H, H), -1.0, Op.mult, float(H), Op.add)
        tt(A("KEY", 1, H + 1), ind(A("cTK"), oN), A("POS"), Op.add)
        act(A("KEYN", 1, H + 1), A("KEY", 1, H + 1), Fn.Identity, -1.0, 1.0)
        for c in range(NB):
            act(A("KB", ROW * c, ROW * c + H + 2), M(-1, H + 1), Fn.Sign, end("DT", c), -1.0)
        for c in range(NB):
            d = NB - 1 - c
            scan(A("LR", part(d) + 1, part(d) + 32 * d + 32, 2), A("KB", ROW * d, ROW * d + 16 * d + 16), A("KEY", 0, 16 * d + 16),
                 0.0, Op.mult, Op.max)
            scan(rev("LR", part(c) + 32 * c, part(c) + C, 2), rev("KB", ROW * c + 16 * c + 2, ROW * c + H + 2), rev("KEYN", 16 * c + 1, H + 1),
                 -1.0, Op.min, Op.max)
        for d in reversed(range(NB)):
            scan(A("LL", part(d) // 2, part(d) // 2 + 16 * d + 16), A("KB", ROW * d, ROW * d + 16 * d + 16), A("cRev", 0, 16 * d + 16),
                 0.0, Op.mult, Op.max)
        for i in range(2):
            scan(A("DS", H * i, H * i + H), A("cC"), A("LR", (C + H) * i, (C + H) * i + H), 0.0, Op.add, Op.min)
        ts(A("I1", 0, NB), A("DS", 31, C, 32), col(7), Op.add, 1.0 / UNIT, Op.mult)
        ts(A("I1", NB, 2 * NB), A("I1", 0, NB), 511, Op.bitwise_and)
        q = A("I1", NB, 2 * NB)
        cp(oQ, q)
        tt(sm(1), q, sm(0), Op.subtract)
        act(sm(10), sm(1), Fn.Square)
        act(sm(2), sm(10), Fn.Relu, 96.0, -96.0)
        act(sm(3), A("DS", 31, C, 32), Fn.Identity, col(11), -1.0 / UNIT)
        tt(sm(4), sm(3), sm(0), Op.max)
        tt(sm(5), sm(4), q, Op.min)
        cp(oB, sm(5))
        gotp, gotq = send(t, 2, [oP], HOP), send(t, 3, [oB], HOP)
        for b in range(4):
            pick = lambda name: ind(A("TH", C * b, C * b + C), A(name % t))
            cp(A("TMP", C * b, C * b + C, 2), pick("lp%d"), "S", **gotp)
            if b < NFAS[t]:
                tt(A("FA", WF * b + AT + 1, WF * b + AT + C, 2), pick("lq%d"), A("TMP", C * b, C * b + C, 2), Op.add, **gotq)
            else:
                cp(A("TMP", C * b + 1, C * b + C, 2), pick("lq%d"), "S", **gotq)
                scan(A("FA", WF * b + AT, WF * b + AT + C), A("c01"), A("TMP", C * b, C * b + C), 0.0, Op.mult, Op.add)
        tt(A("NG"), ind(A("SW"), oQ), M(0, H), Op.subtract)
        tt(A("X3"), ind(A("SW"), oQ), A("X1"), Op.subtract)
        scan(A("DP"), A("cRn"), A("X3"), 0.0, Op.add, Op.max)
        for c in range(nv, NB):
            act(row("JK", c), A("NG"), Fn.Sign, end("DP", c), -1.0)
            act(row("JK2", c), row("JK", c), Fn.Relu, A("SM", 2 * NB + c, 2 * NB + c + 1), 1.0, A("ACC", NB + c, NB + c + 1))
        for c in range(nv):
            ts(row("JK", c), A("NG"), end("DP", c), Op.is_lt)
            cumsum(row("CS", c), row("JK", c), A("SM", 2 * NB + c, 2 * NB + c + 1))
        cp(A(oA, 2 * NB, 2 * NB + nv), A("CS", H - 1, nv * H, H))
        ts(A(oA, 2 * NB + nv, 3 * NB), A("ACC", NB + nv, 2 * NB), float(C), Op.min)
        cp(A("Y"), ind(A("cTY"), oG), "S")
        scan(A("MU"), A("Y"), A("Y"), 0.0, Op.min, Op.min)
        mu = A("MU", H - 1, H)
        act(A("OUT"), A("Y"), Fn.Relu, 0.0, 1.0, sc(0))
        act(A("LE"), A("OUT"), Fn.Identity, 1.0, -1.0)
        ts(A("LT"), A("Y"), mu, Op.is_gt)
        scan(A("UU"), A("LT"), A("OUT"), mu, Op.add, Op.subtract)
        scan(CK, A("LE"), A("UU"), -K - 1.0, Op.add, Op.min)
        act(sc(1), sc(0), Fn.Relu, float(K - H), 1.0)
        act(sc(2), sc(1), Fn.Identity, col(9), 1.0)
        act(sc(3), sc(1), Fn.Identity, -float(K), -1.0)
        act(sc(4), sc(1), Fn.Identity, col(10), 1.0)
        act(A("PF", 8, 12), A("ck", 0, 4), Fn.Identity, sc(3), 1.0)
        act(A("PF", 12, 16), end("D7", 4, 4), Fn.Sign, sc(4), -1.0)
        tt(A("PF", 16, 20), A("PF", 12, 16), A("PF", 4, 8), Op.mult)
        act(A("JN", 0, K), A("cI", 0, K), Fn.Identity, sc(3), 1.0)
        for c in range(4):
            bias = A("PF", 8 + c, 9 + c)
            if c < ne:
                ts(row("JK", c), CK, bias, Op.is_lt, 2.0, Op.mult)
                cumsum(row("CS", c), row("JK", c))
                twice = A("CS", H * c + H - 1, H * c + H)
            else:
                twice = A("ACC", 2 * NB + c, 2 * NB + c + 1)
                act(row("JK2", c), CK, Fn.Sign, bias, -1.0, twice)
            ts(A(oA, 7 * NB + c, 7 * NB + c + 1), twice, float(AT + 1 if c < ne else H + AT + 1), Op.add, A("PF", 16 + c, 17 + c), Op.max)
        got = send(t, 4, [oE], HOP)
        for b in range(4):
            cp(A("ft", b, 4 * K, 4), ind(A("FA", WF * b, WF * b + WF), A("lk%d" % t)), "V" if b < NFS[t] else "S", **got)
        quant(A("qf"), A("sf"), A("ft"))
        for i in range(2):
            hold(A("D6", H // 2 * i, H // 2 * (i + 1)), A("LL", 3 * H // 2 * i, 3 * H // 2 * i + H // 2))
        act(sm(6), end("D6", 0, NB), Fn.Identity, col(8), -1.0)
        act(sm(9), sm(1), Fn.Sign, 0.5, 1.0)
        tt(sm(8), sm(9), A("cj", 0, NB), Op.mult)
        tt(sm(7), sm(8), sm(6), Op.max)
        cp(A(oA, 5 * NB, 7 * NB), A("SM", 6 * NB, 8 * NB))
        scan(A("CK2"), A("LE"), A("UU"), -K - 1.0, Op.add, Op.min)
        tt(A("NM"), ind(A("CK"), oL), A("CK2"), Op.is_ge)
        act(A("N1"), ind(A("CK"), oL2), Fn.Identity, -128.0, 1.0)
        act(A("N2"), CK, Fn.Identity, -129.0, 1.0)
        scan(A("N3"), A("N1"), A("N2"), 0.0, Op.min, Op.subtract)
        act(A("NA"), A("N3"), Fn.Relu, 0.0, 128.0)
        act(A("AN", 1, H + 1), A("N3"), Fn.Identity, 1.0, -1.0)
        scan(A("FS", 1, H + 1), A("NM"), A("KEY", 1, H + 1), 1.0, Op.min, Op.max)
        scan(rev("BS", 0, H), rev("KEY", 1, H + 1), rev("NM", 0, H), 0.0, Op.max, Op.min)
        tt(A("SD"), A("FS", 0, H), A("BS"), Op.is_gt)
        act(A("NS"), A("SD"), Fn.Identity, 1.0, -1.0)
        scan(A("KP"), CK, A("CK", 0, H), 0.0, Op.min, Op.subtract)
        act(A("W1"), A("KP"), Fn.Identity, 128.0, 128.0)
        scan(A("LP"), A("NA"), A("W1"), 256.0, Op.min, Op.add)
        scan(A("XP"), A("N1"), A("LP"), 0.0, Op.min, Op.add)
        scan(A("GO"), A("SD"), A("NA"), 0.0, Op.max, Op.min)
        scan(A("HO"), A("AN", 0, H), A("NS"), 0.0, Op.max, Op.min)
        scan(rev("LB", 0, H), rev("CK", 1, H + 1), rev("GO", 0, H), 0.0, Op.min, Op.add)
        scan(rev("Z", 0, H), rev("GO", 0, H), rev("XP", 0, H), 0.0, Op.mult, Op.min)
        scan(A("O"), A("HO"), A("Z"), 0.0, Op.mult, Op.min)
        scan(A("LAB"), A("LB"), A("O"), -200.0, Op.max, Op.min)
        tt(A("HM", 0, HV[t]), ind(A("LAB"), A("oS", 0, HV[t] // 16)), A("JN", 0, HV[t]), Op.min)
        cp(A("HM", HV[t], C), ind(A("LAB"), A("oS", HV[t] // 16, 2 * NB)), "S")
        scan(A("HS"), A("cHn"), A("HM"), 0.0, Op.add, Op.max)
        ts(A("oH"), end("HS", 0, 20), sc(2), Op.add)
        xn = "xt%d" % (t + 1)
        for b in (2, 3, 0, 1):
            mm(A(banksH[b], 0, 128), E("qw", b), E("sw", b), A("qf"), A("sf"))
            act(A("HR", K * b, K * b + K), A(banksH[b], 0, K), Fn.Relu, 0.0, 0.03125)
        for lo, hi in ((0, C),) if t < R - 1 else halves:
            pick = lambda b: ind(A("HR", K * b, K * b + K), A("oH", lo // 16, hi // 16))
            for b in range(2):
                cp(A("GG", C * b + lo, C * b + hi), pick(b), "S")
                tt(A(xn, 4 * lo + b, 4 * hi, 4), A("pT%d" % b, lo, hi), A("GG", C * b + lo, C * b + hi), Op.add)
            for b in range(2, 4):
                tt(A(xn, 4 * lo + b, 4 * hi, 4), pick(b), A("TF", C * (b - 2) + lo, C * (b - 2) + hi), Op.add)

    scan(A("EC", AT + 1, AT + C, 2), A("cI", 0, C, 2), A("UP", 1, C, 2), 0.0, Op.max, Op.add)
    cp(A("ER"), ind(A("EC"), oE), "S")
    cp(A("OLR"), ind(A("ER"), A("oH")), "S")
    dma("Y", hbm(T.ol[:]), (T.OLR[0:128:16, :], A("OLR")[1]), 0.05)
    for (lo, hi), bank, q in zip(halves, ("pH0", "pH1"), "SV"):
        quant(A("qx2", lo, hi), A("sx2", lo, hi), A("xt2", 4 * lo, 4 * hi))
        mm(A(bank, 0, H), A("qv"), A("sv"), A("qx2", lo, hi), A("sx2", lo, hi))
        dma("Y", hbm(T.oc[:, 4 * lo:4 * hi]), byte(A("qx2", lo, hi)), 0.6)
        cp(A("YO", lo, hi), A(bank, 0, H), q)
        dma("Y" if lo else "S", hbm(T.y[:, lo:hi]), A("YO", lo, hi), 0.6)
    for k in range(4):
        dma("S", hbm(T.osc[4 * k:4 * k + 4, :]), (T.sx2[32 * k:32 * k + 4, :], A("sx2")[1]), 0.05)
    _emit(ops, queue, T)
